import numpy as np, ml_dtypes
CORES = [66,74,82,90,194,202,210,218]
N = 8
import mx_ref
BF = ml_dtypes.bfloat16
def cols(t, e):
    v = np.concatenate([t.reshape(128, -1, 4), np.zeros((128, 1, 4), BF)], axis=1)
    return np.ascontiguousarray(v[:, e]).reshape(128, -1)
def f(rng, *shape):
    return mx_ref.flush((rng.standard_normal(shape, dtype=np.float32) * np.exp2(rng.integers(-2, 3, shape[:-1] + (1,)))).astype(BF))
def wide(rng, *shape, cols=0):
    v = rng.standard_normal(shape, dtype=np.float32) * np.exp2(rng.integers(-12, 13, shape)).astype(np.float32)
    if cols: v *= np.repeat(np.exp2(rng.integers(-cols, cols + 1, shape[:-2] + (1, shape[-1] // 4))) * (rng.random(shape[:-2] + (1, shape[-1] // 4)) > 0.0625), 4, axis=-1).astype(np.float32)
    return mx_ref.flush(v.astype(BF))
T, G, C = 256, 8, 16
def lean(rng, d, sizes):
    p, t = rng.integers(0, 128), rng.integers(0, 4)
    q, v = np.array(d["qw"]), np.array(d["x"])
    q[:, p, t::4] = BF(128)
    v[:, p, t::4] = np.repeat(np.asarray(sizes, np.float32), 16).astype(BF)
    return {"qw": q, "x": v}
def setup_inputs(rng):
    return {"qw": f(rng, N, 128, 512), "x": f(rng, N, 128, 4 * T)}
def setup_inputs_ties(rng):
    d = setup_inputs(rng); v = []
    for s in range(N):
        k = rng.permutation(np.arange(C) // 4)
        v.append(cols(d["x"][s], np.concatenate([16 * c + rng.permutation(16) for c in k])))
    d["x"] = np.stack(v); return d
def setup_inputs_last(rng):
    return lean(rng, setup_inputs(rng), [0] * (C - 1) + [128])
def setup_inputs_alike(rng):
    d = setup_inputs(rng); d["qw"] = np.concatenate([d["qw"][:, :, :64]] * G, axis=2); return d
def setup_inputs_below(rng):
    return lean(rng, setup_inputs(rng), [-128 * 4096] * C)
def setup_inputs_spread(rng):
    d = setup_inputs(rng); d["x"] = wide(rng, N, 128, 4 * T); return d
def check_inputs(d):
    b = []
    for k in ("qw", "x"):
        a = np.abs(np.asarray(d[k]).astype(np.float32))
        if not ((a == 0) | ((a >= 2.0 ** -30) & (a <= 2.0 ** 30))).all(): b.append(k)
    return b
def decode(q, n):
    out = np.zeros((128, 4 * n), np.float32)
    for b in range(4):
        e = np.zeros((128, 128, 4), np.float32); e[np.arange(128), np.arange(128), b] = 1
        out[:, b::4] = mx_ref.matmul(mx_ref.quantize(e.reshape(128, 512).astype(BF)), q)
    return out
def reference(qw, x):
    W = [mx_ref.quantize(qw[r]) for r in range(N)]
    X = [mx_ref.quantize(x[s]) for s in range(N)]
    R = [mx_ref.quantize((x[s].astype(np.float32) - decode(X[s], T)).astype(BF)) for s in range(N)]
    y = np.zeros((N, 128, N * G * 16), np.float32); ch = np.zeros((N, G, N), np.float32)
    for r in range(N):
        for s in range(N):
            a, b = mx_ref.matmul(W[r], X[s]), mx_ref.matmul(W[r], R[s])
            best = a.reshape(G, 16, C, 16).max(axis=(1, 3)).argmax(axis=1)
            ch[r][:, s] = best
            for g in range(G):
                i, j = 16 * (s * G + g), 16 * int(best[g])
                y[r][:, i:i + 16] = a[:, j:j + 16] + b[:, j:j + 16]
    return {"y": y, "ch": ch}

@@ -1,0 +1,490 @@
+from concourse.bass import DstId, RemoteDMATransfer
+from concourse.mybir import dt, AluOpType, AxisListType, ActivationFunctionType
+
+N = 8
+BIG = 1e29
+CODES, PLANE = "float8_e4m3fn_x4", "uint8"
+
+SCRATCH = {
+    "qwb": ("sbuf", [128, 512], "bfloat16"),
+    "xb": ("sbuf", [128, 1024], "bfloat16"),
+    "rb": ("sbuf", [128, 1024], "bfloat16"),
+    "ob": ("sbuf", [128, 528], "bfloat16"),
+    "eb": ("sbuf", [128, 528], "bfloat16"),
+    "onf": ("sbuf", [128, 128], "float32"),
+    "idn": ("sbuf", [128, 128], "float32"),
+    "p16": ("sbuf", [128, 128], "float32"),
+    "pcol": ("sbuf", [128, 8], "float32"),
+    "m24": ("sbuf", [128, 24], "float32"),
+    "scol": ("sbuf", [128, 8], "float32"),
+    "msk": ("sbuf", [128, 256], "float32"),
+    "top": ("sbuf", [128, 256], "float32"),
+    "QC": ("sbuf", [128, 128 * 6], CODES),
+    "QS": ("sbuf", [128, 128 * 6], PLANE),
+    "XC": ("sbuf", [128, 256], CODES),
+    "XS": ("sbuf", [128, 256], PLANE),
+    "RC": ("sbuf", [128, 256], CODES),
+    "RS": ("sbuf", [128, 256], PLANE),
+    "EC": ("sbuf", [128, 512], CODES),
+    "ES": ("sbuf", [128, 512], PLANE),
+    "sc": ("sbuf", [128, 2048], "float32"),
+    "rm": ("sbuf", [128, 768], "float32"),
+    "ltb": ("sbuf", [128, 48], "float32"),
+    "cc": ("sbuf", [128, 12], "float32"),
+    "bc": ("sbuf", [128, 384], "float32"),
+    "off": ("sbuf", [128, 32 * 6], "uint16"),
+    "offl": ("sbuf", [128, 32], "uint16"),
+    "hb": ("sbuf", [128, 1024 * 6], "bfloat16"),
+    "OC": ("sbuf", [128, 256 * 6], CODES),
+    "OS": ("sbuf", [128, 256 * 6], PLANE),
+    "LC": ("sbuf", [128, 256 * 6], CODES),
+    "LS": ("sbuf", [128, 256 * 6], PLANE),
+    "FC": ("sbuf", [128, 1024], CODES),
+    "FS": ("sbuf", [128, 1024], PLANE),
+    "HFC": ("sbuf", [128, 512], CODES),
+    "HFS": ("sbuf", [128, 512], PLANE),
+    "HXC": ("sbuf", [128, 256], CODES),
+    "HXS": ("sbuf", [128, 256], PLANE),
+    "pf": ("sbuf", [128, 768], "float32"),
+    "ysb": ("sbuf", [128, 128 * N], "float32"),
+    "chrow": ("sbuf", [128, 128], "float32"),
+    "chc": ("sbuf", [128, 32], "float32"),
+    "cht": ("sbuf", [128, 32], "float32"),
+    "chk": ("sbuf", [128, 24], "float32"),
+    "chm": ("sbuf", [128, 24], "float32"),
+    "chl": ("sbuf", [128, 8], "float32"),
+    "chf": ("sbuf", [128, 8], "float32"),
+    "chd": ("dram", [128, 1], "float32"),
+    "chland": ("dram", [N, 128, 1], "float32"),
+    "psD": ("psum", [128, 1024], "float32"),
+    "psA": ("psum", [128, 1024], "float32"),
+    "psT": ("psum", [128, 512], "float32"),
+    "psY": ("psum", [128, 1536], "float32"),
+}
+UNITS = ["own", "b0f", "b0s", "b1f", "w0", "w1"]
+SEMAPHORES = (
+    ["lq", "lx", "mo", "mf", "mk", "mtop", "mch", "ms", "qq", "qx", "qr", "qe", "ge", "gi", "gp", "gm"]
+    + ["dm%d" % b for b in range(4)] + ["rs%d" % b for b in range(4)]
+    + [n + u + str(h) for n in ("sm", "sn") for u in UNITS for h in range(2)]
+    + ["tr%d%d" % (b, h) for b in range(3) for h in range(2)]
+    + [n + str(b) for n in ("cel", "bcx", "ctx", "ofx", "pm", "pc", "yg") for b in range(3)]
+    + [n + str(j) for n in ("gv", "gs", "qz", "ym", "yc") for j in range(6)]
+    + [n + str(j) for n in ("q", "d") for j in range(N)]
+    + ["w" + str(i) + str(part) for i in range(2) for part in range(2)]
+    + ["yd", "ye", "chr", "chs", "chi", "chg", "chv", "chl1", "chf1", "cho", "sent"]
+    + ["hfc0", "hfs0", "hfc1", "hfs1", "hxc", "hxs"]
+)
+
+
+def make_plan(me, T, topo):
+    cores = T.cores
+    core = cores[me]
+    same = [r for r in range(N) if r == me or topo.same_plane(core, cores[r])]
+    other = [r for r in range(N) if r not in same]
+    mate = [r for r in other if topo.mates(core, cores[r])][0]
+    P = sorted([r for r in same if r != me], key=lambda r: r ^ me)
+    X = sorted([r for r in other if r != mate], key=lambda r: r ^ me)
+    relays = [c for c in topo.cores_of(core) if topo.die(c) != topo.die(core)
+              and all(topo.may_write(c, cores[x]) for x in X)]
+    near2 = sorted([mate, X[2]])
+    return {
+        "P": P, "M": mate, "X": X, "same": same, "relays": relays[:2], "W": sorted(X[:2]), "B": near2,
+        "slots": same + near2,
+        "w_relay": {X[0]: 0, X[1]: 1},
+        "x_relay": {P[0]: 0, P[2]: 1},
+        "first": [P[0], P[2], P[1]], "second": [X[2], mate],
+        "yorder": [P[0], P[1], P[2], X[2], mate],
+    }
+
+
+def count(mask):
+    return bin(mask).count("1")
+
+
+def rank_program(g, core, T, topo):
+    me = T.rank_of(core)
+    if me is None:
+        homes = [T.rank_of(c) for c in topo.cores_of(core) if T.rank_of(c) is not None]
+        if homes:
+            relay_program(g, core, homes[0], T, topo)
+        return
+    plans = [make_plan(r, T, topo) for r in range(N)]
+    plan = plans[me]
+    P, M, X, W, B, relays = plan["P"], plan["M"], plan["X"], plan["W"], plan["B"], plan["relays"]
+    first, second = plan["first"], plan["second"]
+    chosen_ranks = first + second
+    cores = T.cores
+    sem = T.sem
+    sl = {r: j for j, r in enumerate(plan["slots"])}
+    own = sl[me]
+    u8 = dt.uint8
+    Op = AluOpType
+    Copy = ActivationFunctionType.Copy
+    V, S, PE, SY = g.vector, g.scalar, g.tensor, g.sync
+
+    def qcol(t, j):
+        return t[:, 128 * j:128 * j + 128]
+
+    def xcol(t, j):
+        return t[:, 256 * j:256 * j + 256]
+
+    SY.dma_start(T.qwb[:], T.qw[:]).then_inc(sem.lq, 16)
+    S.dma_start(T.xb[:], T.x[:]).then_inc(sem.lx, 16)
+
+    V.memset(T.ob[:], 1.0).then_inc(sem.mo, 1)
+    V.memset(T.onf[:], 1.0).then_inc(sem.mf, 1)
+    V.memset(T.msk[:], BIG).then_inc(sem.mk, 1)
+    V.memset(T.top[:], BIG).then_inc(sem.mtop, 1)
+    V.memset(T.scol[:], 64.0).then_inc(sem.ms, 1)
+    V.memset(T.chrow[:], 0.0).then_inc(sem.mch, 1)
+    V.memset(T.chc[:], 0.0).then_inc(sem.mch, 1)
+    V.memset(T.chl[:], 0.0).then_inc(sem.mch, 1)
+    V.wait_ge(sem.mk, 1)
+    V.memset(T.msk[:, 0:256:16], -BIG).then_inc(sem.mk, 1)
+    V.wait_ge(sem.ms, 1)
+    V.memset(T.scol[32 * own:32 * own + 32, :], 16.0).then_inc(sem.ms, 1)
+    V.wait_ge(sem.lq, 16)
+    V.quantize_mx(qcol(T.QC, own), qcol(T.QS, own), T.qwb[:]).then_inc(sem.qq, 1)
+    V.wait_ge(sem.lx, 16)
+    V.quantize_mx(T.XC[:], T.XS[:], T.xb[:]).then_inc(sem.qx, 1)
+    V.wait_ge(sem.ge, 1)
+    for b in range(4):
+        V.quantize_mx(qcol(T.EC, b), qcol(T.ES, b), T.eb[:, 4 - b:516 - b]).then_inc(sem.qe, 1)
+    for b in range(4):
+        V.wait_ge(sem["dm%d" % b], 1)
+        k = 512 * (b % 2)
+        V.tensor_tensor(T.rb[:, b:1024:4], T.xb[:, b:1024:4], T.psD[:, k:k + 256], Op.subtract).then_inc(sem["rs%d" % b], 1)
+    for b in range(4):
+        V.wait_ge(sem["rs%d" % b], 1)
+    V.quantize_mx(T.RC[:], T.RS[:], T.rb[:]).then_inc(sem.qr, 1)
+
+    PE.wait_ge(sem.qx, 1)
+    PE.wait_ge(sem.qe, 4)
+    for b in range(4):
+        if b >= 2:
+            PE.wait_ge(sem["rs%d" % (b - 2)], 1)
+        k = 512 * (b % 2)
+        PE.matmul_mx(T.psD[:, k:k + 256], qcol(T.EC, b), qcol(T.ES, b), T.XC[:], T.XS[:], True, True).then_inc(sem["dm%d" % b], 1)
+
+    base, wide, step = (0, 1024, 1536), (512, 256, 256), (4, 2, 2)
+    fp = 1 - own // 2
+    single = own + 1 - 2 * (own % 2)
+    units = {"own": (0, 128 * own, 128, T.psY), "b0f": (0, 256 * fp, 256, T.psA), "b0s": (0, 128 * single, 128, T.psY),
+             "b1f": (1, 0, 256, T.psA), "w0": (2, 0, 128, T.psA), "w1": (2, 128, 128, T.psY)}
+
+    def score(u):
+        bt, a, n, ps = units[u]
+        for h in range(2):
+            if bt < 2:
+                k = 512 * bt + a
+                args = (qcol(T.XC, h), qcol(T.XS, h), T.QC[:, k:k + n], T.QS[:, k:k + n])
+            else:
+                k = 512 * (a // 128) + 128 * h
+                args = (T.FC[:, k:k + 128], T.FS[:, k:k + 128], qcol(T.QC, own), qcol(T.QS, own))
+            PE.matmul_mx(ps[:, 512 * h:512 * h + n], *args, True, True).then_inc(sem["sm%s%d" % (u, h)], 1)
+
+    def groups_v(u):
+        bt, a, n, ps = units[u]
+        for h in range(2):
+            k = base[bt] + wide[bt] * h + a
+            V.wait_ge(sem["sm%s%d" % (u, h)], 1)
+            V.tensor_tensor_scan(T.sc[:, k:k + n], T.msk[:, 0:n], ps[:, 512 * h:512 * h + n], -BIG, Op.min, Op.max).then_inc(sem["sn%s%d" % (u, h)], 1)
+
+    def turn(bt, us):
+        for h in range(2):
+            k = base[bt] + wide[bt] * h
+            for u in us:
+                PE.wait_ge(sem["sn%s%d" % (u, h)], 1)
+            PE.transpose(T.psT[:, 128 * h:128 * h + 128], T.sc[:, k + step[bt] - 1:k + wide[bt]:step[bt]], T.idn[:]).then_inc(sem["tr%d%d" % (bt, h)], 1)
+
+    def spread(bt):
+        PE.wait_ge(sem["bcx%d" % bt], 1)
+        PE.transpose(T.psT[:, 256:384], T.bc[:, 128 * bt:128 * bt + 128], T.idn[:]).then_inc(sem["ctx%d" % bt], 1)
+
+    def cells_v(bt):
+        V.wait_ge(sem["tr%d0" % bt], 1)
+        V.wait_ge(sem["tr%d1" % bt], 1)
+        rm, done = 256 * bt, sem["cel%d" % bt]
+        V.tensor_tensor_scan(T.rm[:, rm:rm + 256], T.top[:], T.psT[:, 0:256], -BIG, Op.min, Op.max).then_inc(done, 1)
+        V.wait_ge(done, 1)
+        lt = T.ltb[:, 16 * bt:16 * bt + 16]
+        unit = (T.scol[:, 0:1], 64.0, 16.0)[bt]
+        V.tensor_scalar(lt, T.rm[:, rm + 15:rm + 256:16], T.rm[:, rm + 255:rm + 256], unit, Op.is_lt, Op.mult).then_inc(done, 1)
+        V.wait_ge(done, 2)
+        V.tensor_reduce(T.cc[:, 4 * bt:4 * bt + 1], lt, AxisListType.X, Op.add).then_inc(done, 1)
+        V.wait_ge(done, 3)
+        V.tensor_scalar(T.bc[:, 128 * bt:128 * bt + 128], T.p16[:], T.cc[:, 4 * bt:4 * bt + 1], None, Op.add).then_inc(sem["bcx%d" % bt], 1)
+
+    def lists_v(bt):
+        V.wait_ge(sem["ctx%d" % bt], 1)
+        s = 2 * step[bt] * 2 if bt else 4
+        src = T.psT[:, 256 + s - 1:384:s]
+        if bt == 2:
+            V.tensor_scalar(T.offl[:, 8:24], src, 0.0, None, Op.add).then_inc(sem.ofx2, 1)
+            V.wait_ge(sem.ofx2, 2)
+            return
+        end = (128, 192)[bt]
+        for e in range(4):
+            V.tensor_scalar(T.off[:, 128 * bt + e:end:4], src, 16.0 * e, None, Op.add).then_inc(sem["ofx%d" % bt], 1)
+        V.wait_ge(sem["ofx%d" % bt], 4)
+
+    share = {r: (22 if r in first else 18) for r in chosen_ranks}
+
+    def gather_s(r):
+        j, k = sl[r], share[r]
+        S.activation(T.hb[:, 1024 * j + 16 * k:1024 * j + 512], T.xb[:, 0:1024].indirect(T.off[:, 32 * j + k:32 * j + 32]), Copy).then_inc(sem["gs%d" % j], 1)
+        S.activation(T.hb[:, 1024 * j + 512:1024 * j + 1024], T.rb[:, 0:1024].indirect(T.off[:, 32 * j:32 * j + 32]), Copy).then_inc(sem["gs%d" % j], 1)
+
+    def gather_v(r):
+        j, k = sl[r], share[r]
+        V.tensor_copy(T.hb[:, 1024 * j:1024 * j + 16 * k], T.xb[:, 0:1024].indirect(T.off[:, 32 * j:32 * j + k])).then_inc(sem["gv%d" % j], 1)
+
+    def pack_v(r):
+        j = sl[r]
+        V.wait_ge(sem["gv%d" % j], 1)
+        V.wait_ge(sem["gs%d" % j], 2)
+        V.quantize_mx(xcol(T.OC, j), xcol(T.OS, j), T.hb[:, 1024 * j:1024 * j + 1024]).then_inc(sem["qz%d" % j], 1)
+
+    whole = [me] + W
+
+    def pick_v(i):
+        s = whole[i]
+        V.wait_ge(sem["pc%d" % i], 1)
+        V.tensor_copy(T.ysb[:, 128 * s:128 * s + 128], T.pf[:, 256 * i:256 * i + 256].indirect(T.offl[:, 8 * i:8 * i + 8])).then_inc(sem["yg%d" % i], 1)
+
+    def full(i, ps, parts):
+        for part, (c, p) in enumerate(parts):
+            mm = PE.matmul_mx(ps, qcol(T.QC, own), qcol(T.QS, own), c, p, part == 0, part == 1)
+        mm.then_inc(sem["pm%d" % i], 1)
+
+    def wparts(f):
+        return [(xcol(T.FC, 2 * f + part), xcol(T.FS, 2 * f + part)) for part in range(2)]
+
+    bankA = [T.psA[:, 0:256], T.psA[:, 512:768]]
+    bankY = [T.psY[:, 512 * i:512 * i + 256] for i in range(3)]
+    PE.wait_ge(sem.qq, 1)
+    score("own")
+    for j in (2 * fp, 2 * fp + 1):
+        PE.wait_ge(sem["q%d" % plan["slots"][j]], 16)
+    score("b0f")
+    PE.wait_ge(sem["q%d" % plan["slots"][single]], 16)
+    PE.wait_ge(sem.snown0, 1)
+    PE.wait_ge(sem.snown1, 1)
+    score("b0s")
+    PE.wait_ge(sem.qr, 1)
+    full(0, bankY[2], [(T.XC[:], T.XS[:]), (T.RC[:], T.RS[:])])
+    PE.wait_ge(sem.gi, 1)
+    turn(0, ["own", "b0f", "b0s"])
+    spread(0)
+    for r in B:
+        PE.wait_ge(sem["q%d" % r], 16)
+    score("b1f")
+    PE.wait_ge(sem.ofx0, 4)
+    turn(1, ["b1f"])
+    spread(1)
+    for f in range(2):
+        PE.wait_ge(sem["w%d0" % f], 16)
+        score("w%d" % f)
+    PE.wait_ge(sem.pc0, 1)
+    PE.wait_ge(sem.w01, 16)
+    full(1, bankY[2], wparts(0))
+    PE.wait_ge(sem.ofx1, 4)
+    turn(2, ["w0", "w1"])
+    PE.wait_ge(sem.w11, 16)
+    full(2, bankA[0], wparts(1))
+    spread(2)
+
+    V.wait_ge(sem.mk, 2)
+    V.wait_ge(sem.mtop, 1)
+    groups_v("own")
+    groups_v("b0f")
+    groups_v("b0s")
+    V.wait_ge(sem.gp, 2)
+    V.wait_ge(sem.ms, 2)
+    cells_v(0)
+    lists_v(0)
+    gather_v(first[0])
+    groups_v("b1f")
+    pack_v(first[0])
+    gather_v(first[1])
+    cells_v(1)
+    pack_v(first[1])
+    gather_v(first[2])
+    lists_v(1)
+    gather_v(second[0])
+    pack_v(first[2])
+    gather_v(second[1])
+    V.wait_ge(sem.mch, 3)
+    V.tensor_scalar(T.chrow[0:1, 0:48], T.off[0:1, 0:192:4], 1.0 / 64.0, None, Op.mult).then_inc(sem.chr, 1)
+    pack_v(second[0])
+    groups_v("w0")
+    groups_v("w1")
+    pack_v(second[1])
+    V.tensor_scalar(T.offl[:, 0:8], T.off[:, 32 * own:32 * own + 32:4], 0.0, None, Op.add).then_inc(sem.ofx2, 1)
+    V.wait_ge(sem.ofx2, 1)
+    pick_v(0)
+    cells_v(2)
+    lists_v(2)
+    pick_v(1)
+    pick_v(2)
+
+    def keep_s(i, ps):
+        S.wait_ge(sem["pm%d" % i], 1)
+        S.activation(T.pf[:, 256 * i:256 * i + 256], ps, Copy).then_inc(sem["pc%d" % i], 1)
+
+    for b in range(4):
+        S.wait_ge(sem["rs%d" % b], 1)
+    keep_s(0, bankY[2])
+    S.wait_ge(sem.ofx0, 4)
+    for r in first:
+        gather_s(r)
+    S.wait_ge(sem.ofx1, 4)
+    for r in second:
+        gather_s(r)
+    keep_s(1, bankY[2])
+    keep_s(2, bankA[0])
+
+    sent = [0]
+
+    def tr(src, dsts, mask, rsem):
+        ids = []
+        for c, ap in dsts:
+            rid, pid = topo.addr(c, core)
+            ids.append(DstId(rid=rid, pnc=pid))
+        sent[0] += count(mask)
+        return RemoteDMATransfer(dst_ids=ids, dma_engine_mask=mask, remote_sem=rsem, srcs=[src], dsts=[ap for c, ap in dsts])
+
+    def post(*transfers):
+        g.remote_dma_fused(list(transfers), local_sem=sem.sent)
+
+    far = topo.mask(core, cores[P[0]])
+    for r in P + [M] + X:
+        far &= topo.mask(core, cores[r])
+    near = topo.mask(core, relays[0]) & topo.mask(core, relays[1]) & ~far
+
+    g.iota(T.p16[:], [[0, 8], [1, 16]], 0, 0, allow_small_or_imprecise_dtypes=True).then_inc(sem.gp, 1)
+    g.iota(T.pcol[:], [[0, 8]], 0, 1, allow_small_or_imprecise_dtypes=True).then_inc(sem.gp, 1)
+    g.wait_ge(sem.mo, 1)
+    g.affine_select(T.eb[:], T.ob[:], [[-1, 528]], Op.is_equal, 0.0, 4, 4).then_inc(sem.ge, 1)
+
+    g.wait_ge(sem.qq, 1)
+    qsem = sem["q%d" % me]
+    for ranks in (P, B):
+        at = [(cores[r], plans[r]["slots"].index(me)) for r in ranks]
+        post(tr(qcol(T.QC, own).bitcast(u8), [(c, qcol(T.QC, j).bitcast(u8)) for c, j in at], far, qsem))
+        post(tr(qcol(T.QS, own), [(c, qcol(T.QS, j)) for c, j in at], far, qsem))
+
+    g.wait_ge(sem.mf, 1)
+    g.affine_select(T.idn[:], T.onf[:], [[-1, 128]], Op.is_equal, 0.0, 0, 1).then_inc(sem.gi, 1)
+
+    for part, (c, p, ready) in enumerate(((T.XC, T.XS, sem.qx), (T.RC, T.RS, sem.qr))):
+        g.wait_ge(ready, 1)
+        post(tr(c[:].bitcast(u8), [(h, xcol(T.HFC, part).bitcast(u8)) for h in relays], near, sem["hfc%d" % part]))
+        post(tr(p[:], [(h, xcol(T.HFS, part)) for h in relays], near, sem["hfs%d" % part]))
+    g.affine_select(T.m24[:], T.onf[:, 0:24], [[0, 3], [-1, 8]], Op.is_equal, 0.0, 0, 1).then_inc(sem.gm, 1)
+
+    def send_chosen(r):
+        j = sl[r]
+        g.wait_ge(sem["qz%d" % j], 1)
+        if r in plan["x_relay"]:
+            h = relays[plan["x_relay"][r]]
+            post(tr(xcol(T.OC, j).bitcast(u8), [(h, T.HXC[:].bitcast(u8))], near, sem.hxc))
+            post(tr(xcol(T.OS, j), [(h, T.HXS[:])], near, sem.hxs))
+        else:
+            k = plans[r]["slots"].index(me)
+            post(tr(xcol(T.OC, j).bitcast(u8), [(cores[r], xcol(T.LC, k).bitcast(u8))], far, sem["d%d" % me]))
+            post(tr(xcol(T.OS, j), [(cores[r], xcol(T.LS, k))], far, sem["d%d" % me]))
+
+    for r in chosen_ranks[:-1]:
+        send_chosen(r)
+    one = 1 << topo.engines(core, cores[M])[0]
+    g.wait_ge(sem.chs, 16)
+    post(tr(T.chd[:], [(cores[r], T.chland[me]) for r in chosen_ranks], one, sem.chi))
+    send_chosen(chosen_ranks[-1])
+    g.wait_ge(sem.sent, sent[0])
+
+    ybank = [T.psY[:, 0:128], T.psY[:, 512:640], T.psA[:, 512:640], T.psY[:, 1024:1152], T.psA[:, 0:128]]
+    for i, s in enumerate(plan["yorder"]):
+        j = sl[s]
+        PE.wait_ge(sem["d%d" % s], 16)
+        if i >= 3:
+            PE.wait_ge(sem["pc%d" % (i - 2)], 1)
+        for part in range(2):
+            a = 256 * j + 128 * part
+            mm = PE.matmul_mx(ybank[i], qcol(T.QC, own), qcol(T.QS, own), T.LC[:, a:a + 128], T.LS[:, a:a + 128], part == 0, part == 1)
+        mm.then_inc(sem["ym%d" % j], 1)
+        S.wait_ge(sem["ym%d" % j], 1)
+        S.activation(T.ysb[:, 128 * s:128 * s + 128], ybank[i], Copy).then_inc(sem["yc%d" % j], 1)
+        S.wait_ge(sem["yc%d" % j], 1)
+        S.dma_start(T.y[:, 128 * s:128 * s + 128], T.ysb[:, 128 * s:128 * s + 128]).then_inc(sem.yd, 16)
+    S.wait_ge(sem.yd, 16 * len(plan["yorder"]))
+
+    SY.wait_ge(sem.chr, 1)
+    SY.dma_start(T.chd[:], T.chrow[0:1, :]).then_inc(sem.chs, 16)
+
+    def store_sy(i):
+        s = whole[i]
+        SY.wait_ge(sem["yg%d" % i], 1)
+        SY.dma_start(T.y[:, 128 * s:128 * s + 128], T.ysb[:, 128 * s:128 * s + 128]).then_inc(sem.ye, 16)
+
+    store_sy(0)
+    SY.wait_ge(sem.chi, len(chosen_ranks))
+    SY.wait_ge(sem.mch, 3)
+    for s in chosen_ranks:
+        a = 8 * plans[s]["slots"].index(me)
+        SY.dma_start(T.chc[s:s + 1, 0:8], T.chland[s:s + 1, a:a + 8, 0]).then_inc(sem.chg, 16)
+    store_sy(1)
+    store_sy(2)
+    V.tensor_scalar(T.chk[0:8, :], T.offl[0:8, 0:24], T.pcol[0:8, 0:1], 1.0 / 16.0, Op.subtract, Op.mult).then_inc(sem.chv, 1)
+    V.wait_ge(sem.chv, 1)
+    V.wait_ge(sem.gm, 1)
+    V.tensor_tensor(T.chm[0:8, :], T.chk[0:8, :], T.m24[0:8, :], Op.mult).then_inc(sem.chv, 1)
+    V.wait_ge(sem.chv, 2)
+    for i, s in enumerate(whole):
+        V.tensor_reduce(T.chl[0:8, s:s + 1], T.chm[0:8, 8 * i:8 * i + 8], AxisListType.X, Op.add).then_inc(sem.chl1, 1)
+    V.wait_ge(sem.chg, 16 * len(chosen_ranks))
+    V.transpose(T.cht[0:32, :], T.chc[0:32, :]).then_inc(sem.chv, 1)
+    V.wait_ge(sem.chv, 3)
+    V.wait_ge(sem.chl1, len(whole))
+    V.tensor_tensor(T.chf[0:8, :], T.cht[0:8, 0:8], T.chl[0:8, :], Op.add).then_inc(sem.chf1, 1)
+    SY.wait_ge(sem.chf1, 1)
+    SY.dma_start(T.ch[:], T.chf[0:8, :]).then_inc(sem.cho, 16)
+    SY.wait_ge(sem.cho, 16)
+    SY.wait_ge(sem.ye, 16 * len(whole))
+
+
+def relay_program(g, core, me, T, topo):
+    plan = make_plan(me, T, topo)
+    if core not in plan["relays"]:
+        return
+    cores, sem = T.cores, T.sem
+    which = plan["relays"].index(core)
+    home = cores[me]
+    near = topo.mask(home, core) & ~topo.mask(home, cores[plan["P"][0]])
+    arrive = count(near)
+    u8 = dt.uint8
+    sent = [0]
+
+    def send(wait, dst, out, src, rsem):
+        g.wait_ge(wait, arrive)
+        rid, pid = topo.addr(dst, core)
+        mask = topo.mask(core, dst)
+        sent[0] += count(mask)
+        g.remote_dma_fused([RemoteDMATransfer(dst_ids=[DstId(rid=rid, pnc=pid)], dma_engine_mask=mask, remote_sem=rsem,
+                                              srcs=[src], dsts=[out])], local_sem=sem.sent)
+
+    for r, i in plan["w_relay"].items():
+        if i == which:
+            f = make_plan(r, T, topo)["W"].index(me)
+            for part in range(2):
+                a, k = 256 * part, 512 * f + 256 * part
+                there = sem["w%d%d" % (f, part)]
+                send(sem["hfc%d" % part], cores[r], T.FC[:, k:k + 256].bitcast(u8), T.HFC[:, a:a + 256].bitcast(u8), there)
+                send(sem["hfs%d" % part], cores[r], T.FS[:, k:k + 256], T.HFS[:, a:a + 256], there)
+    for r, i in plan["x_relay"].items():
+        if i == which:
+            k = 256 * make_plan(r, T, topo)["slots"].index(me)
+            there = sem["d%d" % me]
+            send(sem.hxc, cores[r], T.LC[:, k:k + 256].bitcast(u8), T.HXC[:].bitcast(u8), there)
+            send(sem.hxs, cores[r], T.LS[:, k:k + 256], T.HXS[:], there)
+    g.wait_ge(sem.sent, sent[0])

@@ -4,96 +4,97 @@ from concourse.mybir import dt, AluOpType, AxisListType, ActivationFunctionType
 N = 8
 BIG = 1e29
 CODES, PLANE = "float8_e4m3fn_x4", "uint8"
+F32, BF16, U16 = "float32", "bfloat16", "uint16"
 
 SCRATCH = {
-    "qwb": ("sbuf", [128, 512], "bfloat16"),
-    "xb": ("sbuf", [128, 1024], "bfloat16"),
-    "rb": ("sbuf", [128, 1024], "bfloat16"),
-    "ob": ("sbuf", [128, 528], "bfloat16"),
-    "eb": ("sbuf", [128, 528], "bfloat16"),
-    "onf": ("sbuf", [128, 128], "float32"),
-    "idn": ("sbuf", [128, 128], "float32"),
-    "p16": ("sbuf", [128, 128], "float32"),
-    "pcol": ("sbuf", [128, 8], "float32"),
-    "m24": ("sbuf", [128, 24], "float32"),
-    "scol": ("sbuf", [128, 8], "float32"),
-    "msk": ("sbuf", [128, 256], "float32"),
-    "top": ("sbuf", [128, 256], "float32"),
-    "QC": ("sbuf", [128, 128 * 6], CODES),
-    "QS": ("sbuf", [128, 128 * 6], PLANE),
+    "qwb": ("sbuf", [128, 512], BF16),
+    "xb": ("sbuf", [128, 1024], BF16),
+    "rb": ("sbuf", [128, 1024], BF16),
+    "eb": ("sbuf", [128, 528], BF16),
+    "onf": ("sbuf", [128, 128], F32),
+    "idn": ("sbuf", [128, 128], F32),
+    "p16": ("sbuf", [128, 128], F32),
+    "pa": ("sbuf", [128, 128], F32),
+    "pq": ("sbuf", [128, 128], F32),
+    "pm": ("sbuf", [128, 128], F32),
+    "tq": ("sbuf", [128, 128], F32),
+    "uc": ("sbuf", [128, 8], F32),
+    "msk": ("sbuf", [128, 128], F32),
+    "top": ("sbuf", [128, 256], F32),
+    "QC": ("sbuf", [128, 256], CODES),
+    "QS": ("sbuf", [128, 256], PLANE),
     "XC": ("sbuf", [128, 256], CODES),
     "XS": ("sbuf", [128, 256], PLANE),
     "RC": ("sbuf", [128, 256], CODES),
     "RS": ("sbuf", [128, 256], PLANE),
     "EC": ("sbuf", [128, 512], CODES),
     "ES": ("sbuf", [128, 512], PLANE),
-    "sc": ("sbuf", [128, 2048], "float32"),
-    "rm": ("sbuf", [128, 768], "float32"),
-    "ltb": ("sbuf", [128, 48], "float32"),
-    "cc": ("sbuf", [128, 12], "float32"),
-    "bc": ("sbuf", [128, 384], "float32"),
-    "off": ("sbuf", [128, 32 * 6], "uint16"),
-    "offl": ("sbuf", [128, 32], "uint16"),
-    "hb": ("sbuf", [128, 1024 * 6], "bfloat16"),
-    "OC": ("sbuf", [128, 256 * 6], CODES),
-    "OS": ("sbuf", [128, 256 * 6], PLANE),
-    "LC": ("sbuf", [128, 256 * 6], CODES),
-    "LS": ("sbuf", [128, 256 * 6], PLANE),
-    "FC": ("sbuf", [128, 1024], CODES),
-    "FS": ("sbuf", [128, 1024], PLANE),
-    "HFC": ("sbuf", [128, 512], CODES),
-    "HFS": ("sbuf", [128, 512], PLANE),
+    "sc": ("sbuf", [128, 528], F32),
+    "sw": ("sbuf", [128, 1024], F32),
+    "rm": ("sbuf", [128, 512], F32),
+    "ltb": ("sbuf", [128, 32], F32),
+    "cc": ("sbuf", [128, 12], F32),
+    "bc": ("sbuf", [128, 512], F32),
+    "nin": ("sbuf", [128, 20], F32),
+    "off": ("sbuf", [128, 96], U16),
+    "offl": ("sbuf", [128, 40], U16),
+    "offc": ("sbuf", [128, 4], U16),
+    "hb": ("sbuf", [128, 3072], BF16),
+    "OC": ("sbuf", [128, 768], CODES),
+    "OS": ("sbuf", [128, 768], PLANE),
+    "LC": ("sbuf", [128, 768], CODES),
+    "LS": ("sbuf", [128, 768], PLANE),
+    "FXC": ("sbuf", [128, 1024], CODES),
+    "FXS": ("sbuf", [128, 1024], PLANE),
+    "FRC": ("sbuf", [128, 1024], CODES),
+    "FRS": ("sbuf", [128, 1024], PLANE),
+    "HQC": ("sbuf", [128, 128], CODES),
+    "HQS": ("sbuf", [128, 128], PLANE),
     "HXC": ("sbuf", [128, 256], CODES),
     "HXS": ("sbuf", [128, 256], PLANE),
-    "pf": ("sbuf", [128, 768], "float32"),
-    "ysb": ("sbuf", [128, 128 * N], "float32"),
-    "chrow": ("sbuf", [128, 128], "float32"),
-    "chc": ("sbuf", [128, 32], "float32"),
-    "cht": ("sbuf", [128, 32], "float32"),
-    "chk": ("sbuf", [128, 24], "float32"),
-    "chm": ("sbuf", [128, 24], "float32"),
-    "chl": ("sbuf", [128, 8], "float32"),
-    "chf": ("sbuf", [128, 8], "float32"),
-    "chd": ("dram", [128, 1], "float32"),
-    "chland": ("dram", [N, 128, 1], "float32"),
-    "psD": ("psum", [128, 1024], "float32"),
-    "psA": ("psum", [128, 1024], "float32"),
-    "psT": ("psum", [128, 512], "float32"),
-    "psY": ("psum", [128, 1536], "float32"),
+    "HRC": ("sbuf", [128, 512], CODES),
+    "HRS": ("sbuf", [128, 512], PLANE),
+    "pf": ("sbuf", [128, 1280], F32),
+    "ysb": ("sbuf", [128, 128 * N], F32),
+    "chf": ("sbuf", [128, 128], F32),
+    "chg": ("sbuf", [128, 64], F32),
+    "psD": ("psum", [128, 1024], F32),
+    "psT": ("psum", [128, 1024], F32),
+    "psP": ("psum", [128, 2048], F32),
 }
-UNITS = ["own", "b0f", "b0s", "b1f", "w0", "w1"]
 SEMAPHORES = (
-    ["lq", "lx", "mo", "mf", "mk", "mtop", "mch", "ms", "qq", "qx", "qr", "qe", "ge", "gi", "gp", "gm"]
+    ["lq", "lx", "mf", "me", "mk", "mt", "mu", "qq", "qx", "qr", "qe", "gi", "gp", "gt", "sp", "tc", "oc"]
     + ["dm%d" % b for b in range(4)] + ["rs%d" % b for b in range(4)]
-    + [n + u + str(h) for n in ("sm", "sn") for u in UNITS for h in range(2)]
-    + ["tr%d%d" % (b, h) for b in range(3) for h in range(2)]
-    + [n + str(b) for n in ("cel", "bcx", "ctx", "ofx", "pm", "pc", "yg") for b in range(3)]
-    + [n + str(j) for n in ("gv", "gs", "qz", "ym", "yc") for j in range(6)]
-    + [n + str(j) for n in ("q", "d") for j in range(N)]
-    + ["w" + str(i) + str(part) for i in range(2) for part in range(2)]
-    + ["yd", "ye", "chr", "chs", "chi", "chg", "chv", "chl1", "chf1", "cho", "sent"]
-    + ["hfc0", "hfs0", "hfc1", "hfs1", "hxc", "hxs"]
+    + [n + str(u) for n in ("sm", "sn") for u in range(12)]
+    + ["tr%d%d" % (b, h) for b in range(2) for h in range(2)]
+    + [n + str(b) for n in ("bcx", "ctx", "ofx") for b in range(4)]
+    + [n + str(b) for n in ("cel", "n", "hrc", "hrs") for b in range(2)]
+    + [n + str(j) for n in ("gv", "gs", "qz", "ym", "yc", "d", "pm", "pc") for j in range(3)]
+    + [n + str(j) for n in ("wx", "wr") for j in range(4)]
+    + ["yg%d" % j for j in range(5)]
+    + ["qm", "an", "tn", "chv", "yd", "ye", "sent", "hq", "hxc", "hxs"]
 )
+ENDS = (13, 12)
+SHARE = (22, 20, 26)
+EARLY = (8, 8, 8)
 
 
 def make_plan(me, T, topo):
     cores = T.cores
     core = cores[me]
-    same = [r for r in range(N) if r == me or topo.same_plane(core, cores[r])]
-    other = [r for r in range(N) if r not in same]
-    mate = [r for r in other if topo.mates(core, cores[r])][0]
-    P = sorted([r for r in same if r != me], key=lambda r: r ^ me)
-    X = sorted([r for r in other if r != mate], key=lambda r: r ^ me)
-    relays = [c for c in topo.cores_of(core) if topo.die(c) != topo.die(core)
-              and all(topo.may_write(c, cores[x]) for x in X)]
-    near2 = sorted([mate, X[2]])
+
+    def mate_of(r):
+        return [s for s in range(N) if topo.mates(cores[r], cores[s])][0]
+
+    ring = [r for r in range(N) if r == me or topo.same_plane(core, cores[r])]
+    k, n = ring.index(me), len(ring)
+    mate, before, after, across = mate_of(me), ring[(k - 1) % n], ring[(k + 1) % n], ring[(k + 2) % n]
+    free = [c for c in topo.cores_of(core) if c != core and topo.may_write(c, cores[mate])]
     return {
-        "P": P, "M": mate, "X": X, "same": same, "relays": relays[:2], "W": sorted(X[:2]), "B": near2,
-        "slots": same + near2,
-        "w_relay": {X[0]: 0, X[1]: 1},
-        "x_relay": {P[0]: 0, P[2]: 1},
-        "first": [P[0], P[2], P[1]], "second": [X[2], mate],
-        "yorder": [P[0], P[1], P[2], X[2], mate],
+        "mate": mate, "to": [after, before], "chosen": [mate, across, mate_of(across)],
+        "whole": [before, mate_of(before), after, mate_of(after)],
+        "inb": [c for c in free if topo.die(c) == topo.die(core)][0],
+        "out": [c for c in free if topo.die(c) != topo.die(core)][:2],
     }
 
 
@@ -101,249 +102,7 @@ def count(mask):
     return bin(mask).count("1")
 
 
-def rank_program(g, core, T, topo):
-    me = T.rank_of(core)
-    if me is None:
-        homes = [T.rank_of(c) for c in topo.cores_of(core) if T.rank_of(c) is not None]
-        if homes:
-            relay_program(g, core, homes[0], T, topo)
-        return
-    plans = [make_plan(r, T, topo) for r in range(N)]
-    plan = plans[me]
-    P, M, X, W, B, relays = plan["P"], plan["M"], plan["X"], plan["W"], plan["B"], plan["relays"]
-    first, second = plan["first"], plan["second"]
-    chosen_ranks = first + second
-    cores = T.cores
-    sem = T.sem
-    sl = {r: j for j, r in enumerate(plan["slots"])}
-    own = sl[me]
-    u8 = dt.uint8
-    Op = AluOpType
-    Copy = ActivationFunctionType.Copy
-    V, S, PE, SY = g.vector, g.scalar, g.tensor, g.sync
-
-    def qcol(t, j):
-        return t[:, 128 * j:128 * j + 128]
-
-    def xcol(t, j):
-        return t[:, 256 * j:256 * j + 256]
-
-    SY.dma_start(T.qwb[:], T.qw[:]).then_inc(sem.lq, 16)
-    S.dma_start(T.xb[:], T.x[:]).then_inc(sem.lx, 16)
-
-    V.memset(T.ob[:], 1.0).then_inc(sem.mo, 1)
-    V.memset(T.onf[:], 1.0).then_inc(sem.mf, 1)
-    V.memset(T.msk[:], BIG).then_inc(sem.mk, 1)
-    V.memset(T.top[:], BIG).then_inc(sem.mtop, 1)
-    V.memset(T.scol[:], 64.0).then_inc(sem.ms, 1)
-    V.memset(T.chrow[:], 0.0).then_inc(sem.mch, 1)
-    V.memset(T.chc[:], 0.0).then_inc(sem.mch, 1)
-    V.memset(T.chl[:], 0.0).then_inc(sem.mch, 1)
-    V.wait_ge(sem.mk, 1)
-    V.memset(T.msk[:, 0:256:16], -BIG).then_inc(sem.mk, 1)
-    V.wait_ge(sem.ms, 1)
-    V.memset(T.scol[32 * own:32 * own + 32, :], 16.0).then_inc(sem.ms, 1)
-    V.wait_ge(sem.lq, 16)
-    V.quantize_mx(qcol(T.QC, own), qcol(T.QS, own), T.qwb[:]).then_inc(sem.qq, 1)
-    V.wait_ge(sem.lx, 16)
-    V.quantize_mx(T.XC[:], T.XS[:], T.xb[:]).then_inc(sem.qx, 1)
-    V.wait_ge(sem.ge, 1)
-    for b in range(4):
-        V.quantize_mx(qcol(T.EC, b), qcol(T.ES, b), T.eb[:, 4 - b:516 - b]).then_inc(sem.qe, 1)
-    for b in range(4):
-        V.wait_ge(sem["dm%d" % b], 1)
-        k = 512 * (b % 2)
-        V.tensor_tensor(T.rb[:, b:1024:4], T.xb[:, b:1024:4], T.psD[:, k:k + 256], Op.subtract).then_inc(sem["rs%d" % b], 1)
-    for b in range(4):
-        V.wait_ge(sem["rs%d" % b], 1)
-    V.quantize_mx(T.RC[:], T.RS[:], T.rb[:]).then_inc(sem.qr, 1)
-
-    PE.wait_ge(sem.qx, 1)
-    PE.wait_ge(sem.qe, 4)
-    for b in range(4):
-        if b >= 2:
-            PE.wait_ge(sem["rs%d" % (b - 2)], 1)
-        k = 512 * (b % 2)
-        PE.matmul_mx(T.psD[:, k:k + 256], qcol(T.EC, b), qcol(T.ES, b), T.XC[:], T.XS[:], True, True).then_inc(sem["dm%d" % b], 1)
-
-    base, wide, step = (0, 1024, 1536), (512, 256, 256), (4, 2, 2)
-    fp = 1 - own // 2
-    single = own + 1 - 2 * (own % 2)
-    units = {"own": (0, 128 * own, 128, T.psY), "b0f": (0, 256 * fp, 256, T.psA), "b0s": (0, 128 * single, 128, T.psY),
-             "b1f": (1, 0, 256, T.psA), "w0": (2, 0, 128, T.psA), "w1": (2, 128, 128, T.psY)}
-
-    def score(u):
-        bt, a, n, ps = units[u]
-        for h in range(2):
-            if bt < 2:
-                k = 512 * bt + a
-                args = (qcol(T.XC, h), qcol(T.XS, h), T.QC[:, k:k + n], T.QS[:, k:k + n])
-            else:
-                k = 512 * (a // 128) + 128 * h
-                args = (T.FC[:, k:k + 128], T.FS[:, k:k + 128], qcol(T.QC, own), qcol(T.QS, own))
-            PE.matmul_mx(ps[:, 512 * h:512 * h + n], *args, True, True).then_inc(sem["sm%s%d" % (u, h)], 1)
-
-    def groups_v(u):
-        bt, a, n, ps = units[u]
-        for h in range(2):
-            k = base[bt] + wide[bt] * h + a
-            V.wait_ge(sem["sm%s%d" % (u, h)], 1)
-            V.tensor_tensor_scan(T.sc[:, k:k + n], T.msk[:, 0:n], ps[:, 512 * h:512 * h + n], -BIG, Op.min, Op.max).then_inc(sem["sn%s%d" % (u, h)], 1)
-
-    def turn(bt, us):
-        for h in range(2):
-            k = base[bt] + wide[bt] * h
-            for u in us:
-                PE.wait_ge(sem["sn%s%d" % (u, h)], 1)
-            PE.transpose(T.psT[:, 128 * h:128 * h + 128], T.sc[:, k + step[bt] - 1:k + wide[bt]:step[bt]], T.idn[:]).then_inc(sem["tr%d%d" % (bt, h)], 1)
-
-    def spread(bt):
-        PE.wait_ge(sem["bcx%d" % bt], 1)
-        PE.transpose(T.psT[:, 256:384], T.bc[:, 128 * bt:128 * bt + 128], T.idn[:]).then_inc(sem["ctx%d" % bt], 1)
-
-    def cells_v(bt):
-        V.wait_ge(sem["tr%d0" % bt], 1)
-        V.wait_ge(sem["tr%d1" % bt], 1)
-        rm, done = 256 * bt, sem["cel%d" % bt]
-        V.tensor_tensor_scan(T.rm[:, rm:rm + 256], T.top[:], T.psT[:, 0:256], -BIG, Op.min, Op.max).then_inc(done, 1)
-        V.wait_ge(done, 1)
-        lt = T.ltb[:, 16 * bt:16 * bt + 16]
-        unit = (T.scol[:, 0:1], 64.0, 16.0)[bt]
-        V.tensor_scalar(lt, T.rm[:, rm + 15:rm + 256:16], T.rm[:, rm + 255:rm + 256], unit, Op.is_lt, Op.mult).then_inc(done, 1)
-        V.wait_ge(done, 2)
-        V.tensor_reduce(T.cc[:, 4 * bt:4 * bt + 1], lt, AxisListType.X, Op.add).then_inc(done, 1)
-        V.wait_ge(done, 3)
-        V.tensor_scalar(T.bc[:, 128 * bt:128 * bt + 128], T.p16[:], T.cc[:, 4 * bt:4 * bt + 1], None, Op.add).then_inc(sem["bcx%d" % bt], 1)
-
-    def lists_v(bt):
-        V.wait_ge(sem["ctx%d" % bt], 1)
-        s = 2 * step[bt] * 2 if bt else 4
-        src = T.psT[:, 256 + s - 1:384:s]
-        if bt == 2:
-            V.tensor_scalar(T.offl[:, 8:24], src, 0.0, None, Op.add).then_inc(sem.ofx2, 1)
-            V.wait_ge(sem.ofx2, 2)
-            return
-        end = (128, 192)[bt]
-        for e in range(4):
-            V.tensor_scalar(T.off[:, 128 * bt + e:end:4], src, 16.0 * e, None, Op.add).then_inc(sem["ofx%d" % bt], 1)
-        V.wait_ge(sem["ofx%d" % bt], 4)
-
-    share = {r: (22 if r in first else 18) for r in chosen_ranks}
-
-    def gather_s(r):
-        j, k = sl[r], share[r]
-        S.activation(T.hb[:, 1024 * j + 16 * k:1024 * j + 512], T.xb[:, 0:1024].indirect(T.off[:, 32 * j + k:32 * j + 32]), Copy).then_inc(sem["gs%d" % j], 1)
-        S.activation(T.hb[:, 1024 * j + 512:1024 * j + 1024], T.rb[:, 0:1024].indirect(T.off[:, 32 * j:32 * j + 32]), Copy).then_inc(sem["gs%d" % j], 1)
-
-    def gather_v(r):
-        j, k = sl[r], share[r]
-        V.tensor_copy(T.hb[:, 1024 * j:1024 * j + 16 * k], T.xb[:, 0:1024].indirect(T.off[:, 32 * j:32 * j + k])).then_inc(sem["gv%d" % j], 1)
-
-    def pack_v(r):
-        j = sl[r]
-        V.wait_ge(sem["gv%d" % j], 1)
-        V.wait_ge(sem["gs%d" % j], 2)
-        V.quantize_mx(xcol(T.OC, j), xcol(T.OS, j), T.hb[:, 1024 * j:1024 * j + 1024]).then_inc(sem["qz%d" % j], 1)
-
-    whole = [me] + W
-
-    def pick_v(i):
-        s = whole[i]
-        V.wait_ge(sem["pc%d" % i], 1)
-        V.tensor_copy(T.ysb[:, 128 * s:128 * s + 128], T.pf[:, 256 * i:256 * i + 256].indirect(T.offl[:, 8 * i:8 * i + 8])).then_inc(sem["yg%d" % i], 1)
-
-    def full(i, ps, parts):
-        for part, (c, p) in enumerate(parts):
-            mm = PE.matmul_mx(ps, qcol(T.QC, own), qcol(T.QS, own), c, p, part == 0, part == 1)
-        mm.then_inc(sem["pm%d" % i], 1)
-
-    def wparts(f):
-        return [(xcol(T.FC, 2 * f + part), xcol(T.FS, 2 * f + part)) for part in range(2)]
-
-    bankA = [T.psA[:, 0:256], T.psA[:, 512:768]]
-    bankY = [T.psY[:, 512 * i:512 * i + 256] for i in range(3)]
-    PE.wait_ge(sem.qq, 1)
-    score("own")
-    for j in (2 * fp, 2 * fp + 1):
-        PE.wait_ge(sem["q%d" % plan["slots"][j]], 16)
-    score("b0f")
-    PE.wait_ge(sem["q%d" % plan["slots"][single]], 16)
-    PE.wait_ge(sem.snown0, 1)
-    PE.wait_ge(sem.snown1, 1)
-    score("b0s")
-    PE.wait_ge(sem.qr, 1)
-    full(0, bankY[2], [(T.XC[:], T.XS[:]), (T.RC[:], T.RS[:])])
-    PE.wait_ge(sem.gi, 1)
-    turn(0, ["own", "b0f", "b0s"])
-    spread(0)
-    for r in B:
-        PE.wait_ge(sem["q%d" % r], 16)
-    score("b1f")
-    PE.wait_ge(sem.ofx0, 4)
-    turn(1, ["b1f"])
-    spread(1)
-    for f in range(2):
-        PE.wait_ge(sem["w%d0" % f], 16)
-        score("w%d" % f)
-    PE.wait_ge(sem.pc0, 1)
-    PE.wait_ge(sem.w01, 16)
-    full(1, bankY[2], wparts(0))
-    PE.wait_ge(sem.ofx1, 4)
-    turn(2, ["w0", "w1"])
-    PE.wait_ge(sem.w11, 16)
-    full(2, bankA[0], wparts(1))
-    spread(2)
-
-    V.wait_ge(sem.mk, 2)
-    V.wait_ge(sem.mtop, 1)
-    groups_v("own")
-    groups_v("b0f")
-    groups_v("b0s")
-    V.wait_ge(sem.gp, 2)
-    V.wait_ge(sem.ms, 2)
-    cells_v(0)
-    lists_v(0)
-    gather_v(first[0])
-    groups_v("b1f")
-    pack_v(first[0])
-    gather_v(first[1])
-    cells_v(1)
-    pack_v(first[1])
-    gather_v(first[2])
-    lists_v(1)
-    gather_v(second[0])
-    pack_v(first[2])
-    gather_v(second[1])
-    V.wait_ge(sem.mch, 3)
-    V.tensor_scalar(T.chrow[0:1, 0:48], T.off[0:1, 0:192:4], 1.0 / 64.0, None, Op.mult).then_inc(sem.chr, 1)
-    pack_v(second[0])
-    groups_v("w0")
-    groups_v("w1")
-    pack_v(second[1])
-    V.tensor_scalar(T.offl[:, 0:8], T.off[:, 32 * own:32 * own + 32:4], 0.0, None, Op.add).then_inc(sem.ofx2, 1)
-    V.wait_ge(sem.ofx2, 1)
-    pick_v(0)
-    cells_v(2)
-    lists_v(2)
-    pick_v(1)
-    pick_v(2)
-
-    def keep_s(i, ps):
-        S.wait_ge(sem["pm%d" % i], 1)
-        S.activation(T.pf[:, 256 * i:256 * i + 256], ps, Copy).then_inc(sem["pc%d" % i], 1)
-
-    for b in range(4):
-        S.wait_ge(sem["rs%d" % b], 1)
-    keep_s(0, bankY[2])
-    S.wait_ge(sem.ofx0, 4)
-    for r in first:
-        gather_s(r)
-    S.wait_ge(sem.ofx1, 4)
-    for r in second:
-        gather_s(r)
-    keep_s(1, bankY[2])
-    keep_s(2, bankA[0])
-
+def writer(g, core, T, topo):
     sent = [0]
 
     def tr(src, dsts, mask, rsem):
@@ -355,136 +114,400 @@ def rank_program(g, core, T, topo):
         return RemoteDMATransfer(dst_ids=ids, dma_engine_mask=mask, remote_sem=rsem, srcs=[src], dsts=[ap for c, ap in dsts])
 
     def post(*transfers):
-        g.remote_dma_fused(list(transfers), local_sem=sem.sent)
+        g.remote_dma_fused(list(transfers), local_sem=T.sem.sent)
 
-    far = topo.mask(core, cores[P[0]])
-    for r in P + [M] + X:
-        far &= topo.mask(core, cores[r])
-    near = topo.mask(core, relays[0]) & topo.mask(core, relays[1]) & ~far
+    def finish():
+        g.wait_ge(T.sem.sent, sent[0])
 
+    return tr, post, finish
+
+
+def col(t, j, n):
+    return t[:, n * j:n * j + n]
+
+
+def raw(ap):
+    return ap.bitcast(dt.uint8)
+
+
+def cells(V, T, bt, unit):
+    Op, sem = AluOpType, T.sem
+    V.wait_ge(sem["tr%d0" % bt], 1)
+    V.wait_ge(sem["tr%d1" % bt], 1)
+    rm, done, lt = 256 * bt, sem["cel%d" % bt], col(T.ltb, bt, 16)
+    V.tensor_tensor_scan(T.rm[:, rm:rm + 256], T.top[:], T.psT[:, 0:256], -BIG, Op.min, Op.max).then_inc(done, 1)
+    V.wait_ge(done, 1)
+    V.tensor_scalar(lt, T.rm[:, rm + 15:rm + 256:16], T.rm[:, rm + 255:rm + 256], unit, Op.is_lt, Op.mult).then_inc(done, 1)
+    V.wait_ge(done, 2)
+    V.tensor_reduce(T.cc[:, 4 * bt:4 * bt + 1], lt, AxisListType.X, Op.add).then_inc(done, 1)
+
+
+def rank_program(g, core, T, topo):
+    me = T.rank_of(core)
+    if me is None:
+        homes = [T.rank_of(c) for c in topo.cores_of(core) if T.rank_of(c) is not None]
+        if homes:
+            plan = make_plan(homes[0], T, topo)
+            if core in plan["out"]:
+                scorer_program(g, core, homes[0], T, topo)
+            if core == plan["inb"]:
+                relay_program(g, core, homes[0], T, topo)
+        return
+    plans = [make_plan(r, T, topo) for r in range(N)]
+    plan = plans[me]
+    chosen, whole = plan["chosen"], plan["whole"]
+    cores, sem = T.cores, T.sem
+    Op = AluOpType
+    Copy = ActivationFunctionType.Copy
+    V, S, PE, SY = g.vector, g.scalar, g.tensor, g.sync
+    Q = (col(T.QC, 0, 128), col(T.QS, 0, 128))
+    far = topo.mask(core, cores[chosen[0]])
+    near = topo.mask(core, plan["out"][0]) & ~far
+
+    def bank(b, n):
+        return T.psP[:, 512 * b:512 * b + n]
+
+    SY.dma_start(T.qwb[:], T.qw[:]).then_inc(sem.lq, 16)
+    S.dma_start(T.xb[:], T.x[:]).then_inc(sem.lx, 16)
+
+    V.memset(T.onf[:], 1.0).then_inc(sem.mf, 1)
+    V.memset(T.eb[:], 0.0).then_inc(sem.me, 1)
+    V.memset(T.msk[:], BIG).then_inc(sem.mk, 1)
+    V.wait_ge(sem.me, 1)
+    V.wait_ge(sem.gi, 1)
+    V.tensor_copy(T.eb[:, 4:516:4], T.idn[:]).then_inc(sem.me, 1)
+    V.wait_ge(sem.mk, 1)
+    V.memset(T.msk[:, 0:128:16], -BIG).then_inc(sem.mk, 1)
+    V.wait_ge(sem.me, 2)
+    for b in range(4):
+        V.quantize_mx(col(T.EC, b, 128), col(T.ES, b, 128), T.eb[:, 4 - b:516 - b]).then_inc(sem.qe, 1)
+    V.wait_ge(sem.lq, 16)
+    V.quantize_mx(Q[0], Q[1], T.qwb[:]).then_inc(sem.qq, 1)
+    V.wait_ge(sem.lx, 16)
+    V.quantize_mx(T.XC[:], T.XS[:], T.xb[:]).then_inc(sem.qx, 1)
+    V.memset(T.top[:], BIG).then_inc(sem.mt, 1)
+    for b in range(4):
+        V.wait_ge(sem["dm%d" % b], 1)
+        k = 512 * (b % 2)
+        V.tensor_tensor(T.rb[:, b:1024:4], T.xb[:, b:1024:4], T.psD[:, k:k + 256], Op.subtract).then_inc(sem["rs%d" % b], 1)
+    for b in range(4):
+        V.wait_ge(sem["rs%d" % b], 1)
+    V.quantize_mx(T.RC[:], T.RS[:], T.rb[:]).then_inc(sem.qr, 1)
+    for h in range(2):
+        V.memset(T.sc[:, 264 * h + 256:264 * h + 264], 0.0).then_inc(sem.mt, 1)
+    V.tensor_reduce(T.uc[:, 0:1], T.idn[:, 6:128:8], AxisListType.X, Op.add).then_inc(sem.mu, 1)
+    V.tensor_reduce(T.uc[:, 1:2], T.idn[:, 3:128:4], AxisListType.X, Op.add).then_inc(sem.mu, 1)
+
+    PE.wait_ge(sem.qx, 1)
+    PE.wait_ge(sem.qe, 4)
+    for b in range(4):
+        if b >= 2:
+            PE.wait_ge(sem["rs%d" % (b - 2)], 1)
+        k = 512 * (b % 2)
+        PE.matmul_mx(T.psD[:, k:k + 256], col(T.EC, b, 128), col(T.ES, b, 128), T.XC[:], T.XS[:], True, True).then_inc(sem["dm%d" % b], 1)
+
+    def score(u, b):
+        h = u % 2
+        if u < 4:
+            args = (col(T.XC, h, 128), col(T.XS, h, 128), col(T.QC, u // 2, 128), col(T.QS, u // 2, 128))
+        else:
+            args = (col(T.FXC, u - 4, 128), col(T.FXS, u - 4, 128)) + Q
+        PE.matmul_mx(bank(b, 128), *args, True, True).then_inc(sem["sm%d" % u], 1)
+
+    def groups(u, b):
+        h = u % 2
+        k = 264 * h + 128 * (u // 2)
+        out = T.sc[:, k:k + 128] if u < 4 else col(T.sw, 4 * h + u // 2 - 2, 128)
+        V.wait_ge(sem["sm%d" % u], 1)
+        V.tensor_tensor_scan(out, T.msk[:], bank(b, 128), -BIG, Op.min, Op.max).then_inc(sem["sn%d" % u], 1)
+
+    def turn(bt):
+        for h in range(2):
+            for u in (range(h, 4, 2), range(4 + h, 12, 2))[bt]:
+                PE.wait_ge(sem["sn%d" % u], 1)
+            src = T.sw[:, 512 * h + 3:512 * h + 512:4] if bt else T.sc[:, 264 * h + 3:264 * h + 259:2]
+            PE.transpose(col(T.psT, h, 128), src, T.idn[:]).then_inc(sem["tr%d%d" % (bt, h)], 1)
+
+    spot = [T.psT[:, 512:640], T.psT[:, 0:128], T.psT[:, 512:640], T.psT[:, 512:640]]
+
+    def spread(i):
+        PE.wait_ge(sem["bcx%d" % i], 1)
+        PE.transpose(spot[i], col(T.bc, i, 128), T.idn[:]).then_inc(sem["ctx%d" % i], 1)
+
+    def widen(i, table, number):
+        V.tensor_scalar(col(T.bc, i, 128), table[:], number, None, Op.add).then_inc(sem["bcx%d" % i], 1)
+
+    def lists(j):
+        V.wait_ge(sem["ctx%d" % j], 1)
+        src = (T.psT[:, 512 + 70:640:8], T.psT[:, ENDS[0]:128:16], T.psT[:, 512 + ENDS[1]:640:16])[j]
+        for e in range(4):
+            V.tensor_scalar(T.off[:, 32 * j + e:32 * j + 32:4], src, 64.0, 16.0 * e, Op.mult, Op.add).then_inc(sem["ofx%d" % j], 1)
+        if j == 0:
+            V.tensor_scalar(T.offl[:, 0:8], T.psT[:, 512 + 6:576:8], 16.0, None, Op.mult).then_inc(sem.ofx0, 1)
+
+    made = (5, 4, 4)
+
+    def gather_s(j):
+        k, a = SHARE[j], 1024 * j
+        S.wait_ge(sem["ofx%d" % j], made[j])
+        S.activation(T.hb[:, a + 16 * k:a + 512], T.xb[:, 0:1024].indirect(T.off[:, 32 * j + k:32 * j + 32]), Copy).then_inc(sem["gs%d" % j], 1)
+        S.activation(T.hb[:, a + 512:a + 1024], T.rb[:, 0:1024].indirect(col(T.off, j, 32)), Copy).then_inc(sem["gs%d" % j], 1)
+
+    def gather_v(j, part):
+        lo, hi = (0, EARLY[j], SHARE[j])[part:part + 2]
+        V.wait_ge(sem["ofx%d" % j], made[j])
+        V.tensor_copy(T.hb[:, 1024 * j + 16 * lo:1024 * j + 16 * hi], T.xb[:, 0:1024].indirect(T.off[:, 32 * j + lo:32 * j + hi])).then_inc(sem["gv%d" % j], 1)
+
+    def pack(j):
+        V.wait_ge(sem["gv%d" % j], 2)
+        V.wait_ge(sem["gs%d" % j], 2)
+        V.quantize_mx(col(T.OC, j, 256), col(T.OS, j, 256), col(T.hb, j, 1024)).then_inc(sem["qz%d" % j], 1)
+
+    every = [me] + whole
+
+    def pick(E, i):
+        out, src = col(T.ysb, every[i], 128), col(T.pf, i, 256).indirect(col(T.offl, i, 8))
+        E.wait_ge(sem["pc%d" % ((i + 1) // 2)], 1)
+        call = V.tensor_copy(out, src) if E is V else S.activation(out, src, Copy)
+        call.then_inc(sem["yg%d" % i], 1)
+
+    def full(i, b):
+        parts = [(T.XC[:], T.XS[:]), (T.RC[:], T.RS[:])] if i == 0 else \
+            [(col(c, i - 1, 512), col(p, i - 1, 512)) for c, p in ((T.FXC, T.FXS), (T.FRC, T.FRS))]
+        for f in range(2 * i - 2, 2 * i) if i else ():
+            PE.wait_ge(sem["wr%d" % f], 16)
+        for part, (c, p) in enumerate(parts):
+            mm = PE.matmul_mx(bank(b, 512 if i else 256), Q[0], Q[1], c, p, part == 0, part == 1)
+        mm.then_inc(sem["pm%d" % i], 1)
+
+    def keep(i, b):
+        S.wait_ge(sem["pm%d" % i], 1)
+        out = T.pf[:, 512 * i - 256:512 * i + 256] if i else T.pf[:, 0:256]
+        S.activation(out, bank(b, 512 if i else 256), Copy).then_inc(sem["pc%d" % i], 1)
+
+    def product(j, b):
+        PE.wait_ge(sem["d%d" % j], 16)
+        for part in range(2):
+            mm = PE.matmul_mx(bank(b, 128), Q[0], Q[1], col(T.LC, 2 * j + part, 128), col(T.LS, 2 * j + part, 128), part == 0, part == 1)
+        mm.then_inc(sem["ym%d" % j], 1)
+
+    def out_s(j, b):
+        S.wait_ge(sem["ym%d" % j], 1)
+        S.activation(col(T.ysb, chosen[j], 128), bank(b, 128), Copy).then_inc(sem["yc%d" % j], 1)
+
+    def store(E, s, n, done):
+        E.dma_start(T.y[:, 128 * s:128 * (s + n)], T.ysb[:, 128 * s:128 * (s + n)]).then_inc(done, 16)
+
+    PE.wait_ge(sem.qq, 1)
+    score(0, 0)
+    score(1, 1)
+    PE.wait_ge(sem.qr, 1)
+    full(0, 2)
+    PE.wait_ge(sem.qm, 16)
+    for h in range(2):
+        PE.wait_ge(sem["sn%d" % h], 1)
+        score(2 + h, h)
+    PE.wait_ge(sem.mt, 3)
+    turn(0)
+    spread(0)
+    spread(1)
+    PE.wait_ge(sem.ofx0, made[0])
+    spread(2)
+    PE.wait_ge(sem.gt, N)
+    PE.wait_ge(sem.ofx1, made[1])
+    PE.transpose(T.psT[:, 256:384], T.tq[:], T.idn[:]).then_inc(sem.tc, 1)
+    PE.wait_ge(sem.pc0, 1)
+    for u in range(4, 12):
+        if u % 2 == 0:
+            PE.wait_ge(sem["wx%d" % (u // 2 - 2)], 16)
+        if u >= 7:
+            PE.wait_ge(sem["sn%d" % (u - 3)], 1)
+        score(u, (u - 4) % 3)
+        if u == 8:
+            full(1, 3)
+    PE.wait_ge(sem.oc, 1)
+    turn(1)
+    full(2, 0)
+    product(0, 1)
+    PE.wait_ge(sem.ofx2, made[2])
+    spread(3)
+    product(1, 2)
+    PE.wait_ge(sem.pc1, 1)
+    product(2, 3)
+
+    V.wait_ge(sem.mk, 2)
+    for u in range(4):
+        groups(u, u % 2)
+    V.wait_ge(sem.mt, 3)
+    V.wait_ge(sem.mu, 2)
+    V.wait_ge(sem.sp, 4)
+    cells(V, T, 0, T.uc[:, 0:1])
+    V.wait_ge(sem.cel0, 3)
+    widen(0, T.pm, T.cc[:, 0:1])
+    lists(0)
+    for j in range(3):
+        gather_v(j, 0)
+        if j < 2:
+            V.wait_ge(sem["n%d" % j], count(near))
+            widen(j + 1, T.pq, T.nin[:, 4 * j:4 * j + 1])
+        gather_v(j, 1)
+        if j < 2:
+            lists(j + 1)
+        else:
+            V.wait_ge(sem.tc, 1)
+            V.tensor_copy(T.offc[:], T.psT[:, 256:260]).then_inc(sem.oc, 1)
+        pack(j)
+    for u in range(4, 12):
+        groups(u, (u - 4) % 3)
+    V.wait_ge(sem.an, 24)
+    for lo, first in ((0, T.cc[0:64, 0:1]), (64, T.nin[64:128, 8:9])):
+        V.tensor_scalar(T.cc[lo:lo + 64, 8:9], first, T.nin[lo:lo + 64, 12:13], T.nin[lo:lo + 64, 16:17], Op.add, Op.add).then_inc(sem.tn, 1)
+    cells(V, T, 1, T.uc[:, 1:2])
+    V.wait_ge(sem.cel1, 3)
+    V.wait_ge(sem.tn, 2)
+    V.tensor_scalar(col(T.bc, 3, 128), T.pa[:], T.cc[:, 4:5], T.cc[:, 8:9], Op.add, Op.add).then_inc(sem.bcx3, 1)
+    V.wait_ge(sem.ctx3, 1)
+    V.tensor_scalar(T.offl[:, 8:40], T.psT[:, 512 + 3:640:4], 16.0, None, Op.mult).then_inc(sem.ofx3, 1)
+    V.tensor_copy(T.chf[:], T.psT[:, 512:640]).then_inc(sem.chv, 1)
+    V.wait_ge(sem.ofx3, 1)
+    pick(V, 1)
+    pick(V, 3)
+    V.wait_ge(sem.chv, 1)
+    V.wait_ge(sem.oc, 1)
+    V.tensor_copy(T.chg[:], T.chf[:, 0:128].indirect(T.offc[:, 0:4])).then_inc(sem.chv, 1)
+
+    S.wait_ge(sem.gp, 1)
+    S.activation(T.pa[:], T.p16[:], Copy, scale=1.0 / 16).then_inc(sem.sp, 1)
+    S.activation(T.pq[:], T.p16[:], Copy, scale=1.0 / 64).then_inc(sem.sp, 1)
+    S.activation(T.pm[0:64, :], T.p16[0:64, :], Copy, scale=1.0 / 16).then_inc(sem.sp, 1)
+    S.activation(T.pm[64:128, :], T.p16[64:128, :], Copy, scale=1.0 / 64).then_inc(sem.sp, 1)
+    for b in range(4):
+        S.wait_ge(sem["rs%d" % b], 1)
+    keep(0, 2)
+    gather_s(0)
+    gather_s(1)
+    gather_s(2)
+    pick(S, 0)
+    keep(1, 3)
+    keep(2, 0)
+    out_s(0, 1)
+    S.wait_ge(sem.ofx3, 1)
+    pick(S, 2)
+    out_s(1, 2)
+    pick(S, 4)
+    out_s(2, 3)
+    S.wait_ge(sem.yc1, 1)
+    S.wait_ge(sem.yc2, 1)
+    store(S, min(chosen[1:]), 2, sem.yd)
+    S.wait_ge(sem.yd, 16)
+
+    for ready, s in ((("yg0", "yc0"), min(me, chosen[0])), (("yg1", "yg2"), min(whole[:2])), (("yg3", "yg4"), min(whole[2:]))):
+        for name in ready:
+            SY.wait_ge(sem[name], 1)
+        store(SY, s, 2, sem.ye)
+    SY.wait_ge(sem.chv, 2)
+    SY.dma_start(T.ch[:], T.chg[0:1, :]).then_inc(sem.ye, 16)
+    SY.wait_ge(sem.ye, 16 * 4)
+
+    tr, post, finish = writer(g, core, T, topo)
+    g.wait_ge(sem.mf, 1)
+    g.affine_select(T.idn[:], T.onf[:], [[-1, 128]], Op.is_equal, 0.0, 0, 1).then_inc(sem.gi, 1)
     g.iota(T.p16[:], [[0, 8], [1, 16]], 0, 0, allow_small_or_imprecise_dtypes=True).then_inc(sem.gp, 1)
-    g.iota(T.pcol[:], [[0, 8]], 0, 1, allow_small_or_imprecise_dtypes=True).then_inc(sem.gp, 1)
-    g.wait_ge(sem.mo, 1)
-    g.affine_select(T.eb[:], T.ob[:], [[-1, 528]], Op.is_equal, 0.0, 4, 4).then_inc(sem.ge, 1)
 
+    def pair(codes, plane, dst, land, mask, names):
+        post(tr(raw(codes), [(dst, raw(land[0]))], mask, sem[names[0]]))
+        post(tr(plane, [(dst, land[1])], mask, sem[names[1]]))
+
+    mate = cores[chosen[0]]
+    scorers = [plans[chosen[1 + i]]["out"][i] for i in range(2)]
     g.wait_ge(sem.qq, 1)
-    qsem = sem["q%d" % me]
-    for ranks in (P, B):
-        at = [(cores[r], plans[r]["slots"].index(me)) for r in ranks]
-        post(tr(qcol(T.QC, own).bitcast(u8), [(c, qcol(T.QC, j).bitcast(u8)) for c, j in at], far, qsem))
-        post(tr(qcol(T.QS, own), [(c, qcol(T.QS, j)) for c, j in at], far, qsem))
+    pair(Q[0], Q[1], scorers[0], (T.HQC[:], T.HQS[:]), far, ("hq", "hq"))
+    g.wait_ge(sem.qx, 1)
+    pair(T.XC[:], T.XS[:], plan["out"][0], (T.HXC[:], T.HXS[:]), near, ("hxc", "hxs"))
+    pair(Q[0], Q[1], mate, (col(T.QC, 1, 128), col(T.QS, 1, 128)), far, ("qm", "qm"))
+    pair(T.XC[:], T.XS[:], plan["out"][1], (T.HXC[:], T.HXS[:]), near, ("hxc", "hxs"))
+    pair(Q[0], Q[1], scorers[1], (T.HQC[:], T.HQS[:]), far, ("hq", "hq"))
+    g.wait_ge(sem.qr, 1)
+    for i, r in enumerate(plan["to"]):
+        pair(T.RC[:], T.RS[:], plans[r]["inb"], (col(T.HRC, i, 256), col(T.HRS, i, 256)), far, ("hrc%d" % i, "hrs%d" % i))
+    at = {me: (6, 8), chosen[0]: (70, 8), chosen[1]: (ENDS[0], 16), chosen[2]: (ENDS[1], 16)}
+    at.update({s: (32 * f + 3, 4) for f, s in enumerate(whole)})
+    for s, (first, step) in at.items():
+        g.iota(T.tq[:, s:128:8], [[0, 8], [step, 2]], first, 2 * step, allow_small_or_imprecise_dtypes=True).then_inc(sem.gt, 1)
+    g.wait_ge(sem.cel0, 3)
+    post(tr(T.cc[:, 0:1], [(mate, T.nin[:, 8:9])], far, sem.an))
+    for j, r in enumerate(chosen):
+        g.wait_ge(sem["qz%d" % j], 1)
+        pair(col(T.OC, j, 256), col(T.OS, j, 256), cores[r], (col(T.LC, j, 256), col(T.LS, j, 256)), far, ("d%d" % j,) * 2)
+    finish()
+
+
+def scorer_program(g, core, me, T, topo):
+    plans = [make_plan(r, T, topo) for r in range(N)]
+    plan = plans[me]
+    cores, sem = T.cores, T.sem
+    i = plan["out"].index(core)
+    Op = AluOpType
+    V, PE = g.vector, g.tensor
+    tr, post, finish = writer(g, core, T, topo)
+    askers = [plan["to"][i], plans[plan["to"][i]]["mate"]]
+    far = topo.mask(core, cores[askers[0]])
+    near = topo.mask(core, cores[me]) & ~far
+    arrive = count(near)
+
+    V.memset(T.onf[:], 1.0).then_inc(sem.mf, 1)
+    V.memset(T.msk[:], BIG).then_inc(sem.mk, 1)
+    V.memset(T.top[:], BIG).then_inc(sem.mt, 1)
+    for h in range(2):
+        V.memset(T.sc[:, 264 * h + 128:264 * h + 136], 0.0).then_inc(sem.mt, 1)
+    V.wait_ge(sem.mk, 1)
+    V.memset(T.msk[:, 0:128:16], -BIG).then_inc(sem.mk, 1)
+    V.wait_ge(sem.gi, 1)
+    V.tensor_reduce(T.uc[:, 0:1], T.idn[:, ENDS[i]:128:16], AxisListType.X, Op.add).then_inc(sem.mu, 1)
+    V.wait_ge(sem.mk, 2)
+    for h in range(2):
+        V.wait_ge(sem["sm%d" % h], 1)
+        V.tensor_tensor_scan(T.sc[:, 264 * h:264 * h + 128], T.msk[:], T.psP[:, 512 * h:512 * h + 128], -BIG, Op.min, Op.max).then_inc(sem["sn%d" % h], 1)
+    V.wait_ge(sem.mt, 3)
+    V.wait_ge(sem.mu, 1)
+    cells(V, T, 0, T.uc[:, 0:1])
+
+    PE.wait_ge(sem.hxc, arrive)
+    PE.wait_ge(sem.hxs, arrive)
+    PE.wait_ge(sem.hq, 2 * count(far))
+    for h in range(2):
+        PE.matmul_mx(T.psP[:, 512 * h:512 * h + 128], col(T.HXC, h, 128), col(T.HXS, h, 128), T.HQC[:], T.HQS[:], True, True).then_inc(sem["sm%d" % h], 1)
+    PE.wait_ge(sem.gi, 1)
+    PE.wait_ge(sem.mt, 3)
+    for h in range(2):
+        k = 264 * h + 15 - ENDS[i]
+        PE.wait_ge(sem["sn%d" % h], 1)
+        PE.transpose(col(T.psT, h, 128), T.sc[:, k:k + 128], T.idn[:]).then_inc(sem["tr0%d" % h], 1)
 
     g.wait_ge(sem.mf, 1)
     g.affine_select(T.idn[:], T.onf[:], [[-1, 128]], Op.is_equal, 0.0, 0, 1).then_inc(sem.gi, 1)
-
-    for part, (c, p, ready) in enumerate(((T.XC, T.XS, sem.qx), (T.RC, T.RS, sem.qr))):
-        g.wait_ge(ready, 1)
-        post(tr(c[:].bitcast(u8), [(h, xcol(T.HFC, part).bitcast(u8)) for h in relays], near, sem["hfc%d" % part]))
-        post(tr(p[:], [(h, xcol(T.HFS, part)) for h in relays], near, sem["hfs%d" % part]))
-    g.affine_select(T.m24[:], T.onf[:, 0:24], [[0, 3], [-1, 8]], Op.is_equal, 0.0, 0, 1).then_inc(sem.gm, 1)
-
-    def send_chosen(r):
-        j = sl[r]
-        g.wait_ge(sem["qz%d" % j], 1)
-        if r in plan["x_relay"]:
-            h = relays[plan["x_relay"][r]]
-            post(tr(xcol(T.OC, j).bitcast(u8), [(h, T.HXC[:].bitcast(u8))], near, sem.hxc))
-            post(tr(xcol(T.OS, j), [(h, T.HXS[:])], near, sem.hxs))
-        else:
-            k = plans[r]["slots"].index(me)
-            post(tr(xcol(T.OC, j).bitcast(u8), [(cores[r], xcol(T.LC, k).bitcast(u8))], far, sem["d%d" % me]))
-            post(tr(xcol(T.OS, j), [(cores[r], xcol(T.LS, k))], far, sem["d%d" % me]))
-
-    for r in chosen_ranks[:-1]:
-        send_chosen(r)
-    one = 1 << topo.engines(core, cores[M])[0]
-    g.wait_ge(sem.chs, 16)
-    post(tr(T.chd[:], [(cores[r], T.chland[me]) for r in chosen_ranks], one, sem.chi))
-    send_chosen(chosen_ranks[-1])
-    g.wait_ge(sem.sent, sent[0])
-
-    ybank = [T.psY[:, 0:128], T.psY[:, 512:640], T.psA[:, 512:640], T.psY[:, 1024:1152], T.psA[:, 0:128]]
-    for i, s in enumerate(plan["yorder"]):
-        j = sl[s]
-        PE.wait_ge(sem["d%d" % s], 16)
-        if i >= 3:
-            PE.wait_ge(sem["pc%d" % (i - 2)], 1)
-        for part in range(2):
-            a = 256 * j + 128 * part
-            mm = PE.matmul_mx(ybank[i], qcol(T.QC, own), qcol(T.QS, own), T.LC[:, a:a + 128], T.LS[:, a:a + 128], part == 0, part == 1)
-        mm.then_inc(sem["ym%d" % j], 1)
-        S.wait_ge(sem["ym%d" % j], 1)
-        S.activation(T.ysb[:, 128 * s:128 * s + 128], ybank[i], Copy).then_inc(sem["yc%d" % j], 1)
-        S.wait_ge(sem["yc%d" % j], 1)
-        S.dma_start(T.y[:, 128 * s:128 * s + 128], T.ysb[:, 128 * s:128 * s + 128]).then_inc(sem.yd, 16)
-    S.wait_ge(sem.yd, 16 * len(plan["yorder"]))
-
-    SY.wait_ge(sem.chr, 1)
-    SY.dma_start(T.chd[:], T.chrow[0:1, :]).then_inc(sem.chs, 16)
-
-    def store_sy(i):
-        s = whole[i]
-        SY.wait_ge(sem["yg%d" % i], 1)
-        SY.dma_start(T.y[:, 128 * s:128 * s + 128], T.ysb[:, 128 * s:128 * s + 128]).then_inc(sem.ye, 16)
-
-    store_sy(0)
-    SY.wait_ge(sem.chi, len(chosen_ranks))
-    SY.wait_ge(sem.mch, 3)
-    for s in chosen_ranks:
-        a = 8 * plans[s]["slots"].index(me)
-        SY.dma_start(T.chc[s:s + 1, 0:8], T.chland[s:s + 1, a:a + 8, 0]).then_inc(sem.chg, 16)
-    store_sy(1)
-    store_sy(2)
-    V.tensor_scalar(T.chk[0:8, :], T.offl[0:8, 0:24], T.pcol[0:8, 0:1], 1.0 / 16.0, Op.subtract, Op.mult).then_inc(sem.chv, 1)
-    V.wait_ge(sem.chv, 1)
-    V.wait_ge(sem.gm, 1)
-    V.tensor_tensor(T.chm[0:8, :], T.chk[0:8, :], T.m24[0:8, :], Op.mult).then_inc(sem.chv, 1)
-    V.wait_ge(sem.chv, 2)
-    for i, s in enumerate(whole):
-        V.tensor_reduce(T.chl[0:8, s:s + 1], T.chm[0:8, 8 * i:8 * i + 8], AxisListType.X, Op.add).then_inc(sem.chl1, 1)
-    V.wait_ge(sem.chg, 16 * len(chosen_ranks))
-    V.transpose(T.cht[0:32, :], T.chc[0:32, :]).then_inc(sem.chv, 1)
-    V.wait_ge(sem.chv, 3)
-    V.wait_ge(sem.chl1, len(whole))
-    V.tensor_tensor(T.chf[0:8, :], T.cht[0:8, 0:8], T.chl[0:8, :], Op.add).then_inc(sem.chf1, 1)
-    SY.wait_ge(sem.chf1, 1)
-    SY.dma_start(T.ch[:], T.chf[0:8, :]).then_inc(sem.cho, 16)
-    SY.wait_ge(sem.cho, 16)
-    SY.wait_ge(sem.ye, 16 * len(whole))
+    g.wait_ge(sem.hxc, arrive)
+    for k, r in enumerate(askers):
+        f = 2 * i + k
+        post(tr(raw(T.HXC[:]), [(cores[r], raw(col(T.FXC, f, 256)))], far, sem["wx%d" % f]))
+        g.wait_ge(sem.hxs, arrive)
+        post(tr(T.HXS[:], [(cores[r], col(T.FXS, f, 256))], far, sem["wx%d" % f]))
+    g.wait_ge(sem.cel0, 3)
+    post(tr(T.cc[:, 0:1], [(cores[me], T.nin[:, 4 * i:4 * i + 1])], near, sem["n%d" % i]),
+         tr(T.cc[:, 0:1], [(cores[plan["chosen"][1 + i]], T.nin[:, 12 + 4 * i:13 + 4 * i])], far, sem.an))
+    finish()
 
 
 def relay_program(g, core, me, T, topo):
     plan = make_plan(me, T, topo)
-    if core not in plan["relays"]:
-        return
     cores, sem = T.cores, T.sem
-    which = plan["relays"].index(core)
-    home = cores[me]
-    near = topo.mask(home, core) & ~topo.mask(home, cores[plan["P"][0]])
-    arrive = count(near)
-    u8 = dt.uint8
-    sent = [0]
-
-    def send(wait, dst, out, src, rsem):
-        g.wait_ge(wait, arrive)
-        rid, pid = topo.addr(dst, core)
-        mask = topo.mask(core, dst)
-        sent[0] += count(mask)
-        g.remote_dma_fused([RemoteDMATransfer(dst_ids=[DstId(rid=rid, pnc=pid)], dma_engine_mask=mask, remote_sem=rsem,
-                                              srcs=[src], dsts=[out])], local_sem=sem.sent)
-
-    for r, i in plan["w_relay"].items():
-        if i == which:
-            f = make_plan(r, T, topo)["W"].index(me)
-            for part in range(2):
-                a, k = 256 * part, 512 * f + 256 * part
-                there = sem["w%d%d" % (f, part)]
-                send(sem["hfc%d" % part], cores[r], T.FC[:, k:k + 256].bitcast(u8), T.HFC[:, a:a + 256].bitcast(u8), there)
-                send(sem["hfs%d" % part], cores[r], T.FS[:, k:k + 256], T.HFS[:, a:a + 256], there)
-    for r, i in plan["x_relay"].items():
-        if i == which:
-            k = 256 * make_plan(r, T, topo)["slots"].index(me)
-            there = sem["d%d" % me]
-            send(sem.hxc, cores[r], T.LC[:, k:k + 256].bitcast(u8), T.HXC[:].bitcast(u8), there)
-            send(sem.hxs, cores[r], T.LS[:, k:k + 256], T.HXS[:], there)
-    g.wait_ge(sem.sent, sent[0])
+    tr, post, finish = writer(g, core, T, topo)
+    home, mate = cores[me], cores[plan["mate"]]
+    far = topo.mask(core, mate)
+    near = topo.mask(core, home) & ~far
+    for i in range(2):
+        for wait, src, land, see in (("hrc", T.HRC, T.FRC, raw), ("hrs", T.HRS, T.FRS, lambda ap: ap)):
+            g.wait_ge(sem[wait + str(i)], count(far))
+            post(tr(see(col(src, i, 256)), [(home, see(col(land, 2 * i, 256)))], near, sem["wr%d" % (2 * i)]),
+                 tr(see(col(src, i, 256)), [(mate, see(col(land, 2 * i + 1, 256)))], far, sem["wr%d" % (2 * i + 1)]))
+    finish()

@@ -11,15 +11,16 @@ SCRATCH = {
     "xb": ("sbuf", [128, 1024], BF16),
     "rb": ("sbuf", [128, 1024], BF16),
     "eb": ("sbuf", [128, 528], BF16),
-    "onf": ("sbuf", [128, 128], F32),
+    "onf": ("sbuf", [128, 144], F32),
     "idn": ("sbuf", [128, 128], F32),
     "p16": ("sbuf", [128, 128], F32),
     "pa": ("sbuf", [128, 128], F32),
     "pq": ("sbuf", [128, 128], F32),
-    "pm": ("sbuf", [128, 128], F32),
+    "inc": ("sbuf", [128, 144], F32),
+    "run": ("sbuf", [128, 144], F32),
     "tq": ("sbuf", [128, 128], F32),
     "uc": ("sbuf", [128, 8], F32),
-    "msk": ("sbuf", [128, 128], F32),
+    "msk": ("sbuf", [128, 256], F32),
     "top": ("sbuf", [128, 256], F32),
     "QC": ("sbuf", [128, 256], CODES),
     "QS": ("sbuf", [128, 256], PLANE),
@@ -29,13 +30,14 @@ SCRATCH = {
     "RS": ("sbuf", [128, 256], PLANE),
     "EC": ("sbuf", [128, 512], CODES),
     "ES": ("sbuf", [128, 512], PLANE),
-    "sc": ("sbuf", [128, 528], F32),
-    "sw": ("sbuf", [128, 1024], F32),
+    "sc": ("sbuf", [128, 1088], F32),
     "rm": ("sbuf", [128, 512], F32),
     "ltb": ("sbuf", [128, 32], F32),
-    "cc": ("sbuf", [128, 12], F32),
-    "bc": ("sbuf", [128, 512], F32),
-    "nin": ("sbuf", [128, 20], F32),
+    "cnt": ("sbuf", [128, 32], BF16),
+    "cc": ("sbuf", [128, 8], F32),
+    "bc": ("sbuf", [128, 768], F32),
+    "nin": ("sbuf", [128, 4], F32),
+    "nib": ("sbuf", [128, 64], BF16),
     "off": ("sbuf", [128, 96], U16),
     "offl": ("sbuf", [128, 40], U16),
     "offc": ("sbuf", [128, 4], U16),
@@ -48,10 +50,14 @@ SCRATCH = {
     "FXS": ("sbuf", [128, 1024], PLANE),
     "FRC": ("sbuf", [128, 1024], CODES),
     "FRS": ("sbuf", [128, 1024], PLANE),
-    "HQC": ("sbuf", [128, 128], CODES),
-    "HQS": ("sbuf", [128, 128], PLANE),
+    "HQC": ("sbuf", [128, 384], CODES),
+    "HQS": ("sbuf", [128, 384], PLANE),
     "HXC": ("sbuf", [128, 256], CODES),
     "HXS": ("sbuf", [128, 256], PLANE),
+    "HYC": ("sbuf", [128, 256], CODES),
+    "HYS": ("sbuf", [128, 256], PLANE),
+    "HZC": ("sbuf", [128, 256], CODES),
+    "HZS": ("sbuf", [128, 256], PLANE),
     "HRC": ("sbuf", [128, 512], CODES),
     "HRS": ("sbuf", [128, 512], PLANE),
     "pf": ("sbuf", [128, 1280], F32),
@@ -63,20 +69,23 @@ SCRATCH = {
     "psP": ("psum", [128, 2048], F32),
 }
 SEMAPHORES = (
-    ["lq", "lx", "mf", "me", "mk", "mt", "mu", "qq", "qx", "qr", "qe", "gi", "gp", "gt", "sp", "tc", "oc"]
+    ["lq", "lx", "mf", "me", "mk", "mt", "mu", "qq", "qx", "qr", "qe", "gi", "gp", "gt", "sp", "si", "tc", "oc"]
     + ["dm%d" % b for b in range(4)] + ["rs%d" % b for b in range(4)]
-    + [n + str(u) for n in ("sm", "sn") for u in range(12)]
+    + [n + str(u) for n in ("sm", "sn") for u in range(4)]
     + ["tr%d%d" % (b, h) for b in range(2) for h in range(2)]
-    + [n + str(b) for n in ("bcx", "ctx", "ofx") for b in range(4)]
-    + [n + str(b) for n in ("cel", "n", "hrc", "hrs") for b in range(2)]
-    + [n + str(j) for n in ("gv", "gs", "qz", "ym", "yc", "d", "pm", "pc") for j in range(3)]
+    + [n + str(b) for n in ("bcx", "ctx", "ofx") for b in range(5)]
+    + [n + str(b) for n in ("cel", "n", "aw", "hrc", "hrs") for b in range(2)]
+    + [n + str(j) for n in ("ym", "yc", "d", "pm", "pc", "qz") for j in range(3)]
+    + [n + str(j) for n in ("gv", "gs") for j in range(6)]
     + [n + str(j) for n in ("wx", "wr") for j in range(4)]
     + ["yg%d" % j for j in range(5)]
-    + ["qm", "an", "tn", "chv", "yd", "ye", "sent", "hq", "hxc", "hxs"]
+    + ["qm", "an", "tn", "chv", "yd", "ye", "sent", "hq", "ho", "hm", "hxc", "hxs", "hyc", "hys", "hzc", "hzs"]
 )
 ENDS = (13, 12)
-SHARE = (22, 20, 26)
-EARLY = (8, 8, 8)
+BOTH = (7, 3)
+OWN = 6
+PAD = 272
+SHARE = (32, 26, 26)
 
 
 def make_plan(me, T, topo):
@@ -91,7 +100,7 @@ def make_plan(me, T, topo):
     mate, before, after, across = mate_of(me), ring[(k - 1) % n], ring[(k + 1) % n], ring[(k + 2) % n]
     free = [c for c in topo.cores_of(core) if c != core and topo.may_write(c, cores[mate])]
     return {
-        "mate": mate, "to": [after, before], "chosen": [mate, across, mate_of(across)],
+        "mate": mate, "to": [after, before], "chosen": [mate_of(across), across, mate],
         "whole": [before, mate_of(before), after, mate_of(after)],
         "inb": [c for c in free if topo.die(c) == topo.die(core)][0],
         "out": [c for c in free if topo.die(c) != topo.die(core)][:2],
@@ -130,16 +139,20 @@ def raw(ap):
     return ap.bitcast(dt.uint8)
 
 
-def cells(V, T, bt, unit):
+def same(ap):
+    return ap
+
+
+def cells(V, T, bt, unit, lt, out, terms, n):
     Op, sem = AluOpType, T.sem
     V.wait_ge(sem["tr%d0" % bt], 1)
     V.wait_ge(sem["tr%d1" % bt], 1)
-    rm, done, lt = 256 * bt, sem["cel%d" % bt], col(T.ltb, bt, 16)
-    V.tensor_tensor_scan(T.rm[:, rm:rm + 256], T.top[:], T.psT[:, 0:256], -BIG, Op.min, Op.max).then_inc(done, 1)
+    rm, done = 256 * bt, sem["cel%d" % bt]
+    V.tensor_tensor_scan(T.rm[:, rm:rm + 256], T.top[:], T.psT[:, 512 * bt:512 * bt + 256], -BIG, Op.min, Op.max).then_inc(done, 1)
     V.wait_ge(done, 1)
     V.tensor_scalar(lt, T.rm[:, rm + 15:rm + 256:16], T.rm[:, rm + 255:rm + 256], unit, Op.is_lt, Op.mult).then_inc(done, 1)
     V.wait_ge(done, 2)
-    V.tensor_reduce(T.cc[:, 4 * bt:4 * bt + 1], lt, AxisListType.X, Op.add).then_inc(done, 1)
+    V.tensor_tensor_scan(out, T.onf[:, 0:n], terms, 0.0, Op.mult, Op.add).then_inc(done, 1)
 
 
 def rank_program(g, core, T, topo):
@@ -163,16 +176,20 @@ def rank_program(g, core, T, topo):
     Q = (col(T.QC, 0, 128), col(T.QS, 0, 128))
     far = topo.mask(core, cores[chosen[0]])
     near = topo.mask(core, plan["out"][0]) & ~far
+    E8 = count(far)
 
     def bank(b, n):
         return T.psP[:, 512 * b:512 * b + n]
 
+    def number(k, lo=0, hi=128):
+        return T.nib[lo:hi, 8 * k:8 * k + 1]
+
     SY.dma_start(T.qwb[:], T.qw[:]).then_inc(sem.lq, 16)
-    S.dma_start(T.xb[:], T.x[:]).then_inc(sem.lx, 16)
+    SY.dma_start(T.xb[:], T.x[:]).then_inc(sem.lx, 16)
 
     V.memset(T.onf[:], 1.0).then_inc(sem.mf, 1)
     V.memset(T.eb[:], 0.0).then_inc(sem.me, 1)
-    V.memset(T.msk[:], BIG).then_inc(sem.mk, 1)
+    V.memset(T.msk[:, 0:128], BIG).then_inc(sem.mk, 1)
     V.wait_ge(sem.me, 1)
     V.wait_ge(sem.gi, 1)
     V.tensor_copy(T.eb[:, 4:516:4], T.idn[:]).then_inc(sem.me, 1)
@@ -194,9 +211,8 @@ def rank_program(g, core, T, topo):
         V.wait_ge(sem["rs%d" % b], 1)
     V.quantize_mx(T.RC[:], T.RS[:], T.rb[:]).then_inc(sem.qr, 1)
     for h in range(2):
-        V.memset(T.sc[:, 264 * h + 256:264 * h + 264], 0.0).then_inc(sem.mt, 1)
-    V.tensor_reduce(T.uc[:, 0:1], T.idn[:, 6:128:8], AxisListType.X, Op.add).then_inc(sem.mu, 1)
-    V.tensor_reduce(T.uc[:, 1:2], T.idn[:, 3:128:4], AxisListType.X, Op.add).then_inc(sem.mu, 1)
+        V.memset(T.sc[:, PAD * h + 256:PAD * h + PAD], 0.0).then_inc(sem.mt, 1)
+    V.tensor_reduce(T.uc[:, 0:1], T.idn[:, OWN:128:8], AxisListType.X, Op.add).then_inc(sem.mu, 1)
 
     PE.wait_ge(sem.qx, 1)
     PE.wait_ge(sem.qe, 4)
@@ -206,109 +222,145 @@ def rank_program(g, core, T, topo):
         k = 512 * (b % 2)
         PE.matmul_mx(T.psD[:, k:k + 256], col(T.EC, b, 128), col(T.ES, b, 128), T.XC[:], T.XS[:], True, True).then_inc(sem["dm%d" % b], 1)
 
-    def score(u, b):
+    def score(u):
         h = u % 2
-        if u < 4:
-            args = (col(T.XC, h, 128), col(T.XS, h, 128), col(T.QC, u // 2, 128), col(T.QS, u // 2, 128))
-        else:
-            args = (col(T.FXC, u - 4, 128), col(T.FXS, u - 4, 128)) + Q
-        PE.matmul_mx(bank(b, 128), *args, True, True).then_inc(sem["sm%d" % u], 1)
+        PE.matmul_mx(bank(h, 128), col(T.XC, h, 128), col(T.XS, h, 128), col(T.QC, u // 2, 128), col(T.QS, u // 2, 128), True, True).then_inc(sem["sm%d" % u], 1)
 
-    def groups(u, b):
+    def groups(u):
         h = u % 2
-        k = 264 * h + 128 * (u // 2)
-        out = T.sc[:, k:k + 128] if u < 4 else col(T.sw, 4 * h + u // 2 - 2, 128)
+        k = PAD * h + 128 * (u // 2)
         V.wait_ge(sem["sm%d" % u], 1)
-        V.tensor_tensor_scan(out, T.msk[:], bank(b, 128), -BIG, Op.min, Op.max).then_inc(sem["sn%d" % u], 1)
+        V.tensor_tensor_scan(T.sc[:, k:k + 128], T.msk[:, 0:128], bank(h, 128), -BIG, Op.min, Op.max).then_inc(sem["sn%d" % u], 1)
 
-    def turn(bt):
-        for h in range(2):
-            for u in (range(h, 4, 2), range(4 + h, 12, 2))[bt]:
-                PE.wait_ge(sem["sn%d" % u], 1)
-            src = T.sw[:, 512 * h + 3:512 * h + 512:4] if bt else T.sc[:, 264 * h + 3:264 * h + 259:2]
-            PE.transpose(col(T.psT, h, 128), src, T.idn[:]).then_inc(sem["tr%d%d" % (bt, h)], 1)
-
-    spot = [T.psT[:, 512:640], T.psT[:, 0:128], T.psT[:, 512:640], T.psT[:, 512:640]]
+    def spot(i):
+        return 512 * ((i + 1) % 2)
 
     def spread(i):
-        PE.wait_ge(sem["bcx%d" % i], 1)
-        PE.transpose(spot[i], col(T.bc, i, 128), T.idn[:]).then_inc(sem["ctx%d" % i], 1)
+        PE.wait_ge(*((sem["bcx%d" % i], 1 + i // 3) if i else (sem.cel0, 3)))
+        PE.transpose(T.psT[:, spot(i):spot(i) + 128], col(T.bc, i, 128) if i else T.run[:, 16:144], T.idn[:]).then_inc(sem["ctx%d" % i], 1)
 
-    def widen(i, table, number):
-        V.tensor_scalar(col(T.bc, i, 128), table[:], number, None, Op.add).then_inc(sem["bcx%d" % i], 1)
+    def widen(j):
+        V.wait_ge(sem["n%d" % j], count(near))
+        V.tensor_scalar(col(T.bc, j + 1, 128), T.pq[:], number(j), None, Op.add).then_inc(sem["bcx%d" % (j + 1)], 1)
 
     def lists(j):
         V.wait_ge(sem["ctx%d" % j], 1)
-        src = (T.psT[:, 512 + 70:640:8], T.psT[:, ENDS[0]:128:16], T.psT[:, 512 + ENDS[1]:640:16])[j]
+        first, step = ((64 + OWN, 8), (ENDS[0], 16), (ENDS[1], 16))[j]
+        src = T.psT[:, spot(j) + first:spot(j) + 128:step]
         for e in range(4):
             V.tensor_scalar(T.off[:, 32 * j + e:32 * j + 32:4], src, 64.0, 16.0 * e, Op.mult, Op.add).then_inc(sem["ofx%d" % j], 1)
         if j == 0:
-            V.tensor_scalar(T.offl[:, 0:8], T.psT[:, 512 + 6:576:8], 16.0, None, Op.mult).then_inc(sem.ofx0, 1)
+            V.tensor_scalar(T.offl[:, 0:8], T.psT[:, spot(0) + OWN:spot(0) + 64:8], 16.0, None, Op.mult).then_inc(sem.ofx0, 1)
 
     made = (5, 4, 4)
+    calls = {}
 
-    def gather_s(j):
-        k, a = SHARE[j], 1024 * j
-        S.wait_ge(sem["ofx%d" % j], made[j])
-        S.activation(T.hb[:, a + 16 * k:a + 512], T.xb[:, 0:1024].indirect(T.off[:, 32 * j + k:32 * j + 32]), Copy).then_inc(sem["gs%d" % j], 1)
-        S.activation(T.hb[:, a + 512:a + 1024], T.rb[:, 0:1024].indirect(col(T.off, j, 32)), Copy).then_inc(sem["gs%d" % j], 1)
+    def move(E, out, src):
+        return V.tensor_copy(out, src) if E is V else S.activation(out, src, Copy)
 
-    def gather_v(j, part):
-        lo, hi = (0, EARLY[j], SHARE[j])[part:part + 2]
-        V.wait_ge(sem["ofx%d" % j], made[j])
-        V.tensor_copy(T.hb[:, 1024 * j + 16 * lo:1024 * j + 16 * hi], T.xb[:, 0:1024].indirect(T.off[:, 32 * j + lo:32 * j + hi])).then_inc(sem["gv%d" % j], 1)
+    def gather(E, j, part, lo, hi):
+        if lo == hi:
+            return
+        a, name = 1024 * j + 512 * part, ("gv%d" if E is V else "gs%d") % (2 * j + part)
+        E.wait_ge(sem["ofx%d" % j], made[j])
+        move(E, T.hb[:, a + 16 * lo:a + 16 * hi], (T.xb, T.rb)[part][:, 0:1024].indirect(T.off[:, 32 * j + lo:32 * j + hi])).then_inc(sem[name], 1)
+        calls[name] = calls.get(name, 0) + 1
 
     def pack(j):
-        V.wait_ge(sem["gv%d" % j], 2)
-        V.wait_ge(sem["gs%d" % j], 2)
+        for name in [n % (2 * j + part) for part in range(2) for n in ("gv%d", "gs%d")]:
+            if name in calls:
+                V.wait_ge(sem[name], calls[name])
         V.quantize_mx(col(T.OC, j, 256), col(T.OS, j, 256), col(T.hb, j, 1024)).then_inc(sem["qz%d" % j], 1)
 
     every = [me] + whole
 
     def pick(E, i):
-        out, src = col(T.ysb, every[i], 128), col(T.pf, i, 256).indirect(col(T.offl, i, 8))
         E.wait_ge(sem["pc%d" % ((i + 1) // 2)], 1)
-        call = V.tensor_copy(out, src) if E is V else S.activation(out, src, Copy)
-        call.then_inc(sem["yg%d" % i], 1)
+        if i:
+            E.wait_ge(sem["ofx%d" % (2 + (i + 1) // 2)], 1)
+        move(E, col(T.ysb, every[i], 128), col(T.pf, i, 256).indirect(col(T.offl, i, 8))).then_inc(sem["yg%d" % i], 1)
 
     def full(i, b):
         parts = [(T.XC[:], T.XS[:]), (T.RC[:], T.RS[:])] if i == 0 else \
             [(col(c, i - 1, 512), col(p, i - 1, 512)) for c, p in ((T.FXC, T.FXS), (T.FRC, T.FRS))]
-        for f in range(2 * i - 2, 2 * i) if i else ():
-            PE.wait_ge(sem["wr%d" % f], 16)
         for part, (c, p) in enumerate(parts):
+            for f in range(2 * i - 2, 2 * i) if i else ():
+                PE.wait_ge(sem[("wx%d", "wr%d")[part] % f], 2 * E8)
             mm = PE.matmul_mx(bank(b, 512 if i else 256), Q[0], Q[1], c, p, part == 0, part == 1)
         mm.then_inc(sem["pm%d" % i], 1)
 
-    def keep(i, b):
-        S.wait_ge(sem["pm%d" % i], 1)
-        out = T.pf[:, 512 * i - 256:512 * i + 256] if i else T.pf[:, 0:256]
-        S.activation(out, bank(b, 512 if i else 256), Copy).then_inc(sem["pc%d" % i], 1)
+    def keep(E, i, b):
+        E.wait_ge(sem["pm%d" % i], 1)
+        move(E, T.pf[:, 512 * i - 256:512 * i + 256] if i else T.pf[:, 0:256], bank(b, 512 if i else 256)).then_inc(sem["pc%d" % i], 1)
 
     def product(j, b):
-        PE.wait_ge(sem["d%d" % j], 16)
+        PE.wait_ge(sem["d%d" % j], 2 * E8)
         for part in range(2):
             mm = PE.matmul_mx(bank(b, 128), Q[0], Q[1], col(T.LC, 2 * j + part, 128), col(T.LS, 2 * j + part, 128), part == 0, part == 1)
         mm.then_inc(sem["ym%d" % j], 1)
 
-    def out_s(j, b):
-        S.wait_ge(sem["ym%d" % j], 1)
-        S.activation(col(T.ysb, chosen[j], 128), bank(b, 128), Copy).then_inc(sem["yc%d" % j], 1)
+    def bring(E, j, b):
+        E.wait_ge(sem["ym%d" % j], 1)
+        move(E, col(T.ysb, chosen[j], 128), bank(b, 128)).then_inc(sem["yc%d" % j], 1)
 
-    def store(E, s, n, done):
-        E.dma_start(T.y[:, 128 * s:128 * (s + n)], T.ysb[:, 128 * s:128 * (s + n)]).then_inc(done, 16)
+    def store(E, ready, s, done):
+        for name in ready:
+            E.wait_ge(sem[name], 1)
+        E.dma_start(T.y[:, 128 * s:128 * (s + len(ready))], T.ysb[:, 128 * s:128 * (s + len(ready))]).then_inc(done, 16)
+
+    def arrived(i, base):
+        V.wait_ge(sem["aw%d" % i], 2 * E8)
+        for h in range(2):
+            lo = 64 * h
+            V.tensor_scalar(T.bc[lo:lo + 64, 384 + 128 * i:512 + 128 * i], base[lo:lo + 64, 0:128], number(4 + 2 * i + h, lo, lo + 64),
+                            None, Op.add).then_inc(sem["bcx%d" % (3 + i)], 1)
+
+    def items(i):
+        V.wait_ge(sem["ctx%d" % (3 + i)], 1)
+        k = spot(3 + i)
+        V.tensor_scalar(T.offl[:, 8 + 16 * i:24 + 16 * i], T.psT[:, k + BOTH[i]:k + 128:8], 16.0, None, Op.mult).then_inc(sem["ofx%d" % (3 + i)], 1)
+
+    S.wait_ge(sem.mf, 1)
+    for lo, unit in ((0, 1.0 / 16), (64, 1.0 / 64)):
+        S.activation(T.inc[lo:lo + 64, 16:144], T.onf[lo:lo + 64, 0:128], Copy, scale=unit).then_inc(sem.si, 1)
+    S.wait_ge(sem.si, 2)
+    for lo, unit in ((0, 1.0 / 16), (64, 1.0 / 64)):
+        S.activation(T.inc[lo:lo + 64, 32:144:16], T.onf[lo:lo + 64, 0:7], Copy, scale=-15 * unit).then_inc(sem.sp, 1)
+    S.activation(T.inc[:, 16:17], T.onf[:, 0:1], Copy, scale=0.0).then_inc(sem.sp, 1)
+    S.wait_ge(sem.gp, 1)
+    S.activation(T.pa[:], T.p16[:], Copy, scale=1.0 / 16).then_inc(sem.sp, 1)
+    S.activation(T.pq[:], T.p16[:], Copy, scale=1.0 / 64).then_inc(sem.sp, 1)
+    for b in range(4):
+        S.wait_ge(sem["rs%d" % b], 1)
+    keep(S, 0, 2)
+    for j in range(3):
+        gather(S, j, 1, 0, 32)
+        gather(S, j, 0, SHARE[j], 32)
+        if j == 0:
+            pick(S, 0)
+    keep(S, 1, 0)
+    keep(S, 2, 1)
+    pick(S, 2)
+    bring(S, 1, 3)
+    pick(S, 4)
+    bring(S, 2, 0)
+    store(S, ("yc2",), chosen[2], sem.yd)
+    S.wait_ge(sem.yd, 16)
 
     PE.wait_ge(sem.qq, 1)
-    score(0, 0)
-    score(1, 1)
+    score(0)
+    score(1)
     PE.wait_ge(sem.qr, 1)
     full(0, 2)
-    PE.wait_ge(sem.qm, 16)
+    PE.wait_ge(sem.qm, 2 * E8)
     for h in range(2):
         PE.wait_ge(sem["sn%d" % h], 1)
-        score(2 + h, h)
+        score(2 + h)
     PE.wait_ge(sem.mt, 3)
-    turn(0)
+    for h in range(2):
+        PE.wait_ge(sem["sn%d" % (2 + h)], 1)
+        k = PAD * h + 15 - 2 * OWN
+        PE.transpose(col(T.psT, h, 128), T.sc[:, k:k + 256:2], T.idn[:]).then_inc(sem["tr0%d" % h], 1)
     spread(0)
     spread(1)
     PE.wait_ge(sem.ofx0, made[0])
@@ -316,130 +368,107 @@ def rank_program(g, core, T, topo):
     PE.wait_ge(sem.gt, N)
     PE.wait_ge(sem.ofx1, made[1])
     PE.transpose(T.psT[:, 256:384], T.tq[:], T.idn[:]).then_inc(sem.tc, 1)
-    PE.wait_ge(sem.pc0, 1)
-    for u in range(4, 12):
-        if u % 2 == 0:
-            PE.wait_ge(sem["wx%d" % (u // 2 - 2)], 16)
-        if u >= 7:
-            PE.wait_ge(sem["sn%d" % (u - 3)], 1)
-        score(u, (u - 4) % 3)
-        if u == 8:
-            full(1, 3)
+    full(1, 0)
+    full(2, 1)
     PE.wait_ge(sem.oc, 1)
-    turn(1)
-    full(2, 0)
-    product(0, 1)
-    PE.wait_ge(sem.ofx2, made[2])
     spread(3)
-    product(1, 2)
+    PE.wait_ge(sem.ofx2, made[2])
+    spread(4)
+    product(1, 3)
+    PE.wait_ge(sem.pc0, 1)
+    product(0, 2)
     PE.wait_ge(sem.pc1, 1)
-    product(2, 3)
+    product(2, 0)
 
     V.wait_ge(sem.mk, 2)
     for u in range(4):
-        groups(u, u % 2)
+        groups(u)
     V.wait_ge(sem.mt, 3)
-    V.wait_ge(sem.mu, 2)
-    V.wait_ge(sem.sp, 4)
-    cells(V, T, 0, T.uc[:, 0:1])
-    V.wait_ge(sem.cel0, 3)
-    widen(0, T.pm, T.cc[:, 0:1])
+    V.wait_ge(sem.mu, 1)
+    V.wait_ge(sem.sp, 5)
+    cells(V, T, 0, T.uc[:, 0:1], T.inc[:, 0:16], T.run[:], T.inc[:], 144)
     lists(0)
-    for j in range(3):
-        gather_v(j, 0)
-        if j < 2:
-            V.wait_ge(sem["n%d" % j], count(near))
-            widen(j + 1, T.pq, T.nin[:, 4 * j:4 * j + 1])
-        gather_v(j, 1)
-        if j < 2:
-            lists(j + 1)
-        else:
-            V.wait_ge(sem.tc, 1)
-            V.tensor_copy(T.offc[:], T.psT[:, 256:260]).then_inc(sem.oc, 1)
-        pack(j)
-    for u in range(4, 12):
-        groups(u, (u - 4) % 3)
-    V.wait_ge(sem.an, 24)
-    for lo, first in ((0, T.cc[0:64, 0:1]), (64, T.nin[64:128, 8:9])):
-        V.tensor_scalar(T.cc[lo:lo + 64, 8:9], first, T.nin[lo:lo + 64, 12:13], T.nin[lo:lo + 64, 16:17], Op.add, Op.add).then_inc(sem.tn, 1)
-    cells(V, T, 1, T.uc[:, 1:2])
-    V.wait_ge(sem.cel1, 3)
+    gather(V, 0, 0, 0, SHARE[0])
+    widen(0)
+    pack(0)
+    lists(1)
+    widen(1)
+    gather(V, 1, 0, 0, SHARE[1])
+    lists(2)
+    pack(1)
+    gather(V, 2, 0, 0, SHARE[2])
+    pack(2)
+    V.wait_ge(sem.tc, 1)
+    V.tensor_copy(T.offc[:], T.psT[:, 256:260]).then_inc(sem.oc, 1)
+    arrived(0, T.pa)
+    V.wait_ge(sem.an, 3 * E8)
+    for lo, first in ((0, T.run[0:64, 15:16]), (64, T.nin[64:128, 0:1])):
+        V.tensor_scalar(T.cc[lo:lo + 64, 0:1], first, number(2, lo, lo + 64), number(3, lo, lo + 64), Op.add, Op.add).then_inc(sem.tn, 1)
     V.wait_ge(sem.tn, 2)
-    V.tensor_scalar(col(T.bc, 3, 128), T.pa[:], T.cc[:, 4:5], T.cc[:, 8:9], Op.add, Op.add).then_inc(sem.bcx3, 1)
-    V.wait_ge(sem.ctx3, 1)
-    V.tensor_scalar(T.offl[:, 8:40], T.psT[:, 512 + 3:640:4], 16.0, None, Op.mult).then_inc(sem.ofx3, 1)
-    V.tensor_copy(T.chf[:], T.psT[:, 512:640]).then_inc(sem.chv, 1)
-    V.wait_ge(sem.ofx3, 1)
+    V.wait_ge(sem.bcx3, 2)
+    V.tensor_scalar(col(T.bc, 0, 128), col(T.bc, 3, 128), T.cc[:, 0:1], None, Op.add).then_inc(sem.bcx0, 1)
+    items(0)
+    V.wait_ge(sem.bcx0, 1)
+    arrived(1, T.bc)
     pick(V, 1)
+    items(1)
+    V.tensor_copy(T.chf[:], T.psT[:, spot(4):spot(4) + 128]).then_inc(sem.chv, 1)
     pick(V, 3)
+    bring(V, 0, 2)
     V.wait_ge(sem.chv, 1)
-    V.wait_ge(sem.oc, 1)
     V.tensor_copy(T.chg[:], T.chf[:, 0:128].indirect(T.offc[:, 0:4])).then_inc(sem.chv, 1)
 
-    S.wait_ge(sem.gp, 1)
-    S.activation(T.pa[:], T.p16[:], Copy, scale=1.0 / 16).then_inc(sem.sp, 1)
-    S.activation(T.pq[:], T.p16[:], Copy, scale=1.0 / 64).then_inc(sem.sp, 1)
-    S.activation(T.pm[0:64, :], T.p16[0:64, :], Copy, scale=1.0 / 16).then_inc(sem.sp, 1)
-    S.activation(T.pm[64:128, :], T.p16[64:128, :], Copy, scale=1.0 / 64).then_inc(sem.sp, 1)
-    for b in range(4):
-        S.wait_ge(sem["rs%d" % b], 1)
-    keep(0, 2)
-    gather_s(0)
-    gather_s(1)
-    gather_s(2)
-    pick(S, 0)
-    keep(1, 3)
-    keep(2, 0)
-    out_s(0, 1)
-    S.wait_ge(sem.ofx3, 1)
-    pick(S, 2)
-    out_s(1, 2)
-    pick(S, 4)
-    out_s(2, 3)
-    S.wait_ge(sem.yc1, 1)
-    S.wait_ge(sem.yc2, 1)
-    store(S, min(chosen[1:]), 2, sem.yd)
-    S.wait_ge(sem.yd, 16)
-
-    for ready, s in ((("yg0", "yc0"), min(me, chosen[0])), (("yg1", "yg2"), min(whole[:2])), (("yg3", "yg4"), min(whole[2:]))):
-        for name in ready:
-            SY.wait_ge(sem[name], 1)
-        store(SY, s, 2, sem.ye)
+    SY.wait_ge(sem.ofx3, 1)
+    store(SY, ("yg0",), me, sem.ye)
+    store(SY, ("yg1", "yg2"), min(whole[:2]), sem.ye)
+    store(SY, ("yg3", "yg4"), min(whole[2:]), sem.ye)
+    store(SY, ("yc0", "yc1"), min(chosen[:2]), sem.ye)
     SY.wait_ge(sem.chv, 2)
     SY.dma_start(T.ch[:], T.chg[0:1, :]).then_inc(sem.ye, 16)
-    SY.wait_ge(sem.ye, 16 * 4)
+    SY.wait_ge(sem.ye, 16 * 5)
 
     tr, post, finish = writer(g, core, T, topo)
     g.wait_ge(sem.mf, 1)
-    g.affine_select(T.idn[:], T.onf[:], [[-1, 128]], Op.is_equal, 0.0, 0, 1).then_inc(sem.gi, 1)
+    g.affine_select(T.idn[:], T.onf[:, 0:128], [[-1, 128]], Op.is_equal, 0.0, 0, 1).then_inc(sem.gi, 1)
     g.iota(T.p16[:], [[0, 8], [1, 16]], 0, 0, allow_small_or_imprecise_dtypes=True).then_inc(sem.gp, 1)
 
-    def pair(codes, plane, dst, land, mask, names):
-        post(tr(raw(codes), [(dst, raw(land[0]))], mask, sem[names[0]]))
-        post(tr(plane, [(dst, land[1])], mask, sem[names[1]]))
+    def pair(codes, plane, dsts, land, mask, names):
+        post(tr(raw(codes), [(c, raw(land[0])) for c in dsts], mask, sem[names[0]]))
+        post(tr(plane, [(c, land[1]) for c in dsts], mask, sem[names[1]]))
 
-    mate = cores[chosen[0]]
+    def slot(k):
+        return col(T.HQC, k, 128), col(T.HQS, k, 128)
+
     scorers = [plans[chosen[1 + i]]["out"][i] for i in range(2)]
     g.wait_ge(sem.qq, 1)
-    pair(Q[0], Q[1], scorers[0], (T.HQC[:], T.HQS[:]), far, ("hq", "hq"))
+    pair(Q[0], Q[1], scorers[:1], slot(2), far, ("hq", "hq"))
+    pair(Q[0], Q[1], [cores[chosen[0]]], (col(T.QC, 1, 128), col(T.QS, 1, 128)), far, ("qm", "qm"))
     g.wait_ge(sem.qx, 1)
-    pair(T.XC[:], T.XS[:], plan["out"][0], (T.HXC[:], T.HXS[:]), near, ("hxc", "hxs"))
-    pair(Q[0], Q[1], mate, (col(T.QC, 1, 128), col(T.QS, 1, 128)), far, ("qm", "qm"))
-    pair(T.XC[:], T.XS[:], plan["out"][1], (T.HXC[:], T.HXS[:]), near, ("hxc", "hxs"))
-    pair(Q[0], Q[1], scorers[1], (T.HQC[:], T.HQS[:]), far, ("hq", "hq"))
+    pair(T.XC[:], T.XS[:], plan["out"][:1], (T.HXC[:], T.HXS[:]), near, ("hxc", "hxs"))
+    pair(Q[0], Q[1], scorers[1:], slot(1), far, ("hq", "hq"))
+    pair(T.XC[:], T.XS[:], plan["out"][1:], (T.HXC[:], T.HXS[:]), near, ("hxc", "hxs"))
+    pair(Q[0], Q[1], plan["out"], slot(0), near, ("ho", "ho"))
     g.wait_ge(sem.qr, 1)
     for i, r in enumerate(plan["to"]):
-        pair(T.RC[:], T.RS[:], plans[r]["inb"], (col(T.HRC, i, 256), col(T.HRS, i, 256)), far, ("hrc%d" % i, "hrs%d" % i))
-    at = {me: (6, 8), chosen[0]: (70, 8), chosen[1]: (ENDS[0], 16), chosen[2]: (ENDS[1], 16)}
-    at.update({s: (32 * f + 3, 4) for f, s in enumerate(whole)})
+        pair(T.RC[:], T.RS[:], [plans[r]["inb"]], (col(T.HRC, i, 256), col(T.HRS, i, 256)), far, ("hrc%d" % i, "hrs%d" % i))
+    at = {me: (OWN, 8), chosen[0]: (64 + OWN, 8), chosen[1]: (ENDS[0], 16), chosen[2]: (ENDS[1], 16)}
+    at.update({s: (64 * (f % 2) + BOTH[f // 2], 8) for f, s in enumerate(whole)})
     for s, (first, step) in at.items():
         g.iota(T.tq[:, s:128:8], [[0, 8], [step, 2]], first, 2 * step, allow_small_or_imprecise_dtypes=True).then_inc(sem.gt, 1)
     g.wait_ge(sem.cel0, 3)
-    post(tr(T.cc[:, 0:1], [(mate, T.nin[:, 8:9])], far, sem.an))
-    for j, r in enumerate(chosen):
+    post(tr(T.run[:, 15:16], [(cores[chosen[0]], T.nin[:, 0:1])], far, sem.an))
+    g.wait_ge(sem.qz0, 1)
+    pair(col(T.OC, 0, 256), col(T.OS, 0, 256), plan["out"][:1], (T.HZC[:], T.HZS[:]), near, ("hzc", "hzs"))
+    for j in (1, 2):
         g.wait_ge(sem["qz%d" % j], 1)
-        pair(col(T.OC, j, 256), col(T.OS, j, 256), cores[r], (col(T.LC, j, 256), col(T.LS, j, 256)), far, ("d%d" % j,) * 2)
+        pair(col(T.OC, j, 256), col(T.OS, j, 256), [cores[chosen[j]]], (col(T.LC, j, 256), col(T.LS, j, 256)), far, ("d%d" % j,) * 2)
     finish()
+
+
+def hand_on(g, T, tr, post, wait, src, land, see, name, i, home, mate, near, far):
+    g.wait_ge(T.sem[wait], count(far))
+    post(tr(see(src), [(home, see(col(land, 2 * i, 256)))], near, T.sem[name + str(2 * i)]),
+         tr(see(src), [(mate, see(col(land, 2 * i + 1, 256)))], far, T.sem[name + str(2 * i + 1)]))
 
 
 def scorer_program(g, core, me, T, topo):
@@ -450,64 +479,85 @@ def scorer_program(g, core, me, T, topo):
     Op = AluOpType
     V, PE = g.vector, g.tensor
     tr, post, finish = writer(g, core, T, topo)
-    askers = [plan["to"][i], plans[plan["to"][i]]["mate"]]
-    far = topo.mask(core, cores[askers[0]])
-    near = topo.mask(core, cores[me]) & ~far
-    arrive = count(near)
+    home, mate, on = cores[me], cores[plan["mate"]], plans[plan["to"][i]]["out"][i]
+    far = topo.mask(core, mate)
+    near = topo.mask(core, home) & ~far
+    E8 = count(far)
+    items = ((T.HXC, T.HXS), (T.HYC, T.HYS))
+    asked = ((128 * (2 - i), 128), (0, 256))
+    view = ((15 - ENDS[i], 1), (15 - 2 * BOTH[i], 2))
+    ends = ((ENDS[i], 16), (BOTH[i], 8))
 
     V.memset(T.onf[:], 1.0).then_inc(sem.mf, 1)
     V.memset(T.msk[:], BIG).then_inc(sem.mk, 1)
     V.memset(T.top[:], BIG).then_inc(sem.mt, 1)
-    for h in range(2):
-        V.memset(T.sc[:, 264 * h + 128:264 * h + 136], 0.0).then_inc(sem.mt, 1)
+    for u in range(4):
+        n = asked[u // 2][1]
+        V.memset(T.sc[:, PAD * u + n:PAD * u + n + 16], 0.0).then_inc(sem.mt, 1)
     V.wait_ge(sem.mk, 1)
-    V.memset(T.msk[:, 0:128:16], -BIG).then_inc(sem.mk, 1)
+    V.memset(T.msk[:, 0:256:16], -BIG).then_inc(sem.mk, 1)
     V.wait_ge(sem.gi, 1)
-    V.tensor_reduce(T.uc[:, 0:1], T.idn[:, ENDS[i]:128:16], AxisListType.X, Op.add).then_inc(sem.mu, 1)
+    for bt in range(2):
+        V.tensor_reduce(T.uc[:, bt:bt + 1], T.idn[:, ends[bt][0]:128:ends[bt][1]], AxisListType.X, Op.add).then_inc(sem.mu, 1)
     V.wait_ge(sem.mk, 2)
-    for h in range(2):
-        V.wait_ge(sem["sm%d" % h], 1)
-        V.tensor_tensor_scan(T.sc[:, 264 * h:264 * h + 128], T.msk[:], T.psP[:, 512 * h:512 * h + 128], -BIG, Op.min, Op.max).then_inc(sem["sn%d" % h], 1)
-    V.wait_ge(sem.mt, 3)
-    V.wait_ge(sem.mu, 1)
-    cells(V, T, 0, T.uc[:, 0:1])
-
-    PE.wait_ge(sem.hxc, arrive)
-    PE.wait_ge(sem.hxs, arrive)
-    PE.wait_ge(sem.hq, 2 * count(far))
-    for h in range(2):
-        PE.matmul_mx(T.psP[:, 512 * h:512 * h + 128], col(T.HXC, h, 128), col(T.HXS, h, 128), T.HQC[:], T.HQS[:], True, True).then_inc(sem["sm%d" % h], 1)
+    V.wait_ge(sem.mt, 5)
+    V.wait_ge(sem.mu, 2)
+    V.wait_ge(sem.mf, 1)
     PE.wait_ge(sem.gi, 1)
-    PE.wait_ge(sem.mt, 3)
-    for h in range(2):
-        k = 264 * h + 15 - ENDS[i]
-        PE.wait_ge(sem["sn%d" % h], 1)
-        PE.transpose(col(T.psT, h, 128), T.sc[:, k:k + 128], T.idn[:]).then_inc(sem["tr0%d" % h], 1)
+    PE.wait_ge(sem.mt, 5)
+    for bt in range(2):
+        a, n = asked[bt]
+        for name, times in ((("hxc", 1), ("hxs", 1), ("hq", 2)), (("hyc", 1), ("hys", 1), ("ho", 2), ("hm", 2 - 2 * i)))[bt]:
+            if times:
+                PE.wait_ge(sem[name], times * E8)
+        for h in range(2):
+            u = 2 * bt + h
+            PE.matmul_mx(T.psP[:, 512 * u:512 * u + n], col(items[bt][0], h, 128), col(items[bt][1], h, 128),
+                         T.HQC[:, a:a + n], T.HQS[:, a:a + n], True, True).then_inc(sem["sm%d" % u], 1)
+            V.wait_ge(sem["sm%d" % u], 1)
+            V.tensor_tensor_scan(T.sc[:, PAD * u:PAD * u + n], T.msk[:, 0:n], T.psP[:, 512 * u:512 * u + n], -BIG, Op.min, Op.max).then_inc(sem["sn%d" % u], 1)
+        for h in range(2):
+            u = 2 * bt + h
+            k = PAD * u + view[bt][0]
+            PE.wait_ge(sem["sn%d" % u], 1)
+            PE.transpose(T.psT[:, 512 * bt + 128 * h:512 * bt + 128 * h + 128], T.sc[:, k:k + n:view[bt][1]], T.idn[:]).then_inc(sem["tr%d%d" % (bt, h)], 1)
+        cells(V, T, bt, T.uc[:, bt:bt + 1], col(T.ltb, bt, 16), col(T.cnt, bt, 16), col(T.ltb, bt, 16), 16)
+
+    def tell(bt, there, k_home, k_there, s_home, s_there):
+        g.wait_ge(sem["cel%d" % bt], 3)
+        src = T.cnt[:, 16 * bt + 15:16 * bt + 16]
+        post(tr(src, [(home, T.nib[:, 8 * k_home:8 * k_home + 1])], near, s_home),
+             tr(src, [(there, T.nib[:, 8 * k_there:8 * k_there + 1])], far, s_there))
 
     g.wait_ge(sem.mf, 1)
-    g.affine_select(T.idn[:], T.onf[:], [[-1, 128]], Op.is_equal, 0.0, 0, 1).then_inc(sem.gi, 1)
-    g.wait_ge(sem.hxc, arrive)
-    for k, r in enumerate(askers):
-        f = 2 * i + k
-        post(tr(raw(T.HXC[:]), [(cores[r], raw(col(T.FXC, f, 256)))], far, sem["wx%d" % f]))
-        g.wait_ge(sem.hxs, arrive)
-        post(tr(T.HXS[:], [(cores[r], col(T.FXS, f, 256))], far, sem["wx%d" % f]))
-    g.wait_ge(sem.cel0, 3)
-    post(tr(T.cc[:, 0:1], [(cores[me], T.nin[:, 4 * i:4 * i + 1])], near, sem["n%d" % i]),
-         tr(T.cc[:, 0:1], [(cores[plan["chosen"][1 + i]], T.nin[:, 12 + 4 * i:13 + 4 * i])], far, sem.an))
+    g.affine_select(T.idn[:], T.onf[:, 0:128], [[-1, 128]], Op.is_equal, 0.0, 0, 1).then_inc(sem.gi, 1)
+    g.wait_ge(sem.hxc, E8)
+    post(tr(raw(T.HXC[:]), [(on, raw(T.HYC[:]))], far, sem.hyc))
+    g.wait_ge(sem.hxs, E8)
+    post(tr(T.HXS[:], [(on, T.HYS[:])], far, sem.hys))
+    if i == 1:
+        g.wait_ge(sem.hq, 2 * E8)
+        post(tr(raw(col(T.HQC, 1, 128)), [(plan["out"][0], raw(col(T.HQC, 1, 128)))], near, sem.hm))
+        post(tr(col(T.HQS, 1, 128), [(plan["out"][0], col(T.HQS, 1, 128))], near, sem.hm))
+    tell(0, cores[plan["chosen"][1 + i]], i, 2 + i, sem["n%d" % i], sem.an)
+    hand_on(g, T, tr, post, "hyc", T.HYC[:], T.FXC, raw, "wx", i, home, mate, near, far)
+    hand_on(g, T, tr, post, "hys", T.HYS[:], T.FXS, same, "wx", i, home, mate, near, far)
+    tell(1, mate, 4 + 2 * i, 5 + 2 * i, sem["aw%d" % i], sem["aw%d" % i])
+    if i == 0:
+        for wait, src, land, see in (("hzc", T.HZC, T.LC, raw), ("hzs", T.HZS, T.LS, same)):
+            g.wait_ge(sem[wait], E8)
+            post(tr(see(src[:]), [(cores[plan["chosen"][0]], see(col(land, 0, 256)))], far, sem.d0))
     finish()
 
 
 def relay_program(g, core, me, T, topo):
     plan = make_plan(me, T, topo)
-    cores, sem = T.cores, T.sem
+    cores = T.cores
     tr, post, finish = writer(g, core, T, topo)
     home, mate = cores[me], cores[plan["mate"]]
     far = topo.mask(core, mate)
     near = topo.mask(core, home) & ~far
     for i in range(2):
-        for wait, src, land, see in (("hrc", T.HRC, T.FRC, raw), ("hrs", T.HRS, T.FRS, lambda ap: ap)):
-            g.wait_ge(sem[wait + str(i)], count(far))
-            post(tr(see(col(src, i, 256)), [(home, see(col(land, 2 * i, 256)))], near, sem["wr%d" % (2 * i)]),
-                 tr(see(col(src, i, 256)), [(mate, see(col(land, 2 * i + 1, 256)))], far, sem["wr%d" % (2 * i + 1)]))
+        for wait, src, land, see in (("hrc", T.HRC, T.FRC, raw), ("hrs", T.HRS, T.FRS, same)):
+            hand_on(g, T, tr, post, wait + str(i), col(src, i, 256), land, see, "wr", i, home, mate, near, far)
     finish()

@@ -18,10 +18,11 @@ SCRATCH = {
     "pq": ("sbuf", [128, 128], F32),
     "inc": ("sbuf", [128, 144], F32),
     "run": ("sbuf", [128, 144], F32),
+    "two": ("sbuf", [128, 16], F32),
     "tq": ("sbuf", [128, 128], F32),
     "uc": ("sbuf", [128, 8], F32),
     "msk": ("sbuf", [128, 256], F32),
-    "top": ("sbuf", [128, 256], F32),
+    "top": ("sbuf", [128, 128], F32),
     "QC": ("sbuf", [128, 256], CODES),
     "QS": ("sbuf", [128, 256], PLANE),
     "XC": ("sbuf", [128, 256], CODES),
@@ -30,13 +31,13 @@ SCRATCH = {
     "RS": ("sbuf", [128, 256], PLANE),
     "EC": ("sbuf", [128, 512], CODES),
     "ES": ("sbuf", [128, 512], PLANE),
-    "sc": ("sbuf", [128, 1088], F32),
+    "sc": ("sbuf", [128, 1056], F32),
     "rm": ("sbuf", [128, 512], F32),
     "ltb": ("sbuf", [128, 32], F32),
     "cnt": ("sbuf", [128, 32], BF16),
     "cc": ("sbuf", [128, 8], F32),
-    "bc": ("sbuf", [128, 768], F32),
-    "nin": ("sbuf", [128, 4], F32),
+    "bc": ("sbuf", [128, 512], F32),
+    "nin": ("sbuf", [128, 12], F32),
     "nib": ("sbuf", [128, 64], BF16),
     "off": ("sbuf", [128, 96], U16),
     "offl": ("sbuf", [128, 40], U16),
@@ -69,23 +70,20 @@ SCRATCH = {
     "psP": ("psum", [128, 2048], F32),
 }
 SEMAPHORES = (
-    ["lq", "lx", "mf", "me", "mk", "mt", "mu", "qq", "qx", "qr", "qe", "gi", "gp", "gt", "sp", "si", "tc", "oc"]
+    ["lq", "lx", "mf", "me", "mk", "mt", "mu", "qq", "qx", "qr", "qe", "gi", "gp", "gt", "sp", "si", "st", "tc", "oc", "ol"]
     + ["dm%d" % b for b in range(4)] + ["rs%d" % b for b in range(4)]
-    + [n + str(u) for n in ("sm", "sn") for u in range(4)]
-    + ["tr%d%d" % (b, h) for b in range(2) for h in range(2)]
-    + [n + str(b) for n in ("bcx", "ctx", "ofx") for b in range(5)]
-    + [n + str(b) for n in ("cel", "n", "aw", "hrc", "hrs") for b in range(2)]
-    + [n + str(j) for n in ("ym", "yc", "d", "pm", "pc", "qz") for j in range(3)]
+    + [n + str(u) for n in ("sm", "sn", "bcx", "ctx", "ofx", "wx", "wr") for u in range(4)]
+    + [n + str(b) for n in ("tr", "cel", "n", "hrc", "hrs") for b in range(2)]
+    + [n + str(j) for n in ("ym", "yc", "d", "qz", "pm", "pc") for j in range(3)]
     + [n + str(j) for n in ("gv", "gs") for j in range(6)]
-    + [n + str(j) for n in ("wx", "wr") for j in range(4)]
     + ["yg%d" % j for j in range(5)]
-    + ["qm", "an", "tn", "chv", "yd", "ye", "sent", "hq", "ho", "hm", "hxc", "hxs", "hyc", "hys", "hzc", "hzs"]
+    + ["qm", "an", "aw0", "aw1", "cta", "ofa", "tn", "sg", "chv", "yd", "ye", "sent", "hq", "hp", "ho", "hw", "hm", "hxc", "hxs", "hya", "hyc", "hys", "hzc", "hzs"]
 )
-ENDS = (13, 12)
-BOTH = (7, 3)
-OWN = 6
-PAD = 272
-SHARE = (32, 26, 26)
+ENDS = (7, 5)
+BOTH = (3, 2)
+OWN = 1
+BATCH = 528
+SHARE = (28, 26, 24)
 
 
 def make_plan(me, T, topo):
@@ -109,6 +107,10 @@ def make_plan(me, T, topo):
 
 def count(mask):
     return bin(mask).count("1")
+
+
+def every_other(mask):
+    return sum([1 << e for e in range(mask.bit_length()) if mask >> e & 1][0::2])
 
 
 def writer(g, core, T, topo):
@@ -143,16 +145,24 @@ def same(ap):
     return ap
 
 
-def cells(V, T, bt, unit, lt, out, terms, n):
-    Op, sem = AluOpType, T.sem
-    V.wait_ge(sem["tr%d0" % bt], 1)
-    V.wait_ge(sem["tr%d1" % bt], 1)
-    rm, done = 256 * bt, sem["cel%d" % bt]
-    V.tensor_tensor_scan(T.rm[:, rm:rm + 256], T.top[:], T.psT[:, 512 * bt:512 * bt + 256], -BIG, Op.min, Op.max).then_inc(done, 1)
-    V.wait_ge(done, 1)
-    V.tensor_scalar(lt, T.rm[:, rm + 15:rm + 256:16], T.rm[:, rm + 255:rm + 256], unit, Op.is_lt, Op.mult).then_inc(done, 1)
-    V.wait_ge(done, 2)
-    V.tensor_tensor_scan(out, T.onf[:, 0:n], terms, 0.0, Op.mult, Op.add).then_inc(done, 1)
+def running(V, T, bt, lo):
+    Op, done = AluOpType, T.sem["cel%d" % bt]
+    V.wait_ge(T.sem["tr%d" % bt], 1)
+    for h in range(2):
+        k = 256 * bt + 128 * h
+        start = T.rm[lo:lo + 64, k - 1:k] if h else -BIG
+        V.tensor_tensor_scan(T.rm[lo:lo + 64, k:k + 128], T.top[lo:lo + 64, :], T.psT[64 * h:64 * h + 64, 512 * bt:512 * bt + 128],
+                             start, Op.min, Op.max).then_inc(done, 1)
+        V.wait_ge(done, h + 1)
+    return T.rm[lo:lo + 64, 256 * bt + 15:256 * bt + 256:16], T.rm[lo:lo + 64, 256 * bt + 255:256 * bt + 256]
+
+
+def cells(V, T, bt, lo, unit, lt, out, terms, n):
+    Op, done = AluOpType, T.sem["cel%d" % bt]
+    ends, last = running(V, T, bt, lo)
+    V.tensor_scalar(lt, ends, last, unit, Op.is_lt, Op.mult).then_inc(done, 1)
+    V.wait_ge(done, 3)
+    V.tensor_tensor_scan(out, T.onf[lo:lo + 64, 0:n], terms, 0.0, Op.mult, Op.add).then_inc(done, 1)
 
 
 def rank_program(g, core, T, topo):
@@ -171,7 +181,7 @@ def rank_program(g, core, T, topo):
     chosen, whole = plan["chosen"], plan["whole"]
     cores, sem = T.cores, T.sem
     Op = AluOpType
-    Copy = ActivationFunctionType.Copy
+    Copy, Identity = ActivationFunctionType.Copy, ActivationFunctionType.Identity
     V, S, PE, SY = g.vector, g.scalar, g.tensor, g.sync
     Q = (col(T.QC, 0, 128), col(T.QS, 0, 128))
     far = topo.mask(core, cores[chosen[0]])
@@ -181,7 +191,7 @@ def rank_program(g, core, T, topo):
     def bank(b, n):
         return T.psP[:, 512 * b:512 * b + n]
 
-    def number(k, lo=0, hi=128):
+    def number(k, lo, hi):
         return T.nib[lo:hi, 8 * k:8 * k + 1]
 
     SY.dma_start(T.qwb[:], T.qw[:]).then_inc(sem.lq, 16)
@@ -197,12 +207,14 @@ def rank_program(g, core, T, topo):
     V.memset(T.msk[:, 0:128:16], -BIG).then_inc(sem.mk, 1)
     V.wait_ge(sem.me, 2)
     for b in range(4):
+        if b == 2:
+            V.wait_ge(sem.lq, 16)
+            V.quantize_mx(Q[0], Q[1], T.qwb[:]).then_inc(sem.qq, 1)
         V.quantize_mx(col(T.EC, b, 128), col(T.ES, b, 128), T.eb[:, 4 - b:516 - b]).then_inc(sem.qe, 1)
-    V.wait_ge(sem.lq, 16)
-    V.quantize_mx(Q[0], Q[1], T.qwb[:]).then_inc(sem.qq, 1)
     V.wait_ge(sem.lx, 16)
     V.quantize_mx(T.XC[:], T.XS[:], T.xb[:]).then_inc(sem.qx, 1)
     V.memset(T.top[:], BIG).then_inc(sem.mt, 1)
+    V.memset(T.sc[:, 512:BATCH], 0.0).then_inc(sem.mt, 1)
     for b in range(4):
         V.wait_ge(sem["dm%d" % b], 1)
         k = 512 * (b % 2)
@@ -210,9 +222,7 @@ def rank_program(g, core, T, topo):
     for b in range(4):
         V.wait_ge(sem["rs%d" % b], 1)
     V.quantize_mx(T.RC[:], T.RS[:], T.rb[:]).then_inc(sem.qr, 1)
-    for h in range(2):
-        V.memset(T.sc[:, PAD * h + 256:PAD * h + PAD], 0.0).then_inc(sem.mt, 1)
-    V.tensor_reduce(T.uc[:, 0:1], T.idn[:, OWN:128:8], AxisListType.X, Op.add).then_inc(sem.mu, 1)
+    V.tensor_reduce(T.uc[:, 0:1], T.idn[:, OWN:64:4], AxisListType.X, Op.add).then_inc(sem.mu, 1)
 
     PE.wait_ge(sem.qx, 1)
     PE.wait_ge(sem.qe, 4)
@@ -228,31 +238,28 @@ def rank_program(g, core, T, topo):
 
     def groups(u):
         h = u % 2
-        k = PAD * h + 128 * (u // 2)
         V.wait_ge(sem["sm%d" % u], 1)
-        V.tensor_tensor_scan(T.sc[:, k:k + 128], T.msk[:, 0:128], bank(h, 128), -BIG, Op.min, Op.max).then_inc(sem["sn%d" % u], 1)
+        V.tensor_tensor_scan(col(T.sc, 2 * h + u // 2, 128), T.msk[:, 0:128], bank(h, 128), -BIG, Op.min, Op.max).then_inc(sem["sn%d" % u], 1)
 
     def spot(i):
         return 512 * ((i + 1) % 2)
 
     def spread(i):
-        PE.wait_ge(*((sem["bcx%d" % i], 1 + i // 3) if i else (sem.cel0, 3)))
+        PE.wait_ge(*((sem["bcx%d" % i], 1) if i else (sem.cel0, 4)))
         PE.transpose(T.psT[:, spot(i):spot(i) + 128], col(T.bc, i, 128) if i else T.run[:, 16:144], T.idn[:]).then_inc(sem["ctx%d" % i], 1)
 
     def widen(j):
         V.wait_ge(sem["n%d" % j], count(near))
-        V.tensor_scalar(col(T.bc, j + 1, 128), T.pq[:], number(j), None, Op.add).then_inc(sem["bcx%d" % (j + 1)], 1)
+        V.tensor_scalar(col(T.bc, j + 1, 128), T.pq[:], T.nin[:, 4 + 4 * j:5 + 4 * j], None, Op.add).then_inc(sem["bcx%d" % (j + 1)], 1)
 
     def lists(j):
         V.wait_ge(sem["ctx%d" % j], 1)
-        first, step = ((64 + OWN, 8), (ENDS[0], 16), (ENDS[1], 16))[j]
-        src = T.psT[:, spot(j) + first:spot(j) + 128:step]
+        if j:
+            V.tensor_scalar(col(T.off, j, 32), T.psT[:, spot(j) + 65:spot(j) + 128:2], 64.0, None, Op.mult).then_inc(sem["ofx%d" % j], 4)
+            return
         for e in range(4):
-            V.tensor_scalar(T.off[:, 32 * j + e:32 * j + 32:4], src, 64.0, 16.0 * e, Op.mult, Op.add).then_inc(sem["ofx%d" % j], 1)
-        if j == 0:
-            V.tensor_scalar(T.offl[:, 0:8], T.psT[:, spot(0) + OWN:spot(0) + 64:8], 16.0, None, Op.mult).then_inc(sem.ofx0, 1)
+            V.tensor_scalar(T.off[:, e:32:4], T.psT[:, spot(0) + 32 + OWN:spot(0) + 64:4], 64.0, 16.0 * e, Op.mult, Op.add).then_inc(sem.ofx0, 1)
 
-    made = (5, 4, 4)
     calls = {}
 
     def move(E, out, src):
@@ -262,32 +269,32 @@ def rank_program(g, core, T, topo):
         if lo == hi:
             return
         a, name = 1024 * j + 512 * part, ("gv%d" if E is V else "gs%d") % (2 * j + part)
-        E.wait_ge(sem["ofx%d" % j], made[j])
+        E.wait_ge(sem["ofx%d" % j], 4)
         move(E, T.hb[:, a + 16 * lo:a + 16 * hi], (T.xb, T.rb)[part][:, 0:1024].indirect(T.off[:, 32 * j + lo:32 * j + hi])).then_inc(sem[name], 1)
         calls[name] = calls.get(name, 0) + 1
 
-    def pack(j):
-        for name in [n % (2 * j + part) for part in range(2) for n in ("gv%d", "gs%d")]:
+    def pack(j, parts=(0, 1)):
+        for name in [n % (2 * j + part) for part in parts for n in ("gv%d", "gs%d")]:
             if name in calls:
                 V.wait_ge(sem[name], calls[name])
-        V.quantize_mx(col(T.OC, j, 256), col(T.OS, j, 256), col(T.hb, j, 1024)).then_inc(sem["qz%d" % j], 1)
+        a, n = 256 * j + 128 * parts[0], 128 * len(parts)
+        V.quantize_mx(T.OC[:, a:a + n], T.OS[:, a:a + n], T.hb[:, 4 * a:4 * (a + n)]).then_inc(sem["qz%d" % j], 1)
 
     every = [me] + whole
 
     def pick(E, i):
         E.wait_ge(sem["pc%d" % ((i + 1) // 2)], 1)
-        if i:
-            E.wait_ge(sem["ofx%d" % (2 + (i + 1) // 2)], 1)
+        E.wait_ge(sem[("ol", "ofa", "ofx3")[(i + 1) // 2]], 1)
         move(E, col(T.ysb, every[i], 128), col(T.pf, i, 256).indirect(col(T.offl, i, 8))).then_inc(sem["yg%d" % i], 1)
 
-    def full(i, b):
-        parts = [(T.XC[:], T.XS[:]), (T.RC[:], T.RS[:])] if i == 0 else \
-            [(col(c, i - 1, 512), col(p, i - 1, 512)) for c, p in ((T.FXC, T.FXS), (T.FRC, T.FRS))]
-        for part, (c, p) in enumerate(parts):
-            for f in range(2 * i - 2, 2 * i) if i else ():
-                PE.wait_ge(sem[("wx%d", "wr%d")[part] % f], 2 * E8)
-            mm = PE.matmul_mx(bank(b, 512 if i else 256), Q[0], Q[1], c, p, part == 0, part == 1)
-        mm.then_inc(sem["pm%d" % i], 1)
+    def full(i, b, part):
+        c, p = ((T.FXC, T.FXS), (T.FRC, T.FRS))[part] if i else ((T.XC, T.XS), (T.RC, T.RS))[part]
+        n = 512 if i else 256
+        for f in range(2 * i - 2, 2 * i) if i else ():
+            PE.wait_ge(sem[("wx%d", "wr%d")[part] % f], (3 * E8, (2 + i) * E8 // 2)[part])
+        mm = PE.matmul_mx(bank(b, n), Q[0], Q[1], col(c, max(i - 1, 0), n), col(p, max(i - 1, 0), n), part == 0, part == 1)
+        if part:
+            mm.then_inc(sem["pm%d" % i], 1)
 
     def keep(E, i, b):
         E.wait_ge(sem["pm%d" % i], 1)
@@ -308,41 +315,43 @@ def rank_program(g, core, T, topo):
             E.wait_ge(sem[name], 1)
         E.dma_start(T.y[:, 128 * s:128 * (s + len(ready))], T.ysb[:, 128 * s:128 * (s + len(ready))]).then_inc(done, 16)
 
-    def arrived(i, base):
-        V.wait_ge(sem["aw%d" % i], 2 * E8)
-        for h in range(2):
-            lo = 64 * h
-            V.tensor_scalar(T.bc[lo:lo + 64, 384 + 128 * i:512 + 128 * i], base[lo:lo + 64, 0:128], number(4 + 2 * i + h, lo, lo + 64),
-                            None, Op.add).then_inc(sem["bcx%d" % (3 + i)], 1)
-
-    def items(i):
-        V.wait_ge(sem["ctx%d" % (3 + i)], 1)
-        k = spot(3 + i)
-        V.tensor_scalar(T.offl[:, 8 + 16 * i:24 + 16 * i], T.psT[:, k + BOTH[i]:k + 128:8], 16.0, None, Op.mult).then_inc(sem["ofx%d" % (3 + i)], 1)
-
     S.wait_ge(sem.mf, 1)
-    for lo, unit in ((0, 1.0 / 16), (64, 1.0 / 64)):
-        S.activation(T.inc[lo:lo + 64, 16:144], T.onf[lo:lo + 64, 0:128], Copy, scale=unit).then_inc(sem.si, 1)
+    units = ((0, 1.0 / 16), (32, 1.0 / 64))
+    for lo, unit in units:
+        S.activation(T.inc[lo:lo + 32, 16:144], T.onf[lo:lo + 32, 0:128], Copy, scale=unit).then_inc(sem.si, 1)
+    S.activation(T.run[64:128, :], T.onf[64:128, :], Copy, scale=0.0).then_inc(sem.sp, 1)
+    S.activation(T.bc[64:128, 0:128], T.onf[64:128, 0:128], Copy, scale=0.0).then_inc(sem.sp, 1)
     S.wait_ge(sem.si, 2)
-    for lo, unit in ((0, 1.0 / 16), (64, 1.0 / 64)):
-        S.activation(T.inc[lo:lo + 64, 32:144:16], T.onf[lo:lo + 64, 0:7], Copy, scale=-15 * unit).then_inc(sem.sp, 1)
-    S.activation(T.inc[:, 16:17], T.onf[:, 0:1], Copy, scale=0.0).then_inc(sem.sp, 1)
+    for lo, unit in units:
+        S.activation(T.inc[lo:lo + 32, 32:144:16], T.onf[lo:lo + 32, 0:7], Copy, scale=-15 * unit).then_inc(sem.sp, 1)
+    S.activation(T.inc[0:64, 16:17], T.onf[0:64, 0:1], Copy, scale=0.0).then_inc(sem.sp, 1)
     S.wait_ge(sem.gp, 1)
     S.activation(T.pa[:], T.p16[:], Copy, scale=1.0 / 16).then_inc(sem.sp, 1)
-    S.activation(T.pq[:], T.p16[:], Copy, scale=1.0 / 64).then_inc(sem.sp, 1)
+    S.wait_ge(sem.gi, 1)
+    for e in range(1, 4):
+        S.activation(T.ltb[:, 0:16], T.idn[:, 2 * e + 1:128:8], Copy, scale=0.25 * e, accum_out=T.uc[:, e:e + 1]).then_inc(sem.sg, 1)
+        S.wait_ge(sem.sg, e)
+    for e in range(2):
+        S.activation(T.uc[:, 4 + e:5 + e], T.uc[:, 1 + 3 * e:2 + 3 * e], Identity, bias=T.uc[:, 2 + e:3 + e]).then_inc(sem.sg, 1)
+        S.wait_ge(sem.sg, 4 + e)
+    S.activation(T.pq[:], T.p16[:], Identity, bias=T.uc[:, 5:6], scale=1.0 / 64).then_inc(sem.sp, 1)
+    at = {me: (OWN, 4), chosen[0]: (32 + OWN, 4), chosen[1]: (64 + ENDS[0], 8), chosen[2]: (64 + ENDS[1], 8)}
+    at.update({s: (32 * (f % 2) + BOTH[f // 2], 4) for f, s in enumerate(whole)})
+    S.wait_ge(sem.gt, 1)
+    for s, (first, step) in at.items():
+        S.activation(T.tq[:, s:128:8], T.two[:], Identity, bias=float(first), scale=float(step)).then_inc(sem.st, 1)
     for b in range(4):
         S.wait_ge(sem["rs%d" % b], 1)
     keep(S, 0, 2)
     for j in range(3):
         gather(S, j, 1, 0, 32)
         gather(S, j, 0, SHARE[j], 32)
-        if j == 0:
-            pick(S, 0)
+    pick(S, 0)
     keep(S, 1, 0)
     keep(S, 2, 1)
     pick(S, 2)
-    bring(S, 1, 3)
     pick(S, 4)
+    bring(S, 1, 3)
     bring(S, 2, 0)
     store(S, ("yc2",), chosen[2], sem.yd)
     S.wait_ge(sem.yd, 16)
@@ -350,30 +359,36 @@ def rank_program(g, core, T, topo):
     PE.wait_ge(sem.qq, 1)
     score(0)
     score(1)
-    PE.wait_ge(sem.qr, 1)
-    full(0, 2)
-    PE.wait_ge(sem.qm, 2 * E8)
+    PE.wait_ge(sem.st, N)
+    PE.transpose(T.psT[:, 512:640], T.tq[:], T.idn[:]).then_inc(sem.tc, 1)
+    PE.wait_ge(sem.qm, E8)
+    PE.wait_ge(sem.hp, E8 // 2)
     for h in range(2):
         PE.wait_ge(sem["sn%d" % h], 1)
         score(2 + h)
-    PE.wait_ge(sem.mt, 3)
-    for h in range(2):
-        PE.wait_ge(sem["sn%d" % (2 + h)], 1)
-        k = PAD * h + 15 - 2 * OWN
-        PE.transpose(col(T.psT, h, 128), T.sc[:, k:k + 256:2], T.idn[:]).then_inc(sem["tr0%d" % h], 1)
+    PE.wait_ge(sem.mt, 2)
+    PE.wait_ge(sem.sn2, 1)
+    PE.wait_ge(sem.sn3, 1)
+    k = 15 - 4 * OWN
+    PE.transpose(T.psT[:, 0:128], T.sc[:, k:k + 512:4], T.idn[:]).then_inc(sem.tr0, 1)
+    PE.wait_ge(sem.qr, 1)
+    full(0, 2, 0)
+    full(0, 2, 1)
+    PE.wait_ge(sem.oc, 1)
     spread(0)
     spread(1)
-    PE.wait_ge(sem.ofx0, made[0])
+    PE.wait_ge(sem.ol, 1)
+    PE.wait_ge(sem.ofx0, 4)
     spread(2)
-    PE.wait_ge(sem.gt, N)
-    PE.wait_ge(sem.ofx1, made[1])
-    PE.transpose(T.psT[:, 256:384], T.tq[:], T.idn[:]).then_inc(sem.tc, 1)
-    full(1, 0)
-    full(2, 1)
-    PE.wait_ge(sem.oc, 1)
+    full(1, 0, 0)
+    full(1, 0, 1)
+    full(2, 1, 0)
+    full(2, 1, 1)
+    PE.wait_ge(sem.ofx2, 4)
+    PE.wait_ge(sem.bcx0, 2)
+    PE.transpose(T.psT[:, 512:640], col(T.bc, 0, 128), T.idn[:]).then_inc(sem.cta, 1)
+    PE.wait_ge(sem.ofx1, 4)
     spread(3)
-    PE.wait_ge(sem.ofx2, made[2])
-    spread(4)
     product(1, 3)
     PE.wait_ge(sem.pc0, 1)
     product(0, 2)
@@ -381,44 +396,53 @@ def rank_program(g, core, T, topo):
     product(2, 0)
 
     V.wait_ge(sem.mk, 2)
-    for u in range(4):
-        groups(u)
-    V.wait_ge(sem.mt, 3)
+    groups(0)
+    groups(1)
+    V.wait_ge(sem.tc, 1)
+    V.tensor_copy(T.offc[:], T.psT[:, 512:516]).then_inc(sem.oc, 1)
+    groups(2)
+    groups(3)
+    V.wait_ge(sem.mt, 2)
     V.wait_ge(sem.mu, 1)
-    V.wait_ge(sem.sp, 5)
-    cells(V, T, 0, T.uc[:, 0:1], T.inc[:, 0:16], T.run[:], T.inc[:], 144)
+    V.wait_ge(sem.sp, 7)
+    cells(V, T, 0, 0, T.uc[0:64, 0:1], T.inc[0:64, 0:16], T.run[0:64, :], T.inc[0:64, :], 144)
     lists(0)
-    gather(V, 0, 0, 0, SHARE[0])
     widen(0)
-    pack(0)
+    V.tensor_scalar(T.offl[:, 0:8], T.psT[:, spot(0) + OWN:spot(0) + 32:4], 16.0, None, Op.mult).then_inc(sem.ol, 1)
+    gather(V, 0, 0, 0, SHARE[0])
     lists(1)
     widen(1)
+    pack(0)
     gather(V, 1, 0, 0, SHARE[1])
     lists(2)
     pack(1)
     gather(V, 2, 0, 0, SHARE[2])
-    pack(2)
-    V.wait_ge(sem.tc, 1)
-    V.tensor_copy(T.offc[:], T.psT[:, 256:260]).then_inc(sem.oc, 1)
-    arrived(0, T.pa)
+    pack(2, (1,))
+    pack(2, (0,))
+    V.wait_ge(sem.aw0, 2 * E8)
+    for h in range(2):
+        lo = 32 * h
+        V.tensor_scalar(T.bc[lo:lo + 32, 0:128], T.pa[lo:lo + 32, :], number(4 + h, lo, lo + 32), None, Op.add).then_inc(sem.bcx0, 1)
     V.wait_ge(sem.an, 3 * E8)
-    for lo, first in ((0, T.run[0:64, 15:16]), (64, T.nin[64:128, 0:1])):
-        V.tensor_scalar(T.cc[lo:lo + 64, 0:1], first, number(2, lo, lo + 64), number(3, lo, lo + 64), Op.add, Op.add).then_inc(sem.tn, 1)
-    V.wait_ge(sem.tn, 2)
-    V.wait_ge(sem.bcx3, 2)
-    V.tensor_scalar(col(T.bc, 0, 128), col(T.bc, 3, 128), T.cc[:, 0:1], None, Op.add).then_inc(sem.bcx0, 1)
-    items(0)
-    V.wait_ge(sem.bcx0, 1)
-    arrived(1, T.bc)
+    V.tensor_scalar(T.cc[64:128, 0:1], number(2, 64, 128), number(3, 64, 128), None, Op.add).then_inc(sem.tn, 1)
+    V.wait_ge(sem.aw1, 2 * E8)
+    for h, first in enumerate((T.run[0:32, 15:16], T.nin[32:64, 0:1])):
+        lo = 32 * h
+        V.tensor_scalar(T.cc[lo:lo + 32, 0:1], first, number(4 + h, lo, lo + 32), number(6 + h, lo, lo + 32), Op.add, Op.add).then_inc(sem.tn, 1)
+    V.wait_ge(sem.tn, 3)
+    V.tensor_scalar(col(T.bc, 3, 128), T.pa[:], T.cc[:, 0:1], None, Op.add).then_inc(sem.bcx3, 1)
+    V.wait_ge(sem.cta, 1)
+    V.tensor_scalar(T.offl[:, 8:24], T.psT[:, 512 + BOTH[0]:512 + 64:4], 16.0, None, Op.mult).then_inc(sem.ofa, 1)
     pick(V, 1)
-    items(1)
-    V.tensor_copy(T.chf[:], T.psT[:, spot(4):spot(4) + 128]).then_inc(sem.chv, 1)
+    V.wait_ge(sem.ctx3, 1)
+    V.tensor_scalar(T.offl[:, 24:40], T.psT[:, spot(3) + BOTH[1]:spot(3) + 64:4], 16.0, None, Op.mult).then_inc(sem.ofx3, 1)
     pick(V, 3)
     bring(V, 0, 2)
+    V.tensor_copy(T.chf[:], T.psT[:, spot(3):spot(3) + 128]).then_inc(sem.chv, 1)
     V.wait_ge(sem.chv, 1)
     V.tensor_copy(T.chg[:], T.chf[:, 0:128].indirect(T.offc[:, 0:4])).then_inc(sem.chv, 1)
 
-    SY.wait_ge(sem.ofx3, 1)
+    SY.wait_ge(sem.cta, 1)
     store(SY, ("yg0",), me, sem.ye)
     store(SY, ("yg1", "yg2"), min(whole[:2]), sem.ye)
     store(SY, ("yg3", "yg4"), min(whole[2:]), sem.ye)
@@ -431,36 +455,37 @@ def rank_program(g, core, T, topo):
     g.wait_ge(sem.mf, 1)
     g.affine_select(T.idn[:], T.onf[:, 0:128], [[-1, 128]], Op.is_equal, 0.0, 0, 1).then_inc(sem.gi, 1)
     g.iota(T.p16[:], [[0, 8], [1, 16]], 0, 0, allow_small_or_imprecise_dtypes=True).then_inc(sem.gp, 1)
+    g.iota(T.two[:], [[0, 8], [1, 2]], 0, 2, allow_small_or_imprecise_dtypes=True).then_inc(sem.gt, 1)
 
     def pair(codes, plane, dsts, land, mask, names):
-        post(tr(raw(codes), [(c, raw(land[0])) for c in dsts], mask, sem[names[0]]))
         post(tr(plane, [(c, land[1]) for c in dsts], mask, sem[names[1]]))
+        post(tr(raw(codes), [(c, raw(land[0])) for c in dsts], mask, sem[names[0]]))
 
     def slot(k):
         return col(T.HQC, k, 128), col(T.HQS, k, 128)
 
     scorers = [plans[chosen[1 + i]]["out"][i] for i in range(2)]
     g.wait_ge(sem.qq, 1)
-    pair(Q[0], Q[1], scorers[:1], slot(2), far, ("hq", "hq"))
-    pair(Q[0], Q[1], [cores[chosen[0]]], (col(T.QC, 1, 128), col(T.QS, 1, 128)), far, ("qm", "qm"))
+    bits = [1 << e for e in topo.engines(core, scorers[0])]
+    post(tr(raw(Q[0]), [(scorers[0], raw(slot(2)[0]))], sum(bits[0::2]), sem.hq))
+    post(tr(Q[1], [(scorers[0], slot(2)[1]), (cores[chosen[0]], col(T.QS, 1, 128))], sum(bits[1::2]), sem.hp))
+    post(tr(raw(Q[0]), [(cores[chosen[0]], raw(col(T.QC, 1, 128)))], far, sem.qm))
     g.wait_ge(sem.qx, 1)
     pair(T.XC[:], T.XS[:], plan["out"][:1], (T.HXC[:], T.HXS[:]), near, ("hxc", "hxs"))
-    pair(Q[0], Q[1], scorers[1:], slot(1), far, ("hq", "hq"))
-    pair(T.XC[:], T.XS[:], plan["out"][1:], (T.HXC[:], T.HXS[:]), near, ("hxc", "hxs"))
-    pair(Q[0], Q[1], plan["out"], slot(0), near, ("ho", "ho"))
+    pair(Q[0], Q[1], scorers[1:], slot(1), far, ("hq", "hp"))
+    post(tr(T.XS[:], [(plan["out"][1], T.HXS[:])], near, sem.hxs))
+    post(tr(Q[1], [(plan["out"][0], slot(0)[1])], near, sem.hw))
+    post(tr(raw(T.XC[:]), [(plan["out"][1], raw(T.HXC[:]))], near, sem.hxc))
+    post(tr(raw(Q[0]), [(h, raw(slot(0)[0])) for h in plan["out"]], near, sem.ho))
     g.wait_ge(sem.qr, 1)
     for i, r in enumerate(plan["to"]):
         pair(T.RC[:], T.RS[:], [plans[r]["inb"]], (col(T.HRC, i, 256), col(T.HRS, i, 256)), far, ("hrc%d" % i, "hrs%d" % i))
-    at = {me: (OWN, 8), chosen[0]: (64 + OWN, 8), chosen[1]: (ENDS[0], 16), chosen[2]: (ENDS[1], 16)}
-    at.update({s: (64 * (f % 2) + BOTH[f // 2], 8) for f, s in enumerate(whole)})
-    for s, (first, step) in at.items():
-        g.iota(T.tq[:, s:128:8], [[0, 8], [step, 2]], first, 2 * step, allow_small_or_imprecise_dtypes=True).then_inc(sem.gt, 1)
-    g.wait_ge(sem.cel0, 3)
+    g.wait_ge(sem.cel0, 4)
     post(tr(T.run[:, 15:16], [(cores[chosen[0]], T.nin[:, 0:1])], far, sem.an))
     g.wait_ge(sem.qz0, 1)
-    pair(col(T.OC, 0, 256), col(T.OS, 0, 256), plan["out"][:1], (T.HZC[:], T.HZS[:]), near, ("hzc", "hzs"))
+    pair(col(T.OC, 0, 256), col(T.OS, 0, 256), plan["out"][:1], (T.HZC[:], T.HZS[:]), near | far, ("hzc", "hzs"))
     for j in (1, 2):
-        g.wait_ge(sem["qz%d" % j], 1)
+        g.wait_ge(sem["qz%d" % j], j)
         pair(col(T.OC, j, 256), col(T.OS, j, 256), [cores[chosen[j]]], (col(T.LC, j, 256), col(T.LS, j, 256)), far, ("d%d" % j,) * 2)
     finish()
 
@@ -477,7 +502,7 @@ def scorer_program(g, core, me, T, topo):
     cores, sem = T.cores, T.sem
     i = plan["out"].index(core)
     Op = AluOpType
-    V, PE = g.vector, g.tensor
+    V, S, PE = g.vector, g.scalar, g.tensor
     tr, post, finish = writer(g, core, T, topo)
     home, mate, on = cores[me], cores[plan["mate"]], plans[plan["to"][i]]["out"][i]
     far = topo.mask(core, mate)
@@ -485,20 +510,21 @@ def scorer_program(g, core, me, T, topo):
     E8 = count(far)
     items = ((T.HXC, T.HXS), (T.HYC, T.HYS))
     asked = ((128 * (2 - i), 128), (0, 256))
-    view = ((15 - ENDS[i], 1), (15 - 2 * BOTH[i], 2))
-    ends = ((ENDS[i], 16), (BOTH[i], 8))
+    ends = ((64 + ENDS[i], 128, 8), (BOTH[i], 64, 4))
 
     V.memset(T.onf[:], 1.0).then_inc(sem.mf, 1)
     V.memset(T.msk[:], BIG).then_inc(sem.mk, 1)
     V.memset(T.top[:], BIG).then_inc(sem.mt, 1)
-    for u in range(4):
-        n = asked[u // 2][1]
-        V.memset(T.sc[:, PAD * u + n:PAD * u + n + 16], 0.0).then_inc(sem.mt, 1)
+    V.memset(T.cnt[:], 0.0).then_inc(sem.mt, 1)
+    V.memset(T.cc[:], 0.0).then_inc(sem.mt, 1)
+    for bt in range(2):
+        k = BATCH * bt + 2 * asked[bt][1]
+        V.memset(T.sc[:, k:k + 16], 0.0).then_inc(sem.mt, 1)
     V.wait_ge(sem.mk, 1)
     V.memset(T.msk[:, 0:256:16], -BIG).then_inc(sem.mk, 1)
     V.wait_ge(sem.gi, 1)
     for bt in range(2):
-        V.tensor_reduce(T.uc[:, bt:bt + 1], T.idn[:, ends[bt][0]:128:ends[bt][1]], AxisListType.X, Op.add).then_inc(sem.mu, 1)
+        V.tensor_reduce(T.uc[:, bt:bt + 1], T.idn[:, ends[bt][0]:ends[bt][1]:ends[bt][2]], AxisListType.X, Op.add).then_inc(sem.mu, 1)
     V.wait_ge(sem.mk, 2)
     V.wait_ge(sem.mt, 5)
     V.wait_ge(sem.mu, 2)
@@ -507,45 +533,72 @@ def scorer_program(g, core, me, T, topo):
     PE.wait_ge(sem.mt, 5)
     for bt in range(2):
         a, n = asked[bt]
-        for name, times in ((("hxc", 1), ("hxs", 1), ("hq", 2)), (("hyc", 1), ("hys", 1), ("ho", 2), ("hm", 2 - 2 * i)))[bt]:
-            if times:
-                PE.wait_ge(sem[name], times * E8)
+        for name, halves in ((("hxc", 2), ("hxs", 2), ("hq", 1 + i), ("hp", 1 + i)), (("hya", 2), ("hys", 2), ("ho", 2), ("hw", 2), ("hm", 4 - 4 * i)))[bt]:
+            if halves:
+                PE.wait_ge(sem[name], halves * E8 // 2)
         for h in range(2):
-            u = 2 * bt + h
+            u, k = 2 * bt + h, BATCH * bt + n * h
+            if bt and h:
+                PE.wait_ge(sem.hyc, E8)
             PE.matmul_mx(T.psP[:, 512 * u:512 * u + n], col(items[bt][0], h, 128), col(items[bt][1], h, 128),
                          T.HQC[:, a:a + n], T.HQS[:, a:a + n], True, True).then_inc(sem["sm%d" % u], 1)
             V.wait_ge(sem["sm%d" % u], 1)
-            V.tensor_tensor_scan(T.sc[:, PAD * u:PAD * u + n], T.msk[:, 0:n], T.psP[:, 512 * u:512 * u + n], -BIG, Op.min, Op.max).then_inc(sem["sn%d" % u], 1)
-        for h in range(2):
-            u = 2 * bt + h
-            k = PAD * u + view[bt][0]
-            PE.wait_ge(sem["sn%d" % u], 1)
-            PE.transpose(T.psT[:, 512 * bt + 128 * h:512 * bt + 128 * h + 128], T.sc[:, k:k + n:view[bt][1]], T.idn[:]).then_inc(sem["tr%d%d" % (bt, h)], 1)
-        cells(V, T, bt, T.uc[:, bt:bt + 1], col(T.ltb, bt, 16), col(T.cnt, bt, 16), col(T.ltb, bt, 16), 16)
-
-    def tell(bt, there, k_home, k_there, s_home, s_there):
-        g.wait_ge(sem["cel%d" % bt], 3)
-        src = T.cnt[:, 16 * bt + 15:16 * bt + 16]
-        post(tr(src, [(home, T.nib[:, 8 * k_home:8 * k_home + 1])], near, s_home),
-             tr(src, [(there, T.nib[:, 8 * k_there:8 * k_there + 1])], far, s_there))
+            V.tensor_tensor_scan(T.sc[:, k:k + n], T.msk[:, 0:n], T.psP[:, 512 * u:512 * u + n], -BIG, Op.min, Op.max).then_inc(sem["sn%d" % u], 1)
+        step = n // 64
+        k = BATCH + 15 - step * BOTH[i] if bt else 1
+        PE.wait_ge(sem["sn%d" % (2 * bt)], 1)
+        PE.wait_ge(sem["sn%d" % (2 * bt + 1)], 1)
+        if not bt:
+            for E, places in ((V, (3, 7)), (S, (11,))):
+                E.wait_ge(sem.sn0, 1)
+                E.wait_ge(sem.sn1, 1)
+                for c in places:
+                    out, src = T.sc[:, c:256:16], T.sc[:, 15:256:16]
+                    (V.tensor_copy(out, src) if E is V else S.activation(out, src, ActivationFunctionType.Copy)).then_inc(sem.tn, 1)
+            PE.wait_ge(sem.tn, 3)
+        PE.transpose(T.psT[:, 512 * bt:512 * bt + 128], T.sc[:, k:k + 2 * n:step], T.idn[:]).then_inc(sem["tr%d" % bt], 1)
+        if bt:
+            cells(V, T, 1, 0, T.uc[0:64, 1:2], T.ltb[0:64, 16:32], T.cnt[0:64, 16:32], T.ltb[0:64, 16:32], 16)
+        else:
+            cell_ends, last = running(V, T, 0, 64)
+            S.wait_ge(sem.cel0, 2)
+            S.activation(T.ltb[64:128, 0:16], cell_ends, ActivationFunctionType.Sign, bias=last, scale=-1.0,
+                         accum_out=T.cc[64:128, 0:1]).then_inc(sem.sg, 1)
+            S.wait_ge(sem.sg, 1)
+            S.wait_ge(sem.mu, 2)
+            S.activation(T.cnt[64:128, 15:16], T.cc[64:128, 0:1], ActivationFunctionType.Copy, scale=T.uc[64:128, 0:1]).then_inc(sem.sg, 1)
 
     g.wait_ge(sem.mf, 1)
     g.affine_select(T.idn[:], T.onf[:, 0:128], [[-1, 128]], Op.is_equal, 0.0, 0, 1).then_inc(sem.gi, 1)
-    g.wait_ge(sem.hxc, E8)
-    post(tr(raw(T.HXC[:]), [(on, raw(T.HYC[:]))], far, sem.hyc))
     g.wait_ge(sem.hxs, E8)
     post(tr(T.HXS[:], [(on, T.HYS[:])], far, sem.hys))
     if i == 1:
-        g.wait_ge(sem.hq, 2 * E8)
-        post(tr(raw(col(T.HQC, 1, 128)), [(plan["out"][0], raw(col(T.HQC, 1, 128)))], near, sem.hm))
+        g.wait_ge(sem.hp, E8)
         post(tr(col(T.HQS, 1, 128), [(plan["out"][0], col(T.HQS, 1, 128))], near, sem.hm))
-    tell(0, cores[plan["chosen"][1 + i]], i, 2 + i, sem["n%d" % i], sem.an)
-    hand_on(g, T, tr, post, "hyc", T.HYC[:], T.FXC, raw, "wx", i, home, mate, near, far)
+    g.wait_ge(sem.hxc, E8)
+    for h in range(2):
+        post(tr(raw(col(T.HXC, h, 128)), [(on, raw(col(T.HYC, h, 128)))], far, sem[("hya", "hyc")[h]]))
+    if i == 1:
+        g.wait_ge(sem.hq, E8)
+        post(tr(raw(col(T.HQC, 1, 128)), [(plan["out"][0], raw(col(T.HQC, 1, 128)))], near, sem.hm))
+    else:
+        g.wait_ge(sem.hw, E8)
+        post(tr(col(T.HQS, 0, 128), [(plan["out"][1], col(T.HQS, 0, 128))], near, sem.hw))
+    g.wait_ge(sem.sg, 1)
+    post(tr(T.cc[:, 0:1], [(home, T.nin[:, 4 + 4 * i:5 + 4 * i])], near, sem["n%d" % i]))
+    g.wait_ge(sem.sg, 2)
+    post(tr(T.cnt[:, 15:16], [(cores[plan["chosen"][1 + i]], T.nib[:, 16 + 8 * i:17 + 8 * i])], far, sem.an))
     hand_on(g, T, tr, post, "hys", T.HYS[:], T.FXS, same, "wx", i, home, mate, near, far)
-    tell(1, mate, 4 + 2 * i, 5 + 2 * i, sem["aw%d" % i], sem["aw%d" % i])
+    for h in range(2):
+        g.wait_ge(sem[("hya", "hyc")[h]], E8)
+        post(tr(raw(col(T.HYC, h, 128)), [(home, raw(col(T.FXC, 4 * i + h, 128)))], near, sem["wx%d" % (2 * i)]),
+             tr(raw(col(T.HYC, h, 128)), [(mate, raw(col(T.FXC, 4 * i + 2 + h, 128)))], far, sem["wx%d" % (2 * i + 1)]))
+    g.wait_ge(sem.cel1, 4)
+    post(*[tr(T.cnt[:, 31:32], [(c, T.nib[:, 8 * k:8 * k + 1])], mask, sem["aw%d" % i])
+           for c, k, mask in ((home, 4 + 2 * i, near), (mate, 5 + 2 * i, far))])
     if i == 0:
-        for wait, src, land, see in (("hzc", T.HZC, T.LC, raw), ("hzs", T.HZS, T.LS, same)):
-            g.wait_ge(sem[wait], E8)
+        for wait, src, land, see in (("hzs", T.HZS, T.LS, same), ("hzc", T.HZC, T.LC, raw)):
+            g.wait_ge(sem[wait], count(near | far))
             post(tr(see(src[:]), [(cores[plan["chosen"][0]], see(col(land, 0, 256)))], far, sem.d0))
     finish()
 
@@ -558,6 +611,11 @@ def relay_program(g, core, me, T, topo):
     far = topo.mask(core, mate)
     near = topo.mask(core, home) & ~far
     for i in range(2):
-        for wait, src, land, see in (("hrc", T.HRC, T.FRC, raw), ("hrs", T.HRS, T.FRS, same)):
-            hand_on(g, T, tr, post, wait + str(i), col(src, i, 256), land, see, "wr", i, home, mate, near, far)
+        for wait, src, land, see in (("hrs", T.HRS, T.FRS, same), ("hrc", T.HRC, T.FRC, raw)):
+            if (i, wait) == (0, "hrs"):
+                g.wait_ge(T.sem.hrs0, count(far))
+                post(tr(col(src, 0, 256), [(home, col(land, 0, 256))], every_other(near), T.sem.wr0),
+                     tr(col(src, 0, 256), [(mate, col(land, 1, 256))], every_other(far), T.sem.wr1))
+            else:
+                hand_on(g, T, tr, post, wait + str(i), col(src, i, 256), land, see, "wr", i, home, mate, near, far)
     finish()

@@ -1,28 +1,28 @@
 from concourse.bass import DstId, RemoteDMATransfer
-from concourse.mybir import dt, AluOpType, AxisListType, ActivationFunctionType
+from concourse.mybir import dt, AluOpType, ActivationFunctionType
 
 N = 8
 BIG = 1e29
 CODES, PLANE = "float8_e4m3fn_x4", "uint8"
-F32, BF16, U16 = "float32", "bfloat16", "uint16"
+F32, BF16, U16, I32 = "float32", "bfloat16", "uint16", "int32"
 
 SCRATCH = {
     "qwb": ("sbuf", [128, 512], BF16),
     "xb": ("sbuf", [128, 1024], BF16),
     "rb": ("sbuf", [128, 1024], BF16),
     "eb": ("sbuf", [128, 528], BF16),
-    "onf": ("sbuf", [128, 144], F32),
+    "onb": ("sbuf", [128, 128], BF16),
+    "onf": ("sbuf", [128, 128], F32),
     "idn": ("sbuf", [128, 128], F32),
     "p16": ("sbuf", [128, 128], F32),
-    "pa": ("sbuf", [128, 128], F32),
     "pq": ("sbuf", [128, 128], F32),
-    "inc": ("sbuf", [128, 144], F32),
-    "run": ("sbuf", [128, 144], F32),
-    "two": ("sbuf", [128, 16], F32),
-    "tq": ("sbuf", [128, 128], F32),
-    "uc": ("sbuf", [128, 8], F32),
-    "msk": ("sbuf", [128, 256], F32),
-    "top": ("sbuf", [128, 128], F32),
+    "side": ("sbuf", [128, 128], F32),
+    "pi": ("sbuf", [128, 8], I32),
+    "pm": ("sbuf", [128, 4], F32),
+    "msk": ("sbuf", [128, 32], F32),
+    "anew": ("sbuf", [128, 32], F32),
+    "top": ("sbuf", [128, 256], F32),
+    "offd": ("sbuf", [128, 2], U16),
     "QC": ("sbuf", [128, 256], CODES),
     "QS": ("sbuf", [128, 256], PLANE),
     "XC": ("sbuf", [128, 256], CODES),
@@ -31,17 +31,20 @@ SCRATCH = {
     "RS": ("sbuf", [128, 256], PLANE),
     "EC": ("sbuf", [128, 512], CODES),
     "ES": ("sbuf", [128, 512], PLANE),
-    "sc": ("sbuf", [128, 1056], F32),
-    "rm": ("sbuf", [128, 512], F32),
-    "ltb": ("sbuf", [128, 32], F32),
+    "rm": ("sbuf", [128, 768], F32),
+    "ta": ("sbuf", [128, 96], F32),
+    "tb": ("sbuf", [128, 96], F32),
+    "tc": ("sbuf", [128, 96], F32),
+    "td": ("sbuf", [128, 96], F32),
+    "lt": ("sbuf", [128, 64], F32),
     "cnt": ("sbuf", [128, 32], BF16),
-    "cc": ("sbuf", [128, 8], F32),
-    "bc": ("sbuf", [128, 512], F32),
+    "bc": ("sbuf", [128, 768], F32),
     "nin": ("sbuf", [128, 12], F32),
-    "nib": ("sbuf", [128, 64], BF16),
+    "nb": ("sbuf", [128, 64], BF16),
+    "adj": ("sbuf", [128, 32], F32),
+    "chs": ("sbuf", [128, 8], F32),
     "off": ("sbuf", [128, 96], U16),
     "offl": ("sbuf", [128, 40], U16),
-    "offc": ("sbuf", [128, 4], U16),
     "hb": ("sbuf", [128, 3072], BF16),
     "OC": ("sbuf", [128, 768], CODES),
     "OS": ("sbuf", [128, 768], PLANE),
@@ -55,38 +58,81 @@ SCRATCH = {
     "HQS": ("sbuf", [128, 384], PLANE),
     "HXC": ("sbuf", [128, 256], CODES),
     "HXS": ("sbuf", [128, 256], PLANE),
-    "HYC": ("sbuf", [128, 256], CODES),
-    "HYS": ("sbuf", [128, 256], PLANE),
-    "HZC": ("sbuf", [128, 256], CODES),
-    "HZS": ("sbuf", [128, 256], PLANE),
+    "HYC": ("sbuf", [128, 512], CODES),
+    "HYS": ("sbuf", [128, 512], PLANE),
     "HRC": ("sbuf", [128, 512], CODES),
     "HRS": ("sbuf", [128, 512], PLANE),
+    "HZC": ("sbuf", [128, 256], CODES),
+    "HZS": ("sbuf", [128, 256], PLANE),
     "pf": ("sbuf", [128, 1280], F32),
     "ysb": ("sbuf", [128, 128 * N], F32),
-    "chf": ("sbuf", [128, 128], F32),
-    "chg": ("sbuf", [128, 64], F32),
-    "psD": ("psum", [128, 1024], F32),
-    "psT": ("psum", [128, 1024], F32),
+    "dly": ("sbuf", [128, 1024], F32),
+    "psD": ("psum", [128, 2048], F32),
     "psP": ("psum", [128, 2048], F32),
 }
 SEMAPHORES = (
-    ["lq", "lx", "mf", "me", "mk", "mt", "mu", "qq", "qx", "qr", "qe", "gi", "gp", "gt", "sp", "si", "st", "tc", "oc", "ol"]
+    ["lq", "lx", "mf", "me", "mk", "mt", "mu", "qq", "qx", "qr", "qe", "gi", "gp", "gt", "sp", "si", "so"]
     + ["dm%d" % b for b in range(4)] + ["rs%d" % b for b in range(4)]
-    + [n + str(u) for n in ("sm", "sn", "bcx", "ctx", "ofx", "wx", "wr") for u in range(4)]
-    + [n + str(b) for n in ("tr", "cel", "n", "hrc", "hrs") for b in range(2)]
-    + [n + str(j) for n in ("ym", "yc", "d", "qz", "pm", "pc") for j in range(3)]
-    + [n + str(j) for n in ("gv", "gs") for j in range(6)]
+    + [n + str(u) for n in ("wx", "wr") for u in range(4)]
+    + [n + str(u) for n in ("bcx", "ctx", "ofx", "gv", "gs", "qz", "d") for u in range(6)]
+    + [n + str(b) for n in ("sm", "sn", "cel", "aw", "hq", "hp", "hys", "hya", "hyb") for b in range(2)]
+    + [n + str(j) for n in ("n", "ym", "yc", "pm", "pc") for j in range(3)]
     + ["yg%d" % j for j in range(5)]
-    + ["qm", "an", "aw0", "aw1", "cta", "ofa", "tn", "sg", "chv", "yd", "ye", "sent", "hq", "hp", "ho", "hw", "hm", "hxc", "hxs", "hya", "hyc", "hys", "hzc", "hzs"]
+    + ["an", "chv", "yd", "ye", "sent", "hrc0", "hrs0", "hrc1", "hrs1", "hw", "ho", "hm", "sm2", "sn2", "cel2", "sb", "hxc", "hxs", "hzc", "hzs"]
 )
-ENDS = (7, 5)
-BOTH = (3, 2)
-OWN = 1
-BATCH = 528
-SHARE = (28, 26, 24)
+MARK = 16.0
+SHARE = (24, 24, 24)
+CUT = (20, 10)
+LAST = (12, 10)
+PIECES = ("hys", "hya")
+NUMAT = (None, None)
+TWINS = 1
+SWAP = False
+PLAN = 0
+WORLD = 256
+VIA = ()
+SPLIT = False
+PRE = (0, 0)
+FULL = ((1, 0, True), (1, 1, False), (2, 1, True), (2, 0, False))
+RB = 0
+DELAY = 0
+HOLD = 0
+B1VIA = False
+EARLY = True
+UNITS = (((0, 0), (1, 0), (0, 1), (1, 1)), ((0, 1), (0, 0), (1, 1), (1, 0)))
+HM = 1
+QD = 0
+FOUR = (1, 2)
+XO = 1
+SPARE_DIE = 0
+WIDE = True
+WEAVE = 4
+QAT = 0
+FILL = False
+ANVIA = True
+QP = 0
+QH = 0
+EQ = (0, 1)
+B1P = False
+B0ALL = True
+LEAD = 1
+OWNW = 0
+VSEQ = [("l", 0), ("w", 1), ("g", 0, 0, 0, 28), ("l", 1), ("w", 2), ("p", 0), ("g", 1, 0, 0, 24), ("l", 2), ("p", 1),
+        ("g", 2, 0, 0, 28), ("p", 2, 1), ("p", 2, 0), ("W", 0), ("W", 1), ("n",), ("s", 4), ("s", 5), ("k", 1), ("k", 3), ("b", 0)]
+SSEQ = [("g", 0, 1, 0, 32), ("g", 0, 0, 28, 32), ("g", 1, 1, 0, 32), ("g", 1, 0, 24, 32), ("g", 2, 1, 0, 32), ("g", 2, 0, 28, 32), ("K", 1), ("K", 2),
+        ("k", 2), ("k", 4), ("b", 1), ("b", 2)]
+
+
+PLANS = {}
 
 
 def make_plan(me, T, topo):
+    if me not in PLANS:
+        PLANS[me] = new_plan(me, T, topo)
+    return PLANS[me]
+
+
+def new_plan(me, T, topo):
     cores = T.cores
     core = cores[me]
 
@@ -97,11 +143,16 @@ def make_plan(me, T, topo):
     k, n = ring.index(me), len(ring)
     mate, before, after, across = mate_of(me), ring[(k - 1) % n], ring[(k + 1) % n], ring[(k + 2) % n]
     free = [c for c in topo.cores_of(core) if c != core and topo.may_write(c, cores[mate])]
+    beside = [c for c in free if topo.die(c) == topo.die(core)]
+    other = [c for c in free if c not in beside]
+    taken = [c for r in cores for c in topo.cores_of(r)]
+    idle = [c for c in range(WORLD) if c not in taken and topo.same_plane(c, core) and topo.die(c) == topo.die(other[SPARE_DIE] if SPARE_DIE == 0 else core)
+            and topo.may_write(c, cores[mate])]
+    firsts = [c for c in idle if not any(d < c for d in idle if d in topo.cores_of(c))]
     return {
-        "mate": mate, "to": [after, before], "chosen": [mate_of(across), across, mate],
+        "spare": firsts[k], "home": core, "mate": mate, "to": [after, before], "chosen": [mate_of(across), across, mate],
         "whole": [before, mate_of(before), after, mate_of(after)],
-        "inb": [c for c in free if topo.die(c) == topo.die(core)][0],
-        "out": [c for c in free if topo.die(c) != topo.die(core)][:2],
+        "scorer": other[0], "passers": [beside[0], other[1]], "out": other[:2], "inb": beside[0],
     }
 
 
@@ -109,8 +160,13 @@ def count(mask):
     return bin(mask).count("1")
 
 
-def every_other(mask):
-    return sum([1 << e for e in range(mask.bit_length()) if mask >> e & 1][0::2])
+def every_other(mask, k=0):
+    return sum([1 << e for e in range(mask.bit_length()) if mask >> e & 1][k::2])
+
+
+def engines(core, near_by, plan, T, topo):
+    far = topo.mask(core, T.cores[plan["mate"]])
+    return far, topo.mask(core, near_by) & ~far
 
 
 def writer(g, core, T, topo):
@@ -122,7 +178,7 @@ def writer(g, core, T, topo):
             rid, pid = topo.addr(c, core)
             ids.append(DstId(rid=rid, pnc=pid))
         sent[0] += count(mask)
-        return RemoteDMATransfer(dst_ids=ids, dma_engine_mask=mask, remote_sem=rsem, srcs=[src], dsts=[ap for c, ap in dsts])
+        return RemoteDMATransfer(dst_ids=ids, dma_engine_mask=mask, remote_sem=T.sem[rsem], srcs=[src], dsts=[ap for c, ap in dsts])
 
     def post(*transfers):
         g.remote_dma_fused(list(transfers), local_sem=T.sem.sent)
@@ -145,120 +201,161 @@ def same(ap):
     return ap
 
 
-def running(V, T, bt, lo):
-    Op, done = AluOpType, T.sem["cel%d" % bt]
-    V.wait_ge(T.sem["tr%d" % bt], 1)
-    for h in range(2):
-        k = 256 * bt + 128 * h
-        start = T.rm[lo:lo + 64, k - 1:k] if h else -BIG
-        V.tensor_tensor_scan(T.rm[lo:lo + 64, k:k + 128], T.top[lo:lo + 64, :], T.psT[64 * h:64 * h + 64, 512 * bt:512 * bt + 128],
-                             start, Op.min, Op.max).then_inc(done, 1)
-        V.wait_ge(done, h + 1)
-    return T.rm[lo:lo + 64, 256 * bt + 15:256 * bt + 256:16], T.rm[lo:lo + 64, 256 * bt + 255:256 * bt + 256]
+def pieces(codes, plane, k):
+    return col(plane, k, 256), raw(col(codes, k, 256))
 
 
-def cells(V, T, bt, lo, unit, lt, out, terms, n):
+def running(V, T, u, scores):
+    V.wait_ge(T.sem["sm%d" % u], 1)
+    V.tensor_tensor_scan(col(T.rm, u, 256), T.top[:], scores, -BIG, AluOpType.min, AluOpType.max).then_inc(T.sem["sn%d" % u], 1)
+
+
+def group_steps(V, T, bt, ends, after, repeat=True):
     Op, done = AluOpType, T.sem["cel%d" % bt]
-    ends, last = running(V, T, bt, lo)
-    V.tensor_scalar(lt, ends, last, unit, Op.is_lt, Op.mult).then_inc(done, 1)
+    a, b, c, d = [col(t, bt, 32) for t in (T.ta, T.tb, T.tc, T.td)]
+    calls = [lambda: V.transpose(a, ends), lambda: V.tensor_tensor_scan(b, T.msk[:], a, -BIG, Op.min, Op.max)]
+    calls += [lambda: V.tensor_copy(c, b.indirect(T.offd[:, 0:2])), lambda: V.transpose(d, c)] if repeat else [lambda: V.transpose(d, b)]
+
+    def step(k):
+        for name in after if k == 0 else ():
+            V.wait_ge(T.sem[name], 1)
+        if k:
+            V.wait_ge(done, k)
+        calls[k]().then_inc(done, 1 if k + 1 < len(calls) else 4 - k)
+
+    return [lambda k=k: step(k) for k in range(len(calls))]
+
+
+def by_group(V, T, bt, ends, fill=None, repeat=True):
+    Op, done = AluOpType, T.sem["cel%d" % bt]
+    a, b, c, d = [col(t, bt, 32) for t in (T.ta, T.tb, T.tc, T.td)]
+    V.transpose(a, ends).then_inc(done, 1)
+    if fill:
+        fill()
+    V.wait_ge(done, 1)
+    V.tensor_tensor_scan(b, T.msk[:], a, -BIG, Op.min, Op.max).then_inc(done, 1)
+    V.wait_ge(done, 2)
+    if not repeat:
+        V.transpose(d, b).then_inc(done, 2)
+        return
+    V.tensor_copy(c, b.indirect(T.offd[:, 0:2])).then_inc(done, 1)
     V.wait_ge(done, 3)
-    V.tensor_tensor_scan(out, T.onf[lo:lo + 64, 0:n], terms, 0.0, Op.mult, Op.add).then_inc(done, 1)
+    V.transpose(d, c).then_inc(done, 1)
+
+
+def cell(S, ends, last, scrap, out, done):
+    S.activation(scrap, ends, ActivationFunctionType.Sign, bias=last, scale=-1.0, accum_out=out).then_inc(done, 1)
 
 
 def rank_program(g, core, T, topo):
     me = T.rank_of(core)
     if me is None:
+        for r in range(N):
+            if VIA and not PLAN and core == make_plan(r, T, topo)["spare"]:
+                spare_program(g, core, r, T, topo)
         homes = [T.rank_of(c) for c in topo.cores_of(core) if T.rank_of(c) is not None]
         if homes:
             plan = make_plan(homes[0], T, topo)
-            if core in plan["out"]:
+            if PLAN == 0:
+                if core in plan["out"]:
+                    helper_program(g, core, homes[0], T, topo)
+                if core == plan["inb"]:
+                    relay_program(g, core, homes[0], T, topo)
+            elif core == plan["scorer"]:
                 scorer_program(g, core, homes[0], T, topo)
-            if core == plan["inb"]:
-                relay_program(g, core, homes[0], T, topo)
+            elif core in plan["passers"]:
+                passer_program(g, core, homes[0], T, topo)
         return
     plans = [make_plan(r, T, topo) for r in range(N)]
     plan = plans[me]
     chosen, whole = plan["chosen"], plan["whole"]
     cores, sem = T.cores, T.sem
     Op = AluOpType
-    Copy, Identity = ActivationFunctionType.Copy, ActivationFunctionType.Identity
+    Copy, Identity, Sign = ActivationFunctionType.Copy, ActivationFunctionType.Identity, ActivationFunctionType.Sign
     V, S, PE, SY = g.vector, g.scalar, g.tensor, g.sync
     Q = (col(T.QC, 0, 128), col(T.QS, 0, 128))
-    far = topo.mask(core, cores[chosen[0]])
-    near = topo.mask(core, plan["out"][0]) & ~far
+    far, near = engines(core, plan["scorer"], plan, T, topo)
     E8 = count(far)
 
     def bank(b, n):
         return T.psP[:, 512 * b:512 * b + n]
 
-    def number(k, lo, hi):
-        return T.nib[lo:hi, 8 * k:8 * k + 1]
-
     SY.dma_start(T.qwb[:], T.qw[:]).then_inc(sem.lq, 16)
-    SY.dma_start(T.xb[:], T.x[:]).then_inc(sem.lx, 16)
+    S.wait_ge(sem.mf, 1)
+    S.dma_start(T.xb[:], T.x[:]).then_inc(sem.lx, 16)
 
-    V.memset(T.onf[:], 1.0).then_inc(sem.mf, 1)
+    V.memset(T.onb[:], 1.0).then_inc(sem.mf, 1)
     V.memset(T.eb[:], 0.0).then_inc(sem.me, 1)
-    V.memset(T.msk[:, 0:128], BIG).then_inc(sem.mk, 1)
-    V.wait_ge(sem.me, 1)
-    V.wait_ge(sem.gi, 1)
-    V.tensor_copy(T.eb[:, 4:516:4], T.idn[:]).then_inc(sem.me, 1)
-    V.wait_ge(sem.mk, 1)
-    V.memset(T.msk[:, 0:128:16], -BIG).then_inc(sem.mk, 1)
-    V.wait_ge(sem.me, 2)
+    V.memset(T.onf[:], 1.0).then_inc(sem.mf, 1)
+    V.memset(T.nb[:], 0.0).then_inc(sem.mt, 1)
+    V.wait_ge(sem.gt, 1)
+    V.tensor_scalar(T.pi[:, 4:5], T.pi[:, 0:1], 15, None, Op.bitwise_and).then_inc(sem.mu, 1)
     for b in range(4):
-        if b == 2:
+        if b == EQ[0]:
             V.wait_ge(sem.lq, 16)
             V.quantize_mx(Q[0], Q[1], T.qwb[:]).then_inc(sem.qq, 1)
+        if b == EQ[1]:
+            V.wait_ge(sem.lx, 16)
+            V.quantize_mx(T.XC[:], T.XS[:], T.xb[:]).then_inc(sem.qx, 1)
+        if b == 0:
+            V.wait_ge(sem.mu, 1)
+            V.tensor_copy(T.pm[:, 0:1], T.pi[:, 4:5]).then_inc(sem.mu, 1)
+        V.wait_ge(sem.me, 2)
         V.quantize_mx(col(T.EC, b, 128), col(T.ES, b, 128), T.eb[:, 4 - b:516 - b]).then_inc(sem.qe, 1)
-    V.wait_ge(sem.lx, 16)
-    V.quantize_mx(T.XC[:], T.XS[:], T.xb[:]).then_inc(sem.qx, 1)
-    V.memset(T.top[:], BIG).then_inc(sem.mt, 1)
-    V.memset(T.sc[:, 512:BATCH], 0.0).then_inc(sem.mt, 1)
     for b in range(4):
         V.wait_ge(sem["dm%d" % b], 1)
-        k = 512 * (b % 2)
-        V.tensor_tensor(T.rb[:, b:1024:4], T.xb[:, b:1024:4], T.psD[:, k:k + 256], Op.subtract).then_inc(sem["rs%d" % b], 1)
+        V.tensor_tensor(T.rb[:, b:1024:4], T.xb[:, b:1024:4], T.psD[:, 512 * b:512 * b + 256], Op.subtract).then_inc(sem["rs%d" % b], 1)
+    V.wait_ge(sem.sp, 6)
+    running(V, T, 0, bank(0, 256))
     for b in range(4):
         V.wait_ge(sem["rs%d" % b], 1)
-    V.quantize_mx(T.RC[:], T.RS[:], T.rb[:]).then_inc(sem.qr, 1)
-    V.tensor_reduce(T.uc[:, 0:1], T.idn[:, OWN:64:4], AxisListType.X, Op.add).then_inc(sem.mu, 1)
+
+    def residuals(h):
+        V.quantize_mx(col(T.RC, h, 128), col(T.RS, h, 128), col(T.rb, h, 512)).then_inc(sem.qr, 1)
+
+    if not FILL:
+        V.quantize_mx(T.RC[:], T.RS[:], T.rb[:]).then_inc(sem.qr, 2)
 
     PE.wait_ge(sem.qx, 1)
-    PE.wait_ge(sem.qe, 4)
     for b in range(4):
-        if b >= 2:
-            PE.wait_ge(sem["rs%d" % (b - 2)], 1)
-        k = 512 * (b % 2)
-        PE.matmul_mx(T.psD[:, k:k + 256], col(T.EC, b, 128), col(T.ES, b, 128), T.XC[:], T.XS[:], True, True).then_inc(sem["dm%d" % b], 1)
+        PE.wait_ge(sem.qe, b + 1)
+        PE.matmul_mx(T.psD[:, 512 * b:512 * b + 256], col(T.EC, b, 128), col(T.ES, b, 128), T.XC[:], T.XS[:], True, True).then_inc(sem["dm%d" % b], 1)
 
     def score(u):
-        h = u % 2
-        PE.matmul_mx(bank(h, 128), col(T.XC, h, 128), col(T.XS, h, 128), col(T.QC, u // 2, 128), col(T.QS, u // 2, 128), True, True).then_inc(sem["sm%d" % u], 1)
+        PE.matmul_mx(bank(u, 256), col(T.QC, u, 128), col(T.QS, u, 128), T.XC[:], T.XS[:], True, True).then_inc(sem["sm%d" % u], 1)
 
-    def groups(u):
-        h = u % 2
-        V.wait_ge(sem["sm%d" % u], 1)
-        V.tensor_tensor_scan(col(T.sc, 2 * h + u // 2, 128), T.msk[:, 0:128], bank(h, 128), -BIG, Op.min, Op.max).then_inc(sem["sn%d" % u], 1)
-
-    def spot(i):
-        return 512 * ((i + 1) % 2)
+    spots = [(T.psD, 512 * b + 256) for b in (0, 2, 3, 1, 0, 2)]
 
     def spread(i):
-        PE.wait_ge(*((sem["bcx%d" % i], 1) if i else (sem.cel0, 4)))
-        PE.transpose(T.psT[:, spot(i):spot(i) + 128], col(T.bc, i, 128) if i else T.run[:, 16:144], T.idn[:]).then_inc(sem["ctx%d" % i], 1)
+        t, a = spots[i]
+        PE.wait_ge(sem["bcx%d" % i], 1)
+        PE.transpose(t[:, a:a + 128], col(T.bc, i, 128), T.idn[:]).then_inc(sem["ctx%d" % i], 1)
 
-    def widen(j):
-        V.wait_ge(sem["n%d" % j], count(near))
-        V.tensor_scalar(col(T.bc, j + 1, 128), T.pq[:], T.nin[:, 4 + 4 * j:5 + 4 * j], None, Op.add).then_inc(sem["bcx%d" % (j + 1)], 1)
+    def widen(E, j):
+        E.wait_ge(sem["n%d" % j], E8 if j else 1)
+        out, number = col(T.bc, j, 128), T.nin[:, 4 * j:4 * j + 1]
+        (V.tensor_scalar(out, T.pq[:], number, None, Op.add) if E is V else S.activation(out, T.pq[:], Identity, bias=number)).then_inc(sem["bcx%d" % j], 1)
 
     def lists(j):
+        t, a = spots[j]
         V.wait_ge(sem["ctx%d" % j], 1)
-        if j:
-            V.tensor_scalar(col(T.off, j, 32), T.psT[:, spot(j) + 65:spot(j) + 128:2], 64.0, None, Op.mult).then_inc(sem["ofx%d" % j], 4)
+        if j in FOUR:
+            V.tensor_scalar(col(T.off, j, 32), t[:, a:a + 128:4], 64.0, None, Op.mult).then_inc(sem["ofx%d" % j], 4)
             return
         for e in range(4):
-            V.tensor_scalar(T.off[:, e:32:4], T.psT[:, spot(0) + 32 + OWN:spot(0) + 64:4], 64.0, 16.0 * e, Op.mult, Op.add).then_inc(sem.ofx0, 1)
+            V.tensor_scalar(T.off[:, 32 * j + e:32 * j + 32:4], t[:, a + 15:a + 128:16], 64.0, 16.0 * e - 60, Op.mult, Op.add).then_inc(sem["ofx%d" % j], 1)
+
+    def widen_pair(h):
+        V.wait_ge(sem["aw%d" % h], 2 * E8)
+        lo, hi = [T.adj[:, 4 * s:4 * s + 1] for s in whole[2 * h:2 * h + 2]]
+        V.tensor_scalar(col(T.bc, 4 + h, 128), T.side[:], hi, lo, Op.mult, Op.max).then_inc(sem["bcx%d" % (4 + h)], 1)
+
+    def short_lists(i):
+        t, a = spots[i]
+        V.wait_ge(sem["ctx%d" % i], 1)
+        for k in range(1 if i == 3 else 2):
+            V.tensor_scalar(col(T.offl, 0 if i == 3 else 2 * i - 7 + k, 8), t[:, a + (15 if i == 3 else 8 * k):a + 128:16], 16.0, T.pm[:, 2 * k:2 * k + 1],
+                            Op.mult, Op.add).then_inc(sem["ofx%d" % i], 1)
 
     calls = {}
 
@@ -278,225 +375,254 @@ def rank_program(g, core, T, topo):
             if name in calls:
                 V.wait_ge(sem[name], calls[name])
         a, n = 256 * j + 128 * parts[0], 128 * len(parts)
-        V.quantize_mx(T.OC[:, a:a + n], T.OS[:, a:a + n], T.hb[:, 4 * a:4 * (a + n)]).then_inc(sem["qz%d" % j], 1)
+        V.quantize_mx(T.OC[:, a:a + n], T.OS[:, a:a + n], T.hb[:, 4 * a:4 * (a + n)]).then_inc(sem["qz%d" % (2 * j + parts[0])], 1)
 
     every = [me] + whole
 
     def pick(E, i):
         E.wait_ge(sem["pc%d" % ((i + 1) // 2)], 1)
-        E.wait_ge(sem[("ol", "ofa", "ofx3")[(i + 1) // 2]], 1)
+        E.wait_ge(sem["ofx%d" % (3 + (i + 1) // 2)], 2 if i else 1)
         move(E, col(T.ysb, every[i], 128), col(T.pf, i, 256).indirect(col(T.offl, i, 8))).then_inc(sem["yg%d" % i], 1)
 
-    def full(i, b, part):
+    def full(i, b, part, first):
         c, p = ((T.FXC, T.FXS), (T.FRC, T.FRS))[part] if i else ((T.XC, T.XS), (T.RC, T.RS))[part]
         n = 512 if i else 256
         for f in range(2 * i - 2, 2 * i) if i else ():
-            PE.wait_ge(sem[("wx%d", "wr%d")[part] % f], (3 * E8, (2 + i) * E8 // 2)[part])
-        mm = PE.matmul_mx(bank(b, n), Q[0], Q[1], col(c, max(i - 1, 0), n), col(p, max(i - 1, 0), n), part == 0, part == 1)
-        if part:
+            PE.wait_ge(sem[("wx%d", "wr%d")[part] % f], len(PIECES) * E8 if PLAN else ((2 if f % 2 and f // 2 in VIA else 3) * E8, (2 + i + 2 * RB * (i - 1)) * E8 // 2)[part])
+        mm = PE.matmul_mx(bank(b, n), Q[0], Q[1], col(c, max(i - 1, 0), n), col(p, max(i - 1, 0), n), first, not first)
+        if not first:
             mm.then_inc(sem["pm%d" % i], 1)
 
     def keep(E, i, b):
         E.wait_ge(sem["pm%d" % i], 1)
         move(E, T.pf[:, 512 * i - 256:512 * i + 256] if i else T.pf[:, 0:256], bank(b, 512 if i else 256)).then_inc(sem["pc%d" % i], 1)
 
-    def product(j, b):
-        PE.wait_ge(sem["d%d" % j], 2 * E8)
-        for part in range(2):
-            mm = PE.matmul_mx(bank(b, 128), Q[0], Q[1], col(T.LC, 2 * j + part, 128), col(T.LS, 2 * j + part, 128), part == 0, part == 1)
-        mm.then_inc(sem["ym%d" % j], 1)
+    places = bank(2, 128), bank(3, 128), T.psD[:, 1536:1664]
 
-    def bring(E, j, b):
+    def product(j, part, first):
+        if first:
+            PE.wait_ge(sem["d%d" % (2 * j)], 2 * E8)
+        mm = PE.matmul_mx(places[j], Q[0], Q[1], col(T.LC, 2 * j + part, 128), col(T.LS, 2 * j + part, 128), first, not first)
+        if not first:
+            mm.then_inc(sem["ym%d" % j], 1)
+
+    def bring(E, j):
         E.wait_ge(sem["ym%d" % j], 1)
-        move(E, col(T.ysb, chosen[j], 128), bank(b, 128)).then_inc(sem["yc%d" % j], 1)
+        move(E, col(T.ysb, chosen[j], 128), places[j]).then_inc(sem["yc%d" % j], 1)
 
     def store(E, ready, s, done):
         for name in ready:
             E.wait_ge(sem[name], 1)
         E.dma_start(T.y[:, 128 * s:128 * (s + len(ready))], T.ysb[:, 128 * s:128 * (s + len(ready))]).then_inc(done, 16)
 
-    S.wait_ge(sem.mf, 1)
-    units = ((0, 1.0 / 16), (32, 1.0 / 64))
-    for lo, unit in units:
-        S.activation(T.inc[lo:lo + 32, 16:144], T.onf[lo:lo + 32, 0:128], Copy, scale=unit).then_inc(sem.si, 1)
-    S.activation(T.run[64:128, :], T.onf[64:128, :], Copy, scale=0.0).then_inc(sem.sp, 1)
-    S.activation(T.bc[64:128, 0:128], T.onf[64:128, 0:128], Copy, scale=0.0).then_inc(sem.sp, 1)
-    S.wait_ge(sem.si, 2)
-    for lo, unit in units:
-        S.activation(T.inc[lo:lo + 32, 32:144:16], T.onf[lo:lo + 32, 0:7], Copy, scale=-15 * unit).then_inc(sem.sp, 1)
-    S.activation(T.inc[0:64, 16:17], T.onf[0:64, 0:1], Copy, scale=0.0).then_inc(sem.sp, 1)
+    def numbers(E):
+        for h in range(2):
+            V.wait_ge(sem["aw%d" % h], 2 * E8)
+        V.wait_ge(sem.an, (2 if PLAN else 3) * E8)
+        V.wait_ge(sem.so, 1)
+        V.tensor_tensor(T.chs[:], T.nb[:, 0:64:8], T.adj[:, 0:32:4], Op.add).then_inc(sem.chv, 1)
+
+    steps = {"l": lambda E, j: lists(j), "w": widen, "g": gather, "s": lambda E, i: short_lists(i), "p": lambda E, j, *parts: pack(j, parts or (0, 1)),
+             "W": lambda E, h: widen_pair(h), "k": pick, "K": lambda E, i: keep(E, i, i - 1), "b": bring, "n": numbers}
+
+    S.wait_ge(sem.mf, 2)
+    S.activation(T.top[:, 0:128], T.onf[:], Copy, scale=BIG)
+    S.activation(T.top[:, 128:256], T.onf[:], Copy, scale=BIG).then_inc(sem.sp, 1)
+    S.activation(T.msk[:], T.onf[:, 0:32], Copy, scale=BIG).then_inc(sem.si, 1)
+    S.activation(T.adj[:, 4 * min(chosen[:2]):4 * min(chosen[:2]) + 5:4], T.onf[:, 0:2], Copy, scale=0.0).then_inc(sem.sp, 2)
+    S.wait_ge(sem.mt, 1)
+    for s in whole[1::2]:
+        S.activation(T.nb[:, 8 * s:8 * s + 1], T.onf[:, 0:1], Copy, scale=-MARK).then_inc(sem.sp, 1)
+    S.wait_ge(sem.si, 1)
+    S.activation(T.msk[:, 0:32:16], T.onf[:, 0:2], Copy, scale=-BIG).then_inc(sem.sp, 1)
+    S.wait_ge(sem.mu, 2)
+    S.activation(T.pm[:, 1:2], T.pm[:, 0:1], Copy, scale=1.0 / 16).then_inc(sem.si, 1)
+    S.activation(T.pm[:, 2:3], T.pm[:, 0:1], Identity, bias=-16 * MARK).then_inc(sem.sp, 1)
+    S.activation(T.side[:], T.onf[:, 0:128], Sign, scale=T.pm[:, 0:1], bias=-7.5).then_inc(sem.sp, 1)
     S.wait_ge(sem.gp, 1)
-    S.activation(T.pa[:], T.p16[:], Copy, scale=1.0 / 16).then_inc(sem.sp, 1)
-    S.wait_ge(sem.gi, 1)
-    for e in range(1, 4):
-        S.activation(T.ltb[:, 0:16], T.idn[:, 2 * e + 1:128:8], Copy, scale=0.25 * e, accum_out=T.uc[:, e:e + 1]).then_inc(sem.sg, 1)
-        S.wait_ge(sem.sg, e)
-    for e in range(2):
-        S.activation(T.uc[:, 4 + e:5 + e], T.uc[:, 1 + 3 * e:2 + 3 * e], Identity, bias=T.uc[:, 2 + e:3 + e]).then_inc(sem.sg, 1)
-        S.wait_ge(sem.sg, 4 + e)
-    S.activation(T.pq[:], T.p16[:], Identity, bias=T.uc[:, 5:6], scale=1.0 / 64).then_inc(sem.sp, 1)
-    at = {me: (OWN, 4), chosen[0]: (32 + OWN, 4), chosen[1]: (64 + ENDS[0], 8), chosen[2]: (64 + ENDS[1], 8)}
-    at.update({s: (32 * (f % 2) + BOTH[f // 2], 4) for f, s in enumerate(whole)})
-    S.wait_ge(sem.gt, 1)
-    for s, (first, step) in at.items():
-        S.activation(T.tq[:, s:128:8], T.two[:], Identity, bias=float(first), scale=float(step)).then_inc(sem.st, 1)
+    S.wait_ge(sem.si, 2)
+    S.activation(T.pq[:], T.p16[:], Identity, bias=T.pm[:, 1:2], scale=1.0 / 64).then_inc(sem.si, 1)
     for b in range(4):
         S.wait_ge(sem["rs%d" % b], 1)
     keep(S, 0, 2)
-    for j in range(3):
-        gather(S, j, 1, 0, 32)
-        gather(S, j, 0, SHARE[j], 32)
+    S.wait_ge(sem.si, 3)
+    S.wait_ge(sem.cel1, 4)
+    cell(S, T.td[:, 33:64:2], T.td[:, 63:64], T.lt[:, 0:16], T.adj[:, 4 * me:4 * me + 1], sem.so)
+    for k in range(2):
+        if k == OWNW:
+            S.wait_ge(sem.so, 1)
+            S.activation(col(T.bc, 3, 128), T.onf[:, 0:128], Copy, scale=T.adj[:, 4 * me:4 * me + 1]).then_inc(sem.bcx3, 1)
+        if k == 0:
+            S.wait_ge(sem.cel0, 4)
+            cell(S, T.td[:, 1:32:2], T.td[:, 31:32], T.lt[:, 16:32], T.nin[:, 0:1], sem.n0)
+    widen(S, 0)
+    S.activation(T.cnt[:, 0:1], T.nin[:, 0:1], Copy).then_inc(sem.sb, 1)
     pick(S, 0)
-    keep(S, 1, 0)
-    keep(S, 2, 1)
-    pick(S, 2)
-    pick(S, 4)
-    bring(S, 1, 3)
-    bring(S, 2, 0)
+    for name, *args in SSEQ:
+        steps[name](S, *args)
     store(S, ("yc2",), chosen[2], sem.yd)
     S.wait_ge(sem.yd, 16)
 
     PE.wait_ge(sem.qq, 1)
     score(0)
+    full(0, 2, 0, True)
+    PE.wait_ge(sem.hq0, E8 // 2 if SWAP else E8)
+    PE.wait_ge(sem.hp0, E8 // 2)
     score(1)
-    PE.wait_ge(sem.st, N)
-    PE.transpose(T.psT[:, 512:640], T.tq[:], T.idn[:]).then_inc(sem.tc, 1)
-    PE.wait_ge(sem.qm, E8)
-    PE.wait_ge(sem.hp, E8 // 2)
-    for h in range(2):
-        PE.wait_ge(sem["sn%d" % h], 1)
-        score(2 + h)
-    PE.wait_ge(sem.mt, 2)
-    PE.wait_ge(sem.sn2, 1)
-    PE.wait_ge(sem.sn3, 1)
-    k = 15 - 4 * OWN
-    PE.transpose(T.psT[:, 0:128], T.sc[:, k:k + 512:4], T.idn[:]).then_inc(sem.tr0, 1)
-    PE.wait_ge(sem.qr, 1)
-    full(0, 2, 0)
-    full(0, 2, 1)
-    PE.wait_ge(sem.oc, 1)
-    spread(0)
-    spread(1)
-    PE.wait_ge(sem.ol, 1)
+    PE.wait_ge(sem.qr, 2)
+    full(0, 2, 1, False)
+    PE.wait_ge(sem.gi, 1)
+    for i in (3, 0, 1, 2):
+        spread(i)
+    PE.wait_ge(sem.sn1, 1)
+    for i, part, first in FULL:
+        full(i, i - 1, part, first)
     PE.wait_ge(sem.ofx0, 4)
-    spread(2)
-    full(1, 0, 0)
-    full(1, 0, 1)
-    full(2, 1, 0)
-    full(2, 1, 1)
-    PE.wait_ge(sem.ofx2, 4)
-    PE.wait_ge(sem.bcx0, 2)
-    PE.transpose(T.psT[:, 512:640], col(T.bc, 0, 128), T.idn[:]).then_inc(sem.cta, 1)
+    spread(4)
     PE.wait_ge(sem.ofx1, 4)
-    spread(3)
-    product(1, 3)
+    spread(5)
     PE.wait_ge(sem.pc0, 1)
-    product(0, 2)
-    PE.wait_ge(sem.pc1, 1)
-    product(2, 0)
+    PE.wait_ge(sem.ofx2, 4)
+    for j in (1, 0, 2):
+        for part in range(2):
+            product(j, part, part == 0)
 
-    V.wait_ge(sem.mk, 2)
-    groups(0)
-    groups(1)
-    V.wait_ge(sem.tc, 1)
-    V.tensor_copy(T.offc[:], T.psT[:, 512:516]).then_inc(sem.oc, 1)
-    groups(2)
-    groups(3)
-    V.wait_ge(sem.mt, 2)
-    V.wait_ge(sem.mu, 1)
-    V.wait_ge(sem.sp, 7)
-    cells(V, T, 0, 0, T.uc[0:64, 0:1], T.inc[0:64, 0:16], T.run[0:64, :], T.inc[0:64, :], 144)
-    lists(0)
-    widen(0)
-    V.tensor_scalar(T.offl[:, 0:8], T.psT[:, spot(0) + OWN:spot(0) + 32:4], 16.0, None, Op.mult).then_inc(sem.ol, 1)
-    gather(V, 0, 0, 0, SHARE[0])
-    lists(1)
-    widen(1)
-    pack(0)
-    gather(V, 1, 0, 0, SHARE[1])
-    lists(2)
-    pack(1)
-    gather(V, 2, 0, 0, SHARE[2])
-    pack(2, (1,))
-    pack(2, (0,))
-    V.wait_ge(sem.aw0, 2 * E8)
-    for h in range(2):
-        lo = 32 * h
-        V.tensor_scalar(T.bc[lo:lo + 32, 0:128], T.pa[lo:lo + 32, :], number(4 + h, lo, lo + 32), None, Op.add).then_inc(sem.bcx0, 1)
-    V.wait_ge(sem.an, 3 * E8)
-    V.tensor_scalar(T.cc[64:128, 0:1], number(2, 64, 128), number(3, 64, 128), None, Op.add).then_inc(sem.tn, 1)
-    V.wait_ge(sem.aw1, 2 * E8)
-    for h, first in enumerate((T.run[0:32, 15:16], T.nin[32:64, 0:1])):
-        lo = 32 * h
-        V.tensor_scalar(T.cc[lo:lo + 32, 0:1], first, number(4 + h, lo, lo + 32), number(6 + h, lo, lo + 32), Op.add, Op.add).then_inc(sem.tn, 1)
-    V.wait_ge(sem.tn, 3)
-    V.tensor_scalar(col(T.bc, 3, 128), T.pa[:], T.cc[:, 0:1], None, Op.add).then_inc(sem.bcx3, 1)
-    V.wait_ge(sem.cta, 1)
-    V.tensor_scalar(T.offl[:, 8:24], T.psT[:, 512 + BOTH[0]:512 + 64:4], 16.0, None, Op.mult).then_inc(sem.ofa, 1)
-    pick(V, 1)
-    V.wait_ge(sem.ctx3, 1)
-    V.tensor_scalar(T.offl[:, 24:40], T.psT[:, spot(3) + BOTH[1]:spot(3) + 64:4], 16.0, None, Op.mult).then_inc(sem.ofx3, 1)
-    pick(V, 3)
-    bring(V, 0, 2)
-    V.tensor_copy(T.chf[:], T.psT[:, spot(3):spot(3) + 128]).then_inc(sem.chv, 1)
-    V.wait_ge(sem.chv, 1)
-    V.tensor_copy(T.chg[:], T.chf[:, 0:128].indirect(T.offc[:, 0:4])).then_inc(sem.chv, 1)
+    V.wait_ge(sem.mt, 1)
+    own = group_steps(V, T, 1, T.rm[:, 7:256:8], ["sn0"], False)
+    asked = [lambda: running(V, T, 1, bank(1, 256))] + group_steps(V, T, 0, T.rm[:, 256 + 7:512:8], ["sn1"], 0 in FOUR)
+    for k, step in enumerate(asked):
+        for mine in own[k + LEAD:k + LEAD + 1] if k else own[:LEAD + 1]:
+            mine()
+        step()
+    V.wait_ge(sem.sp, 8)
+    V.wait_ge(sem.si, 3)
+    short_lists(3)
+    for name, *args in VSEQ:
+        if DELAY and (name, *args) == ("l", 2):
+            V.wait_ge(sem.ctx2, 1)
+            V.memset(T.dly[:], 0.0)
+        steps[name](V, *args)
 
-    SY.wait_ge(sem.cta, 1)
+    if not EARLY:
+        SY.wait_ge(sem.ctx4, 1)
     store(SY, ("yg0",), me, sem.ye)
+    SY.wait_ge(sem.chv, 1)
+    SY.dma_start(T.ch[:], T.chs[15:128:16, :]).then_inc(sem.ye, 16)
     store(SY, ("yg1", "yg2"), min(whole[:2]), sem.ye)
     store(SY, ("yg3", "yg4"), min(whole[2:]), sem.ye)
-    store(SY, ("yc0", "yc1"), min(chosen[:2]), sem.ye)
-    SY.wait_ge(sem.chv, 2)
-    SY.dma_start(T.ch[:], T.chg[0:1, :]).then_inc(sem.ye, 16)
-    SY.wait_ge(sem.ye, 16 * 5)
+    store(SY, ("yc1",), chosen[1], sem.ye)
+    store(SY, ("yc0",), chosen[0], sem.ye)
+    SY.wait_ge(sem.ye, 16 * 6)
 
     tr, post, finish = writer(g, core, T, topo)
+    g.iota(T.pi[:, 0:1], [[0, 1]], 0, 1).then_inc(sem.gt, 1)
     g.wait_ge(sem.mf, 1)
-    g.affine_select(T.idn[:], T.onf[:, 0:128], [[-1, 128]], Op.is_equal, 0.0, 0, 1).then_inc(sem.gi, 1)
-    g.iota(T.p16[:], [[0, 8], [1, 16]], 0, 0, allow_small_or_imprecise_dtypes=True).then_inc(sem.gp, 1)
-    g.iota(T.two[:], [[0, 8], [1, 2]], 0, 2, allow_small_or_imprecise_dtypes=True).then_inc(sem.gt, 1)
+    g.wait_ge(sem.me, 1)
+    g.affine_select(T.eb[:, 4:516:4], T.onb[:], [[-1, 128]], Op.is_equal, 0.0, 0, 1).then_inc(sem.me, 1)
 
-    def pair(codes, plane, dsts, land, mask, names):
-        post(tr(plane, [(c, land[1]) for c in dsts], mask, sem[names[1]]))
-        post(tr(raw(codes), [(c, raw(land[0])) for c in dsts], mask, sem[names[0]]))
+
+    def pair(codes, plane, dst, land, mask, names):
+        post(tr(plane, [(dst, land[1])], mask, names[1]))
+        post(tr(raw(codes), [(dst, raw(land[0]))], mask, names[0]))
 
     def slot(k):
         return col(T.HQC, k, 128), col(T.HQS, k, 128)
 
-    scorers = [plans[chosen[1 + i]]["out"][i] for i in range(2)]
+    scorers = [plans[chosen[1 + i]]["out"][0 if PLAN else i] for i in range(2)]
     g.wait_ge(sem.qq, 1)
-    bits = [1 << e for e in topo.engines(core, scorers[0])]
-    post(tr(raw(Q[0]), [(scorers[0], raw(slot(2)[0]))], sum(bits[0::2]), sem.hq))
-    post(tr(Q[1], [(scorers[0], slot(2)[1]), (cores[chosen[0]], col(T.QS, 1, 128))], sum(bits[1::2]), sem.hp))
-    post(tr(raw(Q[0]), [(cores[chosen[0]], raw(col(T.QC, 1, 128)))], far, sem.qm))
+    first = [(scorers[0], slot(0 if PLAN else 2)), (cores[chosen[0]], (col(T.QC, 1, 128), col(T.QS, 1, 128)))][::-1 if SWAP else 1]
+    post(tr(raw(Q[0]), [(first[0][0], raw(first[0][1][0]))], every_other(far), "hq0"))
+    post(tr(Q[1], [(c, land[1]) for c, land in first], every_other(far, 1), "hp0"), *([tr(Q[1], [(plan["inb"] if QP else plan["out"][0], slot(0)[1])], near, "hw")] if QP or QH else []))
+    post(tr(raw(Q[0]), [(first[1][0], raw(first[1][1][0]))], far, "hq0"))
     g.wait_ge(sem.qx, 1)
-    pair(T.XC[:], T.XS[:], plan["out"][:1], (T.HXC[:], T.HXS[:]), near, ("hxc", "hxs"))
-    pair(Q[0], Q[1], scorers[1:], slot(1), far, ("hq", "hp"))
-    post(tr(T.XS[:], [(plan["out"][1], T.HXS[:])], near, sem.hxs))
-    post(tr(Q[1], [(plan["out"][0], slot(0)[1])], near, sem.hw))
-    post(tr(raw(T.XC[:]), [(plan["out"][1], raw(T.HXC[:]))], near, sem.hxc))
-    post(tr(raw(Q[0]), [(h, raw(slot(0)[0])) for h in plan["out"]], near, sem.ho))
-    g.wait_ge(sem.qr, 1)
-    for i, r in enumerate(plan["to"]):
-        pair(T.RC[:], T.RS[:], [plans[r]["inb"]], (col(T.HRC, i, 256), col(T.HRS, i, 256)), far, ("hrc%d" % i, "hrs%d" % i))
-    g.wait_ge(sem.cel0, 4)
-    post(tr(T.run[:, 15:16], [(cores[chosen[0]], T.nin[:, 0:1])], far, sem.an))
+    pair(T.XC[:], T.XS[:], plan["out"][0], (T.HXC[:], T.HXS[:]), near, ("hxc", "hxs"))
+    if PLAN == 0:
+        if QP:
+            post(tr(raw(Q[0]), [(scorers[1], raw(slot(1)[0]))], far, "hq0"))
+        else:
+            pair(Q[0], Q[1], scorers[1], slot(1), far, ("hq0", "hp0"))
+        post(tr(T.XS[:], [(plan["out"][1], T.HXS[:])], near, "hxs"))
+        if not XO:
+            post(tr(Q[1], [(plan["out"][0], slot(0)[1])], near, "hw"))
+        post(tr(raw(T.XC[:]), [(plan["out"][1], raw(T.HXC[:]))], near, "hxc"))
+        if QD == 2:
+            for name, src, land in (("hw", Q[1], slot(0)[1]), ("ho", raw(Q[0]), raw(slot(0)[0]))):
+                post(*[tr(src, [(h, land)], mask, name) for h, mask in zip(plan["out"], (near, far))])
+        else:
+            if XO and not QP and not QH:
+                post(tr(Q[1], [(h, slot(0)[1]) for h in plan["out"][:1 + QD]], near, "hw"))
+            post(tr(raw(Q[0]), [(h, raw(slot(0)[0])) for h in plan["out"]], near, "ho"))
+        g.wait_ge(sem.mf, 2)
+        g.iota(T.p16[:], [[0, 8], [1, 16]], 0, 0, allow_small_or_imprecise_dtypes=True).then_inc(sem.gp, 1)
+        g.affine_select(T.idn[:], T.onf[:], [[-1, 128]], Op.is_equal, 0.0, 0, 1).then_inc(sem.gi, 1)
+        g.wait_ge(sem.qr, 2)
+        for i, r in enumerate(plan["to"]):
+            if i and RB:
+                post(tr(T.RS[:], [(plans[r]["inb"], col(T.HRS, 1, 256))], far, "hrs1"))
+                for h, c in enumerate((plans[r]["inb"], plans[r]["out"][1])):
+                    post(tr(raw(col(T.RC, h, 128)), [(c, raw(col(T.HRC, 2 + h, 128)))], far, "hrc1"))
+                continue
+            pair(T.RC[:], T.RS[:], plans[r]["inb"], (col(T.HRC, i, 256), col(T.HRS, i, 256)), far, ("hrc%d" % i, "hrs%d" % i))
+    else:
+        for k, name, see in ((1, "hp", same), (0, "hq", raw)):
+            post(tr(see(Q[k]), [(scorers[1], see(slot(1)[k]))], far, name + "1"), tr(see(Q[k]), [(plan["passers"][0], see(slot(0)[k]))], near, name + "0"))
+        on = plans[plan["to"][0]]["passers"][0]
+        for name, src, land in zip(PIECES, pieces(T.XC, T.XS, 0), pieces(T.HYC, T.HYS, 0)):
+            post(tr(src, [(on, land)], far, name + "0"))
+        g.wait_ge(sem.qr, 2)
+        for name, src, land, here, home in zip(PIECES, pieces(T.RC, T.RS, 0), pieces(T.HYC, T.HYS, 1), pieces(T.HRC, T.HRS, 0), ("hrs0", "hrc0")):
+            post(tr(src, [(on, land)], far, name + "1"), tr(src, [(plan["scorer"], here)], near, home))
+    g.wait_ge(sem.sb, 1)
+    if ANVIA:
+        post(tr(T.cnt[:, 0:1], [(plan["inb"], T.cnt[:, 0:1])], near, "an"))
+    else:
+        post(tr(T.cnt[:, 0:1], [(cores[chosen[0]], T.nb[:, 8 * me:8 * me + 1])], far, "an"))
     g.wait_ge(sem.qz0, 1)
-    pair(col(T.OC, 0, 256), col(T.OS, 0, 256), plan["out"][:1], (T.HZC[:], T.HZS[:]), near | far, ("hzc", "hzs"))
+    pair(col(T.OC, 0, 256), col(T.OS, 0, 256), plan["scorer"], (T.HZC[:], T.HZS[:]), near | far if B0ALL else near, ("hzc", "hzs"))
     for j in (1, 2):
-        g.wait_ge(sem["qz%d" % j], j)
-        pair(col(T.OC, j, 256), col(T.OS, j, 256), [cores[chosen[j]]], (col(T.LC, j, 256), col(T.LS, j, 256)), far, ("d%d" % j,) * 2)
+        g.wait_ge(sem["qz%d" % (2 * j)], 1)
+        if j == 2:
+            g.wait_ge(sem.qz5, 1)
+        if j == 1 and B1P:
+            post(tr(col(T.OS, 1, 256), [(plan["out"][1], T.HZS[:])], near, "hzs"))
+            post(tr(raw(col(T.OC, 1, 256)), [(cores[chosen[1]], raw(col(T.LC, 1, 256)))], far, "d2"))
+            continue
+        if j == 1 and B1VIA:
+            pair(col(T.OC, 1, 256), col(T.OS, 1, 256), plan["out"][1], (T.HZC[:], T.HZS[:]), near | far, ("hzc", "hzs"))
+            continue
+        post(tr(raw(col(T.OC, j, 256)), [(cores[chosen[j]], raw(col(T.LC, j, 256)))], far, "d%d" % (2 * j)))
+        post(tr(col(T.OS, j, 256), [(cores[chosen[j]], col(T.LS, j, 256))], far, "d%d" % (2 * j)))
     finish()
 
 
-def hand_on(g, T, tr, post, wait, src, land, see, name, i, home, mate, near, far):
-    g.wait_ge(T.sem[wait], count(far))
-    post(tr(see(src), [(home, see(col(land, 2 * i, 256)))], near, T.sem[name + str(2 * i)]),
-         tr(see(src), [(mate, see(col(land, 2 * i + 1, 256)))], far, T.sem[name + str(2 * i + 1)]))
+def helper_constants(V, T):
+    V.memset(T.top[:], BIG).then_inc(T.sem.mt, 1)
+    V.memset(T.msk[:], BIG).then_inc(T.sem.mk, 1)
+    for h in range(2):
+        V.memset(T.offd[:, h:h + 1], 16 * h + 15).then_inc(T.sem.mt, 1)
+    V.wait_ge(T.sem.mk, 1)
+    V.memset(T.msk[:, 0:32:16], -BIG).then_inc(T.sem.mt, 1)
+    V.wait_ge(T.sem.mt, 4)
 
 
-def scorer_program(g, core, me, T, topo):
+def hand_on(g, T, tr, post, wait, src, here, there, name, i, home, mate, near, far):
+    g.wait_ge(T.sem[wait[0]], wait[1])
+    post(*[tr(src, [(c, land)], mask, name + str(f)) for c, land, mask, f in ((home, here, near, 2 * i), (mate, there, far, 2 * i + 1)) if mask])
+
+
+def spare_program(g, core, me, T, topo):
+    plan = make_plan(me, T, topo)
+    tr, post, finish = writer(g, core, T, topo)
+    i = VIA[0]
+    to = T.cores[make_plan(plan["to"][i], T, topo)["mate"]]
+    far = topo.mask(core, to)
+    for name, src, land, see in (("hys0", T.HYS, T.FXS, same), ("hya0", T.HYC, T.FXC, raw)):
+        g.wait_ge(T.sem[name], count(far))
+        post(tr(see(col(src, 0, 256)), [(to, see(col(land, 2 * i + 1, 256)))], far, "wx%d" % (2 * i + 1)))
+    finish()
+
+
+def helper_program(g, core, me, T, topo):
     plans = [make_plan(r, T, topo) for r in range(N)]
     plan = plans[me]
     cores, sem = T.cores, T.sem
@@ -505,117 +631,241 @@ def scorer_program(g, core, me, T, topo):
     V, S, PE = g.vector, g.scalar, g.tensor
     tr, post, finish = writer(g, core, T, topo)
     home, mate, on = cores[me], cores[plan["mate"]], plans[plan["to"][i]]["out"][i]
-    far = topo.mask(core, mate)
-    near = topo.mask(core, home) & ~far
+    far, near = engines(core, home, plan, T, topo)
     E8 = count(far)
-    items = ((T.HXC, T.HXS), (T.HYC, T.HYS))
-    asked = ((128 * (2 - i), 128), (0, 256))
-    ends = ((64 + ENDS[i], 128, 8), (BOTH[i], 64, 4))
+    V.memset(T.td[:, 32:32 + int(MARK)], -BIG).then_inc(sem.mf, 1)
+    helper_constants(V, T)
 
-    V.memset(T.onf[:], 1.0).then_inc(sem.mf, 1)
-    V.memset(T.msk[:], BIG).then_inc(sem.mk, 1)
-    V.memset(T.top[:], BIG).then_inc(sem.mt, 1)
-    V.memset(T.cnt[:], 0.0).then_inc(sem.mt, 1)
-    V.memset(T.cc[:], 0.0).then_inc(sem.mt, 1)
-    for bt in range(2):
-        k = BATCH * bt + 2 * asked[bt][1]
-        V.memset(T.sc[:, k:k + 16], 0.0).then_inc(sem.mt, 1)
-    V.wait_ge(sem.mk, 1)
-    V.memset(T.msk[:, 0:256:16], -BIG).then_inc(sem.mk, 1)
-    V.wait_ge(sem.gi, 1)
-    for bt in range(2):
-        V.tensor_reduce(T.uc[:, bt:bt + 1], T.idn[:, ends[bt][0]:ends[bt][1]:ends[bt][2]], AxisListType.X, Op.add).then_inc(sem.mu, 1)
-    V.wait_ge(sem.mk, 2)
-    V.wait_ge(sem.mt, 5)
-    V.wait_ge(sem.mu, 2)
-    V.wait_ge(sem.mf, 1)
-    PE.wait_ge(sem.gi, 1)
-    PE.wait_ge(sem.mt, 5)
-    for bt in range(2):
-        a, n = asked[bt]
-        for name, halves in ((("hxc", 2), ("hxs", 2), ("hq", 1 + i), ("hp", 1 + i)), (("hya", 2), ("hys", 2), ("ho", 2), ("hw", 2), ("hm", 4 - 4 * i)))[bt]:
-            if halves:
-                PE.wait_ge(sem[name], halves * E8 // 2)
-        for h in range(2):
-            u, k = 2 * bt + h, BATCH * bt + n * h
-            if bt and h:
-                PE.wait_ge(sem.hyc, E8)
-            PE.matmul_mx(T.psP[:, 512 * u:512 * u + n], col(items[bt][0], h, 128), col(items[bt][1], h, 128),
-                         T.HQC[:, a:a + n], T.HQS[:, a:a + n], True, True).then_inc(sem["sm%d" % u], 1)
-            V.wait_ge(sem["sm%d" % u], 1)
-            V.tensor_tensor_scan(T.sc[:, k:k + n], T.msk[:, 0:n], T.psP[:, 512 * u:512 * u + n], -BIG, Op.min, Op.max).then_inc(sem["sn%d" % u], 1)
-        step = n // 64
-        k = BATCH + 15 - step * BOTH[i] if bt else 1
-        PE.wait_ge(sem["sn%d" % (2 * bt)], 1)
-        PE.wait_ge(sem["sn%d" % (2 * bt + 1)], 1)
-        if not bt:
-            for E, places in ((V, (3, 7)), (S, (11,))):
-                E.wait_ge(sem.sn0, 1)
-                E.wait_ge(sem.sn1, 1)
-                for c in places:
-                    out, src = T.sc[:, c:256:16], T.sc[:, 15:256:16]
-                    (V.tensor_copy(out, src) if E is V else S.activation(out, src, ActivationFunctionType.Copy)).then_inc(sem.tn, 1)
-            PE.wait_ge(sem.tn, 3)
-        PE.transpose(T.psT[:, 512 * bt:512 * bt + 128], T.sc[:, k:k + 2 * n:step], T.idn[:]).then_inc(sem["tr%d" % bt], 1)
-        if bt:
-            cells(V, T, 1, 0, T.uc[0:64, 1:2], T.ltb[0:64, 16:32], T.cnt[0:64, 16:32], T.ltb[0:64, 16:32], 16)
-        else:
-            cell_ends, last = running(V, T, 0, 64)
-            S.wait_ge(sem.cel0, 2)
-            S.activation(T.ltb[64:128, 0:16], cell_ends, ActivationFunctionType.Sign, bias=last, scale=-1.0,
-                         accum_out=T.cc[64:128, 0:1]).then_inc(sem.sg, 1)
-            S.wait_ge(sem.sg, 1)
-            S.wait_ge(sem.mu, 2)
-            S.activation(T.cnt[64:128, 15:16], T.cc[64:128, 0:1], ActivationFunctionType.Copy, scale=T.uc[64:128, 0:1]).then_inc(sem.sg, 1)
+    def score(u, a, c, p):
+        PE.matmul_mx(T.psP[:, 512 * u:512 * u + 256], col(T.HQC, a, 128), col(T.HQS, a, 128), c[:, 0:256], p[:, 0:256], True, True).then_inc(sem["sm%d" % u], 1)
+        running(V, T, u, T.psP[:, 512 * u:512 * u + 256])
 
-    g.wait_ge(sem.mf, 1)
-    g.affine_select(T.idn[:], T.onf[:, 0:128], [[-1, 128]], Op.is_equal, 0.0, 0, 1).then_inc(sem.gi, 1)
+    for name, halves in (("hxc", 2), ("hxs", 2), ("hq0", 2 if SWAP else 1 + i), ("hp0", 1 + i)):
+        PE.wait_ge(sem[name], halves * E8 // 2)
+    score(2, 2 - i, T.HXC, T.HXS)
+    V.wait_ge(sem.sn2, 1)
+    by_group(V, T, 2, T.rm[:, 512 + 7:768:8], None, 1 + i in FOUR)
+    S.wait_ge(sem.cel2, 4)
+    cell(S, T.td[:, 65:96:2], T.td[:, 95:96], col(T.lt, 3, 16), T.nin[:, 0:1], sem.n0)
+    if i == 0:
+        S.wait_ge(sem.n0, 1)
+        S.activation(T.cnt[:, 0:1], T.nin[:, 0:1], ActivationFunctionType.Copy).then_inc(sem.sb, 1)
+    for h, a in UNITS[i]:
+        for name, n in (("hys0", 1), (("hya0", "hyb0")[h], 1)) + ((("hm", 2 - 2 * i),) if a else (("ho", 1), ("hw", 1))):
+            if n:
+                PE.wait_ge(sem[name], n * E8)
+        if True:
+            out, k = T.psD[:, 512 * (2 * h + a):512 * (2 * h + a) + 128], 256 * a + 128 * h
+            PE.matmul_mx(out, col(T.HQC, a, 128), col(T.HQS, a, 128), col(T.HYC, h, 128), col(T.HYS, h, 128), True, True).then_inc(sem["sm%d" % a], 1)
+            V.wait_ge(sem["sm%d" % a], h + 1)
+            if h:
+                V.wait_ge(sem["sn%d" % a], 1)
+            V.tensor_tensor_scan(T.rm[:, k:k + 128], T.top[:, 0:128], out, T.rm[:, k - 1:k] if h else -BIG, Op.min, Op.max).then_inc(sem["sn%d" % a], 1)
+    V.wait_ge(sem.sn0, 2)
+    V.wait_ge(sem.sn1, 2)
+    by_group(V, T, 0, T.rm[:, 15:512:16])
+    S.wait_ge(sem.cel0, 4)
+    S.wait_ge(sem.mf, 1)
+    for a in range(2):
+        n = 16 + a * int(MARK)
+        cell(S, T.td[:, 16 * a:16 * a + n], T.td[:, 16 * a + 15:16 * a + 16], T.lt[:, 16 * a:16 * a + n], T.nin[:, 4 + 4 * a:5 + 4 * a], sem.so)
+
+    ons = [on] + ([plan["spare"]] if i in VIA else [])
+    if QH == 2 and i == 0:
+        g.wait_ge(sem.hw, E8)
+        post(tr(col(T.HQS, 0, 128), [(plan["out"][1], col(T.HQS, 0, 128))], near, "hw"))
     g.wait_ge(sem.hxs, E8)
-    post(tr(T.HXS[:], [(on, T.HYS[:])], far, sem.hys))
+    post(tr(T.HXS[:], [(c, col(T.HYS, 0, 256)) for c in ons], far, "hys0"))
     if i == 1:
-        g.wait_ge(sem.hp, E8)
-        post(tr(col(T.HQS, 1, 128), [(plan["out"][0], col(T.HQS, 1, 128))], near, sem.hm))
+        g.wait_ge(sem.hp0, E8)
+        post(tr(col(T.HQS, 1, 128), [(plan["out"][0], col(T.HQS, 1, 128))], near, "hm"))
     g.wait_ge(sem.hxc, E8)
     for h in range(2):
-        post(tr(raw(col(T.HXC, h, 128)), [(on, raw(col(T.HYC, h, 128)))], far, sem[("hya", "hyc")[h]]))
+        more = []
+        if SPLIT and (i, h) == (1, 0):
+            continue
+        if i == 1 and h == HM:
+            g.wait_ge(sem.hq0, E8)
+            more = [tr(raw(col(T.HQC, 1, 128)), [(plan["out"][0], raw(col(T.HQC, 1, 128)))], near, "hm")]
+        post(tr(raw(col(T.HXC, h, 128)), [(on, raw(col(T.HYC, h, 128)))], far, ("hya0", "hyb0")[h]), *more)
+    if SPLIT and i == 0:
+        post(tr(raw(col(T.HXC, 0, 128)), [(plans[plan["to"][1]]["out"][1], raw(col(T.HYC, 0, 128)))], far, "hya0"))
+    for c in ons[1:]:
+        post(tr(raw(T.HXC[:]), [(c, raw(col(T.HYC, 0, 256)))], far, "hya0"))
     if i == 1:
-        g.wait_ge(sem.hq, E8)
-        post(tr(raw(col(T.HQC, 1, 128)), [(plan["out"][0], raw(col(T.HQC, 1, 128)))], near, sem.hm))
-    else:
+        if HM == 2:
+            g.wait_ge(sem.hq0, E8)
+            post(tr(raw(col(T.HQC, 1, 128)), [(plan["out"][0], raw(col(T.HQC, 1, 128)))], near, "hm"))
+    elif QP == 1:
         g.wait_ge(sem.hw, E8)
-        post(tr(col(T.HQS, 0, 128), [(plan["out"][1], col(T.HQS, 0, 128))], near, sem.hw))
-    g.wait_ge(sem.sg, 1)
-    post(tr(T.cc[:, 0:1], [(home, T.nin[:, 4 + 4 * i:5 + 4 * i])], near, sem["n%d" % i]))
-    g.wait_ge(sem.sg, 2)
-    post(tr(T.cnt[:, 15:16], [(cores[plan["chosen"][1 + i]], T.nib[:, 16 + 8 * i:17 + 8 * i])], far, sem.an))
-    hand_on(g, T, tr, post, "hys", T.HYS[:], T.FXS, same, "wx", i, home, mate, near, far)
-    for h in range(2):
-        g.wait_ge(sem[("hya", "hyc")[h]], E8)
-        post(tr(raw(col(T.HYC, h, 128)), [(home, raw(col(T.FXC, 4 * i + h, 128)))], near, sem["wx%d" % (2 * i)]),
-             tr(raw(col(T.HYC, h, 128)), [(mate, raw(col(T.FXC, 4 * i + 2 + h, 128)))], far, sem["wx%d" % (2 * i + 1)]))
-    g.wait_ge(sem.cel1, 4)
-    post(*[tr(T.cnt[:, 31:32], [(c, T.nib[:, 8 * k:8 * k + 1])], mask, sem["aw%d" % i])
-           for c, k, mask in ((home, 4 + 2 * i, near), (mate, 5 + 2 * i, far))])
+        post(tr(col(T.HQS, 0, 128), [(plan["out"][1], col(T.HQS, 0, 128))], near, "hw"))
+    elif QD == 0 and not QP and QH < 2:
+        g.wait_ge(sem.hw, E8)
+        post(tr(col(T.HQS, 0, 128), [(plan["out"][1], col(T.HQS, 0, 128))], near, "hw"))
+    for k in range(4):
+        if k == PRE[i]:
+            g.wait_ge(sem.n0, 1)
+            post(tr(T.nin[:, 0:1], [(home, T.nin[:, 4 + 4 * i:5 + 4 * i])], near, "n%d" % (1 + i)),
+                 *[tr(T.nin[:, 0:1], [(cores[plan["chosen"][2]], T.adj[:, 4 * me:4 * me + 1])], far, "an") for once in range(i)])
+        if k == 0:
+            hand_on(g, T, tr, post, ("hys0", E8), col(T.HYS, 0, 256), col(T.FXS, 2 * i, 256), col(T.FXS, 2 * i + 1, 256), "wx", i, home, mate, near, 0 if i in VIA else far)
+        elif k < 3:
+            h = k - 1
+            hand_on(g, T, tr, post, (("hya0", "hyb0")[h], E8), raw(col(T.HYC, h, 128)), raw(col(T.FXC, 4 * i + h, 128)), raw(col(T.FXC, 4 * i + 2 + h, 128)),
+                    "wx", i, home, mate, near, 0 if i in VIA else far)
+    if i == 1 and RB:
+        hand_on(g, T, tr, post, ("hrc1", E8), raw(col(T.HRC, 3, 128)), raw(col(T.FRC, 5, 128)), raw(col(T.FRC, 7, 128)), "wr", 1, home, mate, near, far)
+    s = plan["whole"][2 * i]
     if i == 0:
+        g.wait_ge(sem.sb, 1)
+        post(tr(T.cnt[:, 0:1], [(cores[plan["chosen"][1]], T.nb[:, 8 * me:8 * me + 1])], far, "an"))
+    g.wait_ge(sem.so, 2)
+    post(*[tr(T.nin[:, 4 + 4 * a:5 + 4 * a], [(c, T.adj[:, 4 * s:4 * s + 1])], mask, "aw%d" % i)
+           for a, (c, mask) in enumerate(((home, near), (mate, far)))])
+    if i == 1 and B1P:
+        g.wait_ge(sem.hzs, E8)
+        post(tr(T.HZS[:], [(cores[plan["chosen"][1]], col(T.LS, 1, 256))], far, "d2"))
+    if i == 0 or B1VIA:
         for wait, src, land, see in (("hzs", T.HZS, T.LS, same), ("hzc", T.HZC, T.LC, raw)):
-            g.wait_ge(sem[wait], count(near | far))
-            post(tr(see(src[:]), [(cores[plan["chosen"][0]], see(col(land, 0, 256)))], far, sem.d0))
+            g.wait_ge(sem[wait], count(near | far) if B0ALL else E8)
+            post(tr(see(src[:]), [(cores[plan["chosen"][i]], see(col(land, i, 256)))], far, "d%d" % (2 * i)))
     finish()
 
 
 def relay_program(g, core, me, T, topo):
     plan = make_plan(me, T, topo)
-    cores = T.cores
     tr, post, finish = writer(g, core, T, topo)
-    home, mate = cores[me], cores[plan["mate"]]
-    far = topo.mask(core, mate)
-    near = topo.mask(core, home) & ~far
+    home, mate = T.cores[me], T.cores[plan["mate"]]
+    far, near = engines(core, home, plan, T, topo)
+    if QP:
+        g.wait_ge(T.sem.hw, count(near))
+        post(tr(col(T.HQS, 0, 128), [(make_plan(plan["mate"], T, topo)["out"][1], col(T.HQS, 1, 128))], far, "hp0"),
+             tr(col(T.HQS, 0, 128), [(h, col(T.HQS, 0, 128)) for h in plan["out"][:QP]], near, "hw"))
     for i in range(2):
         for wait, src, land, see in (("hrs", T.HRS, T.FRS, same), ("hrc", T.HRC, T.FRC, raw)):
-            if (i, wait) == (0, "hrs"):
-                g.wait_ge(T.sem.hrs0, count(far))
-                post(tr(col(src, 0, 256), [(home, col(land, 0, 256))], every_other(near), T.sem.wr0),
-                     tr(col(src, 0, 256), [(mate, col(land, 1, 256))], every_other(far), T.sem.wr1))
-            else:
-                hand_on(g, T, tr, post, wait + str(i), col(src, i, 256), land, see, "wr", i, home, mate, near, far)
+            masks = (every_other(near), every_other(far)) if (i, wait) == (0, "hrs") else (near, far)
+            if HOLD == 1 and (i, wait) == (1, "hrc"):
+                g.wait_ge(T.sem.hrc1, count(far))
+                g.iota(T.dly[:, 0:400], [[1, 400]], 0, 0, allow_small_or_imprecise_dtypes=True)
+            if RB and (i, wait) == (1, "hrc"):
+                hand_on(g, T, tr, post, ("hrc1", count(far)), raw(col(src, 2, 128)), raw(col(land, 4, 128)), raw(col(land, 6, 128)), "wr", i, home, mate, *masks)
+                continue
+            hand_on(g, T, tr, post, (wait + str(i), count(far)), see(col(src, i, 256)), see(col(land, 2 * i, 256)), see(col(land, 2 * i + 1, 256)), "wr", i, home, mate, *masks)
+    if ANVIA:
+        g.wait_ge(T.sem.an, count(near))
+        post(tr(T.cnt[:, 0:1], [(T.cores[plan["chosen"][0]], T.nb[:, 8 * me:8 * me + 1])], far, "an"))
+    finish()
+
+
+def scorer_program(g, core, me, T, topo):
+    plans = [make_plan(r, T, topo) for r in range(N)]
+    plan = plans[me]
+    cores, sem = T.cores, T.sem
+    V, S, PE = g.vector, g.scalar, g.tensor
+    tr, post, finish = writer(g, core, T, topo)
+    far, near = engines(core, plan["home"], plan, T, topo)
+    E8 = count(far)
+    helper_constants(V, T)
+    PE.wait_ge(sem.hxc, E8)
+    PE.wait_ge(sem.hxs, E8)
+    chains = []
+    for u in range(2):
+        PE.wait_ge(sem["hq%d" % u], E8 if SWAP else (1 + u) * E8 // 2)
+        PE.wait_ge(sem["hp%d" % u], (1 + u) * E8 // 2)
+        PE.matmul_mx(T.psP[:, 512 * u:512 * u + 256], col(T.HQC, u, 128), col(T.HQS, u, 128), T.HXC[:], T.HXS[:], True, True).then_inc(sem["sm%d" % u], 1)
+        chains.append([lambda u=u: running(V, T, u, T.psP[:, 512 * u:512 * u + 256])]
+                      + group_steps(V, T, u, T.rm[:, 256 * u + 7:256 * u + 256:8], ["sn%d" % u]))
+    order = chains[0][:WEAVE + 1]
+    for k in range(5):
+        order += chains[1][k:k + 1] + chains[0][WEAVE + 1 + k:WEAVE + 2 + k]
+    for step in order:
+        step()
+    for u in range(2):
+        S.wait_ge(sem["cel%d" % u], 4)
+        cell(S, T.td[:, 32 * u + 1:32 * u + 32:2], T.td[:, 32 * u + 31:32 * u + 32], col(T.lt, u, 16), T.nin[:, 4 * u:4 * u + 1], sem["n%d" % u])
+
+    on, beside = plans[plan["to"][1]]["passers"][1], plan["passers"][1]
+
+    def send(k, c, p, waits):
+        for name, wait, src, land in zip(PIECES, waits, pieces(c, p, 0), pieces(T.HYC, T.HYS, k)):
+            g.wait_ge(sem[wait], E8)
+            post(tr(src, [(on, land)], far, name + str(k)))
+
+    def number(u):
+        g.wait_ge(sem["n%d" % u], 1)
+        post(tr(T.nin[:, 4 * u:4 * u + 1], [(plan["home"], T.nin[:, 4 * u + 4:4 * u + 5])], near | far if WIDE else near, "n%d" % (u + 1)))
+
+    send(0, T.HXC, T.HXS, ("hxs", "hxc", "hxc"))
+    if TWINS == 1:
+        g.wait_ge(sem.hp1, E8)
+        post(tr(col(T.HQS, 1, 128), [(beside, col(T.HQS, 1, 128))], near, "hp1"))
+    if QAT == 0:
+        g.wait_ge(sem.hq1, E8)
+        post(tr(raw(col(T.HQC, 1, 128)), [(beside, raw(col(T.HQC, 1, 128)))], near, "hq1"))
+    number(0)
+    if QAT == 1:
+        g.wait_ge(sem.hq1, E8)
+        post(tr(raw(col(T.HQC, 1, 128)), [(beside, raw(col(T.HQC, 1, 128)))], near, "hq1"))
+    number(1)
+    send(1, T.HRC, T.HRS, ("hrs0", "hrc0", "hrc0"))
+    post(*[tr(T.nin[:, 4 * u:4 * u + 1], [(cores[plan["chosen"][1 + u]], T.adj[:, 4 * me:4 * me + 1])], every_other(far, u), "an") for u in range(2)])
+    for wait, src, land, see in (("hzs", T.HZS, T.LS, same), ("hzc", T.HZC, T.LC, raw)):
+        g.wait_ge(sem[wait], count(near | far))
+        post(tr(see(src[:]), [(cores[plan["chosen"][0]], see(col(land, 0, 256)))], far, "d0"))
+    finish()
+
+
+def passer_program(g, core, me, T, topo):
+    plan = make_plan(me, T, topo)
+    cores, sem = T.cores, T.sem
+    Op = AluOpType
+    i = plan["passers"].index(core)
+    V, PE = g.vector, g.tensor
+    tr, post, finish = writer(g, core, T, topo)
+    home, mate = cores[me], cores[plan["mate"]]
+    far, near = engines(core, home, plan, T, topo)
+    E8 = count(far)
+    V.memset(T.anew[:], 1.0).then_inc(sem.mf, 1)
+    V.wait_ge(sem.mf, 1)
+    V.memset(T.anew[:, 16:17], 0.0).then_inc(sem.mf, 1)
+    helper_constants(V, T)
+    V.wait_ge(sem.mf, 2)
+    for name in PIECES:
+        PE.wait_ge(sem[name + "0"], E8)
+    for a in range(2):
+        PE.wait_ge(sem["hq%d" % a], E8)
+        PE.wait_ge(sem["hp%d" % a], E8)
+        PE.matmul_mx(T.psP[:, 512 * a:512 * a + 256], col(T.HQC, a, 128), col(T.HQS, a, 128), col(T.HYC, 0, 256), col(T.HYS, 0, 256),
+                     True, True).then_inc(sem["sm%d" % a], 1)
+        running(V, T, a, T.psP[:, 512 * a:512 * a + 256])
+    V.wait_ge(sem.sn0, 1)
+    V.wait_ge(sem.sn1, 1)
+    by_group(V, T, 0, T.rm[:, 15:512:16])
+    V.wait_ge(sem.cel0, 4)
+    for a in range(2):
+        k = 16 * a
+        V.tensor_scalar(T.lt[:, k:k + 16], T.td[:, k:k + 16], T.td[:, k + 15:k + 16], a * MARK / 16, Op.is_lt, Op.add).then_inc(sem.cel0, 1)
+    V.wait_ge(sem.cel0, 6)
+    V.tensor_tensor_scan(T.cnt[:, 0:32], T.anew[:], T.lt[:, 0:32], 0.0, Op.mult, Op.add).then_inc(sem.cel0, 1)
+
+    def numbers():
+        s = plan["whole"][2 * i]
+        g.wait_ge(sem.cel0, 7)
+        post(*[tr(T.cnt[:, 16 * a + 15:16 * a + 16], [(c, T.nb[:, 8 * s:8 * s + 1])], mask, "aw%d" % i)
+               for a, (c, mask) in enumerate(((home, near), (mate, far)))])
+
+    if i == 0:
+        twins = make_plan(plan["mate"], T, topo)["passers"][:TWINS]
+        for name, t, see in (("hp", T.HQS, same), ("hq", T.HQC, raw)):
+            g.wait_ge(sem[name + "0"], E8)
+            post(*[tr(see(col(t, 0, 128)), [(c, see(col(t, a, 128))) for c in to], mask, name + str(a))
+                   for a, (to, mask) in enumerate(((plan["passers"][1:], near), (twins, far)))])
+    for k, (c, p) in enumerate(((T.FXC, T.FXS), (T.FRC, T.FRS))):
+        for name, src, here, there in zip(PIECES, pieces(T.HYC, T.HYS, k), pieces(c, p, 2 * i), pieces(c, p, 2 * i + 1)):
+            if (k, name) == NUMAT[i]:
+                numbers()
+            g.wait_ge(sem[name + str(k)], E8)
+            post(tr(src, [(home, here)], near, ("wx%d", "wr%d")[k] % (2 * i)), tr(src, [(mate, there)], far, ("wx%d", "wr%d")[k] % (2 * i + 1)))
+    if not NUMAT[i]:
+        numbers()
     finish()

from concourse.bass import DstId, RemoteDMATransfer
from concourse.mybir import dt, AluOpType, ActivationFunctionType

N = 8
BIG = 1e29
CODES, PLANE = "float8_e4m3fn_x4", "uint8"
F32, BF16, U16, I32 = "float32", "bfloat16", "uint16", "int32"

SCRATCH = {
    "qwb": ("sbuf", [128, 512], BF16),
    "xb": ("sbuf", [128, 1024], BF16),
    "rb": ("sbuf", [128, 1024], BF16),
    "eb": ("sbuf", [128, 528], BF16),
    "onb": ("sbuf", [128, 128], BF16),
    "onf": ("sbuf", [128, 128], F32),
    "idn": ("sbuf", [128, 128], F32),
    "p16": ("sbuf", [128, 128], F32),
    "pq": ("sbuf", [128, 128], F32),
    "side": ("sbuf", [128, 128], F32),
    "pi": ("sbuf", [128, 8], I32),
    "pm": ("sbuf", [128, 4], F32),
    "msk": ("sbuf", [128, 32], F32),
    "anew": ("sbuf", [128, 32], F32),
    "top": ("sbuf", [128, 256], F32),
    "offd": ("sbuf", [128, 2], U16),
    "QC": ("sbuf", [128, 256], CODES),
    "QS": ("sbuf", [128, 256], PLANE),
    "XC": ("sbuf", [128, 256], CODES),
    "XS": ("sbuf", [128, 256], PLANE),
    "RC": ("sbuf", [128, 256], CODES),
    "RS": ("sbuf", [128, 256], PLANE),
    "EC": ("sbuf", [128, 512], CODES),
    "ES": ("sbuf", [128, 512], PLANE),
    "rm": ("sbuf", [128, 768], F32),
    "ta": ("sbuf", [128, 96], F32),
    "tb": ("sbuf", [128, 96], F32),
    "tc": ("sbuf", [128, 96], F32),
    "td": ("sbuf", [128, 96], F32),
    "lt": ("sbuf", [128, 64], F32),
    "cnt": ("sbuf", [128, 32], BF16),
    "bc": ("sbuf", [128, 768], F32),
    "nin": ("sbuf", [128, 12], F32),
    "nb": ("sbuf", [128, 64], BF16),
    "adj": ("sbuf", [128, 32], F32),
    "chs": ("sbuf", [128, 8], F32),
    "off": ("sbuf", [128, 96], U16),
    "offl": ("sbuf", [128, 40], U16),
    "hb": ("sbuf", [128, 3072], BF16),
    "OC": ("sbuf", [128, 768], CODES),
    "OS": ("sbuf", [128, 768], PLANE),
    "LC": ("sbuf", [128, 768], CODES),
    "LS": ("sbuf", [128, 768], PLANE),
    "FXC": ("sbuf", [128, 1024], CODES),
    "FXS": ("sbuf", [128, 1024], PLANE),
    "FRC": ("sbuf", [128, 1024], CODES),
    "FRS": ("sbuf", [128, 1024], PLANE),
    "HQC": ("sbuf", [128, 384], CODES),
    "HQS": ("sbuf", [128, 384], PLANE),
    "HXC": ("sbuf", [128, 256], CODES),
    "HXS": ("sbuf", [128, 256], PLANE),
    "HYC": ("sbuf", [128, 512], CODES),
    "HYS": ("sbuf", [128, 512], PLANE),
    "HRC": ("sbuf", [128, 512], CODES),
    "HRS": ("sbuf", [128, 512], PLANE),
    "HZC": ("sbuf", [128, 256], CODES),
    "HZS": ("sbuf", [128, 256], PLANE),
    "pf": ("sbuf", [128, 1280], F32),
    "ysb": ("sbuf", [128, 128 * N], F32),
    "dly": ("sbuf", [128, 1024], F32),
    "psD": ("psum", [128, 2048], F32),
    "psP": ("psum", [128, 2048], F32),
}
SEMAPHORES = (
    ["lq", "lx", "mf", "me", "mk", "mt", "mu", "qq", "qx", "qr", "qe", "gi", "gp", "gt", "sp", "si", "so"]
    + ["dm%d" % b for b in range(4)] + ["rs%d" % b for b in range(4)]
    + [n + str(u) for n in ("wx", "wr") for u in range(4)]
    + [n + str(u) for n in ("bcx", "ctx", "ofx", "gv", "gs", "qz", "d") for u in range(6)]
    + [n + str(b) for n in ("sm", "sn", "cel", "aw", "hq", "hp", "hys", "hya", "hyb") for b in range(2)]
    + [n + str(j) for n in ("n", "ym", "yc", "pm", "pc") for j in range(3)]
    + ["yg%d" % j for j in range(5)]
    + ["an", "chv", "yd", "ye", "sent", "hrc0", "hrs0", "hrc1", "hrs1", "hw", "ho", "hm", "sm2", "sn2", "cel2", "sb", "hxc", "hxs", "hzc", "hzs"]
)
MARK = 16.0
SHARE = (24, 24, 24)
CUT = (20, 10)
LAST = (12, 10)
PIECES = ("hys", "hya")
NUMAT = (None, None)
TWINS = 1
SWAP = False
PLAN = 0
WORLD = 256
VIA = ()
SPLIT = False
PRE = (0, 0)
FULL = ((1, 0, True), (1, 1, False), (2, 1, True), (2, 0, False))
RB = 0
DELAY = 0
HOLD = 0
B1VIA = False
EARLY = True
UNITS = (((0, 0), (1, 0), (0, 1), (1, 1)), ((0, 1), (0, 0), (1, 1), (1, 0)))
HM = 1
QD = 0
FOUR = (1, 2)
XO = 1
SPARE_DIE = 0
WIDE = True
WEAVE = 4
QAT = 0
FILL = False
ANVIA = True
QP = 0
QH = 0
EQ = (0, 1)
B1P = False
B0ALL = True
LEAD = 1
OWNW = 0
VSEQ = [("l", 0), ("w", 1), ("g", 0, 0, 0, 28), ("l", 1), ("w", 2), ("p", 0), ("g", 1, 0, 0, 24), ("l", 2), ("p", 1),
        ("g", 2, 0, 0, 28), ("p", 2, 1), ("p", 2, 0), ("W", 0), ("W", 1), ("n",), ("s", 4), ("s", 5), ("k", 1), ("k", 3), ("b", 0)]
SSEQ = [("g", 0, 1, 0, 32), ("g", 0, 0, 28, 32), ("g", 1, 1, 0, 32), ("g", 1, 0, 24, 32), ("g", 2, 1, 0, 32), ("g", 2, 0, 28, 32), ("K", 1), ("K", 2),
        ("k", 2), ("k", 4), ("b", 1), ("b", 2)]


PLANS = {}


def make_plan(me, T, topo):
    if me not in PLANS:
        PLANS[me] = new_plan(me, T, topo)
    return PLANS[me]


def new_plan(me, T, topo):
    cores = T.cores
    core = cores[me]

    def mate_of(r):
        return [s for s in range(N) if topo.mates(cores[r], cores[s])][0]

    ring = [r for r in range(N) if r == me or topo.same_plane(core, cores[r])]
    k, n = ring.index(me), len(ring)
    mate, before, after, across = mate_of(me), ring[(k - 1) % n], ring[(k + 1) % n], ring[(k + 2) % n]
    free = [c for c in topo.cores_of(core) if c != core and topo.may_write(c, cores[mate])]
    beside = [c for c in free if topo.die(c) == topo.die(core)]
    other = [c for c in free if c not in beside]
    taken = [c for r in cores for c in topo.cores_of(r)]
    idle = [c for c in range(WORLD) if c not in taken and topo.same_plane(c, core) and topo.die(c) == topo.die(other[SPARE_DIE] if SPARE_DIE == 0 else core)
            and topo.may_write(c, cores[mate])]
    firsts = [c for c in idle if not any(d < c for d in idle if d in topo.cores_of(c))]
    return {
        "spare": firsts[k], "home": core, "mate": mate, "to": [after, before], "chosen": [mate_of(across), across, mate],
        "whole": [before, mate_of(before), after, mate_of(after)],
        "scorer": other[0], "passers": [beside[0], other[1]], "out": other[:2], "inb": beside[0],
    }


def count(mask):
    return bin(mask).count("1")


def every_other(mask, k=0):
    return sum([1 << e for e in range(mask.bit_length()) if mask >> e & 1][k::2])


def engines(core, near_by, plan, T, topo):
    far = topo.mask(core, T.cores[plan["mate"]])
    return far, topo.mask(core, near_by) & ~far


def writer(g, core, T, topo):
    sent = [0]

    def tr(src, dsts, mask, rsem):
        ids = []
        for c, ap in dsts:
            rid, pid = topo.addr(c, core)
            ids.append(DstId(rid=rid, pnc=pid))
        sent[0] += count(mask)
        return RemoteDMATransfer(dst_ids=ids, dma_engine_mask=mask, remote_sem=T.sem[rsem], srcs=[src], dsts=[ap for c, ap in dsts])

    def post(*transfers):
        g.remote_dma_fused(list(transfers), local_sem=T.sem.sent)

    def finish():
        g.wait_ge(T.sem.sent, sent[0])

    return tr, post, finish


def col(t, j, n):
    return t[:, n * j:n * j + n]


def raw(ap):
    return ap.bitcast(dt.uint8)


def same(ap):
    return ap


def pieces(codes, plane, k):
    return col(plane, k, 256), raw(col(codes, k, 256))


def running(V, T, u, scores):
    V.wait_ge(T.sem["sm%d" % u], 1)
    V.tensor_tensor_scan(col(T.rm, u, 256), T.top[:], scores, -BIG, AluOpType.min, AluOpType.max).then_inc(T.sem["sn%d" % u], 1)


def group_steps(V, T, bt, ends, after, repeat=True):
    Op, done = AluOpType, T.sem["cel%d" % bt]
    a, b, c, d = [col(t, bt, 32) for t in (T.ta, T.tb, T.tc, T.td)]
    calls = [lambda: V.transpose(a, ends), lambda: V.tensor_tensor_scan(b, T.msk[:], a, -BIG, Op.min, Op.max)]
    calls += [lambda: V.tensor_copy(c, b.indirect(T.offd[:, 0:2])), lambda: V.transpose(d, c)] if repeat else [lambda: V.transpose(d, b)]

    def step(k):
        for name in after if k == 0 else ():
            V.wait_ge(T.sem[name], 1)
        if k:
            V.wait_ge(done, k)
        calls[k]().then_inc(done, 1 if k + 1 < len(calls) else 4 - k)

    return [lambda k=k: step(k) for k in range(len(calls))]


def by_group(V, T, bt, ends, fill=None, repeat=True):
    Op, done = AluOpType, T.sem["cel%d" % bt]
    a, b, c, d = [col(t, bt, 32) for t in (T.ta, T.tb, T.tc, T.td)]
    V.transpose(a, ends).then_inc(done, 1)
    if fill:
        fill()
    V.wait_ge(done, 1)
    V.tensor_tensor_scan(b, T.msk[:], a, -BIG, Op.min, Op.max).then_inc(done, 1)
    V.wait_ge(done, 2)
    if not repeat:
        V.transpose(d, b).then_inc(done, 2)
        return
    V.tensor_copy(c, b.indirect(T.offd[:, 0:2])).then_inc(done, 1)
    V.wait_ge(done, 3)
    V.transpose(d, c).then_inc(done, 1)


def cell(S, ends, last, scrap, out, done):
    S.activation(scrap, ends, ActivationFunctionType.Sign, bias=last, scale=-1.0, accum_out=out).then_inc(done, 1)


def rank_program(g, core, T, topo):
    me = T.rank_of(core)
    if me is None:
        for r in range(N):
            if VIA and not PLAN and core == make_plan(r, T, topo)["spare"]:
                spare_program(g, core, r, T, topo)
        homes = [T.rank_of(c) for c in topo.cores_of(core) if T.rank_of(c) is not None]
        if homes:
            plan = make_plan(homes[0], T, topo)
            if PLAN == 0:
                if core in plan["out"]:
                    helper_program(g, core, homes[0], T, topo)
                if core == plan["inb"]:
                    relay_program(g, core, homes[0], T, topo)
            elif core == plan["scorer"]:
                scorer_program(g, core, homes[0], T, topo)
            elif core in plan["passers"]:
                passer_program(g, core, homes[0], T, topo)
        return
    plans = [make_plan(r, T, topo) for r in range(N)]
    plan = plans[me]
    chosen, whole = plan["chosen"], plan["whole"]
    cores, sem = T.cores, T.sem
    Op = AluOpType
    Copy, Identity, Sign = ActivationFunctionType.Copy, ActivationFunctionType.Identity, ActivationFunctionType.Sign
    V, S, PE, SY = g.vector, g.scalar, g.tensor, g.sync
    Q = (col(T.QC, 0, 128), col(T.QS, 0, 128))
    far, near = engines(core, plan["scorer"], plan, T, topo)
    E8 = count(far)

    def bank(b, n):
        return T.psP[:, 512 * b:512 * b + n]

    SY.dma_start(T.qwb[:], T.qw[:]).then_inc(sem.lq, 16)
    S.wait_ge(sem.mf, 1)
    S.dma_start(T.xb[:], T.x[:]).then_inc(sem.lx, 16)

    V.memset(T.onb[:], 1.0).then_inc(sem.mf, 1)
    V.memset(T.eb[:], 0.0).then_inc(sem.me, 1)
    V.memset(T.onf[:], 1.0).then_inc(sem.mf, 1)
    V.memset(T.nb[:], 0.0).then_inc(sem.mt, 1)
    V.wait_ge(sem.gt, 1)
    V.tensor_scalar(T.pi[:, 4:5], T.pi[:, 0:1], 15, None, Op.bitwise_and).then_inc(sem.mu, 1)
    for b in range(4):
        if b == EQ[0]:
            V.wait_ge(sem.lq, 16)
            V.quantize_mx(Q[0], Q[1], T.qwb[:]).then_inc(sem.qq, 1)
        if b == EQ[1]:
            V.wait_ge(sem.lx, 16)
            V.quantize_mx(T.XC[:], T.XS[:], T.xb[:]).then_inc(sem.qx, 1)
        if b == 0:
            V.wait_ge(sem.mu, 1)
            V.tensor_copy(T.pm[:, 0:1], T.pi[:, 4:5]).then_inc(sem.mu, 1)
        V.wait_ge(sem.me, 2)
        V.quantize_mx(col(T.EC, b, 128), col(T.ES, b, 128), T.eb[:, 4 - b:516 - b]).then_inc(sem.qe, 1)
    for b in range(4):
        V.wait_ge(sem["dm%d" % b], 1)
        V.tensor_tensor(T.rb[:, b:1024:4], T.xb[:, b:1024:4], T.psD[:, 512 * b:512 * b + 256], Op.subtract).then_inc(sem["rs%d" % b], 1)
    V.wait_ge(sem.sp, 6)
    running(V, T, 0, bank(0, 256))
    for b in range(4):
        V.wait_ge(sem["rs%d" % b], 1)

    def residuals(h):
        V.quantize_mx(col(T.RC, h, 128), col(T.RS, h, 128), col(T.rb, h, 512)).then_inc(sem.qr, 1)

    if not FILL:
        V.quantize_mx(T.RC[:], T.RS[:], T.rb[:]).then_inc(sem.qr, 2)

    PE.wait_ge(sem.qx, 1)
    for b in range(4):
        PE.wait_ge(sem.qe, b + 1)
        PE.matmul_mx(T.psD[:, 512 * b:512 * b + 256], col(T.EC, b, 128), col(T.ES, b, 128), T.XC[:], T.XS[:], True, True).then_inc(sem["dm%d" % b], 1)

    def score(u):
        PE.matmul_mx(bank(u, 256), col(T.QC, u, 128), col(T.QS, u, 128), T.XC[:], T.XS[:], True, True).then_inc(sem["sm%d" % u], 1)

    spots = [(T.psD, 512 * b + 256) for b in (0, 2, 3, 1, 0, 2)]

    def spread(i):
        t, a = spots[i]
        PE.wait_ge(sem["bcx%d" % i], 1)
        PE.transpose(t[:, a:a + 128], col(T.bc, i, 128), T.idn[:]).then_inc(sem["ctx%d" % i], 1)

    def widen(E, j):
        E.wait_ge(sem["n%d" % j], E8 if j else 1)
        out, number = col(T.bc, j, 128), T.nin[:, 4 * j:4 * j + 1]
        (V.tensor_scalar(out, T.pq[:], number, None, Op.add) if E is V else S.activation(out, T.pq[:], Identity, bias=number)).then_inc(sem["bcx%d" % j], 1)

    def lists(j):
        t, a = spots[j]
        V.wait_ge(sem["ctx%d" % j], 1)
        if j in FOUR:
            V.tensor_scalar(col(T.off, j, 32), t[:, a:a + 128:4], 64.0, None, Op.mult).then_inc(sem["ofx%d" % j], 4)
            return
        for e in range(4):
            V.tensor_scalar(T.off[:, 32 * j + e:32 * j + 32:4], t[:, a + 15:a + 128:16], 64.0, 16.0 * e - 60, Op.mult, Op.add).then_inc(sem["ofx%d" % j], 1)

    def widen_pair(h):
        V.wait_ge(sem["aw%d" % h], 2 * E8)
        lo, hi = [T.adj[:, 4 * s:4 * s + 1] for s in whole[2 * h:2 * h + 2]]
        V.tensor_scalar(col(T.bc, 4 + h, 128), T.side[:], hi, lo, Op.mult, Op.max).then_inc(sem["bcx%d" % (4 + h)], 1)

    def short_lists(i):
        t, a = spots[i]
        V.wait_ge(sem["ctx%d" % i], 1)
        for k in range(1 if i == 3 else 2):
            V.tensor_scalar(col(T.offl, 0 if i == 3 else 2 * i - 7 + k, 8), t[:, a + (15 if i == 3 else 8 * k):a + 128:16], 16.0, T.pm[:, 2 * k:2 * k + 1],
                            Op.mult, Op.add).then_inc(sem["ofx%d" % i], 1)

    calls = {}

    def move(E, out, src):
        return V.tensor_copy(out, src) if E is V else S.activation(out, src, Copy)

    def gather(E, j, part, lo, hi):
        if lo == hi:
            return
        a, name = 1024 * j + 512 * part, ("gv%d" if E is V else "gs%d") % (2 * j + part)
        E.wait_ge(sem["ofx%d" % j], 4)
        move(E, T.hb[:, a + 16 * lo:a + 16 * hi], (T.xb, T.rb)[part][:, 0:1024].indirect(T.off[:, 32 * j + lo:32 * j + hi])).then_inc(sem[name], 1)
        calls[name] = calls.get(name, 0) + 1

    def pack(j, parts=(0, 1)):
        for name in [n % (2 * j + part) for part in parts for n in ("gv%d", "gs%d")]:
            if name in calls:
                V.wait_ge(sem[name], calls[name])
        a, n = 256 * j + 128 * parts[0], 128 * len(parts)
        V.quantize_mx(T.OC[:, a:a + n], T.OS[:, a:a + n], T.hb[:, 4 * a:4 * (a + n)]).then_inc(sem["qz%d" % (2 * j + parts[0])], 1)

    every = [me] + whole

    def pick(E, i):
        E.wait_ge(sem["pc%d" % ((i + 1) // 2)], 1)
        E.wait_ge(sem["ofx%d" % (3 + (i + 1) // 2)], 2 if i else 1)
        move(E, col(T.ysb, every[i], 128), col(T.pf, i, 256).indirect(col(T.offl, i, 8))).then_inc(sem["yg%d" % i], 1)

    def full(i, b, part, first):
        c, p = ((T.FXC, T.FXS), (T.FRC, T.FRS))[part] if i else ((T.XC, T.XS), (T.RC, T.RS))[part]
        n = 512 if i else 256
        for f in range(2 * i - 2, 2 * i) if i else ():
            PE.wait_ge(sem[("wx%d", "wr%d")[part] % f], len(PIECES) * E8 if PLAN else ((2 if f % 2 and f // 2 in VIA else 3) * E8, (2 + i + 2 * RB * (i - 1)) * E8 // 2)[part])
        mm = PE.matmul_mx(bank(b, n), Q[0], Q[1], col(c, max(i - 1, 0), n), col(p, max(i - 1, 0), n), first, not first)
        if not first:
            mm.then_inc(sem["pm%d" % i], 1)

    def keep(E, i, b):
        E.wait_ge(sem["pm%d" % i], 1)
        move(E, T.pf[:, 512 * i - 256:512 * i + 256] if i else T.pf[:, 0:256], bank(b, 512 if i else 256)).then_inc(sem["pc%d" % i], 1)

    places = bank(2, 128), bank(3, 128), T.psD[:, 1536:1664]

    def product(j, part, first):
        if first:
            PE.wait_ge(sem["d%d" % (2 * j)], 2 * E8)
        mm = PE.matmul_mx(places[j], Q[0], Q[1], col(T.LC, 2 * j + part, 128), col(T.LS, 2 * j + part, 128), first, not first)
        if not first:
            mm.then_inc(sem["ym%d" % j], 1)

    def bring(E, j):
        E.wait_ge(sem["ym%d" % j], 1)
        move(E, col(T.ysb, chosen[j], 128), places[j]).then_inc(sem["yc%d" % j], 1)

    def store(E, ready, s, done):
        for name in ready:
            E.wait_ge(sem[name], 1)
        E.dma_start(T.y[:, 128 * s:128 * (s + len(ready))], T.ysb[:, 128 * s:128 * (s + len(ready))]).then_inc(done, 16)

    def numbers(E):
        for h in range(2):
            V.wait_ge(sem["aw%d" % h], 2 * E8)
        V.wait_ge(sem.an, (2 if PLAN else 3) * E8)
        V.wait_ge(sem.so, 1)
        V.tensor_tensor(T.chs[:], T.nb[:, 0:64:8], T.adj[:, 0:32:4], Op.add).then_inc(sem.chv, 1)

    steps = {"l": lambda E, j: lists(j), "w": widen, "g": gather, "s": lambda E, i: short_lists(i), "p": lambda E, j, *parts: pack(j, parts or (0, 1)),
             "W": lambda E, h: widen_pair(h), "k": pick, "K": lambda E, i: keep(E, i, i - 1), "b": bring, "n": numbers}

    S.wait_ge(sem.mf, 2)
    S.activation(T.top[:, 0:128], T.onf[:], Copy, scale=BIG)
    S.activation(T.top[:, 128:256], T.onf[:], Copy, scale=BIG).then_inc(sem.sp, 1)
    S.activation(T.msk[:], T.onf[:, 0:32], Copy, scale=BIG).then_inc(sem.si, 1)
    S.activation(T.adj[:, 4 * min(chosen[:2]):4 * min(chosen[:2]) + 5:4], T.onf[:, 0:2], Copy, scale=0.0).then_inc(sem.sp, 2)
    S.wait_ge(sem.mt, 1)
    for s in whole[1::2]:
        S.activation(T.nb[:, 8 * s:8 * s + 1], T.onf[:, 0:1], Copy, scale=-MARK).then_inc(sem.sp, 1)
    S.wait_ge(sem.si, 1)
    S.activation(T.msk[:, 0:32:16], T.onf[:, 0:2], Copy, scale=-BIG).then_inc(sem.sp, 1)
    S.wait_ge(sem.mu, 2)
    S.activation(T.pm[:, 1:2], T.pm[:, 0:1], Copy, scale=1.0 / 16).then_inc(sem.si, 1)
    S.activation(T.pm[:, 2:3], T.pm[:, 0:1], Identity, bias=-16 * MARK).then_inc(sem.sp, 1)
    S.activation(T.side[:], T.onf[:, 0:128], Sign, scale=T.pm[:, 0:1], bias=-7.5).then_inc(sem.sp, 1)
    S.wait_ge(sem.gp, 1)
    S.wait_ge(sem.si, 2)
    S.activation(T.pq[:], T.p16[:], Identity, bias=T.pm[:, 1:2], scale=1.0 / 64).then_inc(sem.si, 1)
    for b in range(4):
        S.wait_ge(sem["rs%d" % b], 1)
    keep(S, 0, 2)
    S.wait_ge(sem.si, 3)
    S.wait_ge(sem.cel1, 4)
    cell(S, T.td[:, 33:64:2], T.td[:, 63:64], T.lt[:, 0:16], T.adj[:, 4 * me:4 * me + 1], sem.so)
    for k in range(2):
        if k == OWNW:
            S.wait_ge(sem.so, 1)
            S.activation(col(T.bc, 3, 128), T.onf[:, 0:128], Copy, scale=T.adj[:, 4 * me:4 * me + 1]).then_inc(sem.bcx3, 1)
        if k == 0:
            S.wait_ge(sem.cel0, 4)
            cell(S, T.td[:, 1:32:2], T.td[:, 31:32], T.lt[:, 16:32], T.nin[:, 0:1], sem.n0)
    widen(S, 0)
    S.activation(T.cnt[:, 0:1], T.nin[:, 0:1], Copy).then_inc(sem.sb, 1)
    pick(S, 0)
    for name, *args in SSEQ:
        steps[name](S, *args)
    store(S, ("yc2",), chosen[2], sem.yd)
    S.wait_ge(sem.yd, 16)

    PE.wait_ge(sem.qq, 1)
    score(0)
    full(0, 2, 0, True)
    PE.wait_ge(sem.hq0, E8 // 2 if SWAP else E8)
    PE.wait_ge(sem.hp0, E8 // 2)
    score(1)
    PE.wait_ge(sem.qr, 2)
    full(0, 2, 1, False)
    PE.wait_ge(sem.gi, 1)
    for i in (3, 0, 1, 2):
        spread(i)
    PE.wait_ge(sem.sn1, 1)
    for i, part, first in FULL:
        full(i, i - 1, part, first)
    PE.wait_ge(sem.ofx0, 4)
    spread(4)
    PE.wait_ge(sem.ofx1, 4)
    spread(5)
    PE.wait_ge(sem.pc0, 1)
    PE.wait_ge(sem.ofx2, 4)
    for j in (1, 0, 2):
        for part in range(2):
            product(j, part, part == 0)

    V.wait_ge(sem.mt, 1)
    own = group_steps(V, T, 1, T.rm[:, 7:256:8], ["sn0"], False)
    asked = [lambda: running(V, T, 1, bank(1, 256))] + group_steps(V, T, 0, T.rm[:, 256 + 7:512:8], ["sn1"], 0 in FOUR)
    for k, step in enumerate(asked):
        for mine in own[k + LEAD:k + LEAD + 1] if k else own[:LEAD + 1]:
            mine()
        step()
    V.wait_ge(sem.sp, 8)
    V.wait_ge(sem.si, 3)
    short_lists(3)
    for name, *args in VSEQ:
        if DELAY and (name, *args) == ("l", 2):
            V.wait_ge(sem.ctx2, 1)
            V.memset(T.dly[:], 0.0)
        steps[name](V, *args)

    if not EARLY:
        SY.wait_ge(sem.ctx4, 1)
    store(SY, ("yg0",), me, sem.ye)
    SY.wait_ge(sem.chv, 1)
    SY.dma_start(T.ch[:], T.chs[15:128:16, :]).then_inc(sem.ye, 16)
    store(SY, ("yg1", "yg2"), min(whole[:2]), sem.ye)
    store(SY, ("yg3", "yg4"), min(whole[2:]), sem.ye)
    store(SY, ("yc1",), chosen[1], sem.ye)
    store(SY, ("yc0",), chosen[0], sem.ye)
    SY.wait_ge(sem.ye, 16 * 6)

    tr, post, finish = writer(g, core, T, topo)
    g.iota(T.pi[:, 0:1], [[0, 1]], 0, 1).then_inc(sem.gt, 1)
    g.wait_ge(sem.mf, 1)
    g.wait_ge(sem.me, 1)
    g.affine_select(T.eb[:, 4:516:4], T.onb[:], [[-1, 128]], Op.is_equal, 0.0, 0, 1).then_inc(sem.me, 1)


    def pair(codes, plane, dst, land, mask, names):
        post(tr(plane, [(dst, land[1])], mask, names[1]))
        post(tr(raw(codes), [(dst, raw(land[0]))], mask, names[0]))

    def slot(k):
        return col(T.HQC, k, 128), col(T.HQS, k, 128)

    scorers = [plans[chosen[1 + i]]["out"][0 if PLAN else i] for i in range(2)]
    g.wait_ge(sem.qq, 1)
    first = [(scorers[0], slot(0 if PLAN else 2)), (cores[chosen[0]], (col(T.QC, 1, 128), col(T.QS, 1, 128)))][::-1 if SWAP else 1]
    post(tr(raw(Q[0]), [(first[0][0], raw(first[0][1][0]))], every_other(far), "hq0"))
    post(tr(Q[1], [(c, land[1]) for c, land in first], every_other(far, 1), "hp0"), *([tr(Q[1], [(plan["inb"] if QP else plan["out"][0], slot(0)[1])], near, "hw")] if QP or QH else []))
    post(tr(raw(Q[0]), [(first[1][0], raw(first[1][1][0]))], far, "hq0"))
    g.wait_ge(sem.qx, 1)
    pair(T.XC[:], T.XS[:], plan["out"][0], (T.HXC[:], T.HXS[:]), near, ("hxc", "hxs"))
    if PLAN == 0:
        if QP:
            post(tr(raw(Q[0]), [(scorers[1], raw(slot(1)[0]))], far, "hq0"))
        else:
            pair(Q[0], Q[1], scorers[1], slot(1), far, ("hq0", "hp0"))
        post(tr(T.XS[:], [(plan["out"][1], T.HXS[:])], near, "hxs"))
        if not XO:
            post(tr(Q[1], [(plan["out"][0], slot(0)[1])], near, "hw"))
        post(tr(raw(T.XC[:]), [(plan["out"][1], raw(T.HXC[:]))], near, "hxc"))
        if QD == 2:
            for name, src, land in (("hw", Q[1], slot(0)[1]), ("ho", raw(Q[0]), raw(slot(0)[0]))):
                post(*[tr(src, [(h, land)], mask, name) for h, mask in zip(plan["out"], (near, far))])
        else:
            if XO and not QP and not QH:
                post(tr(Q[1], [(h, slot(0)[1]) for h in plan["out"][:1 + QD]], near, "hw"))
            post(tr(raw(Q[0]), [(h, raw(slot(0)[0])) for h in plan["out"]], near, "ho"))
        g.wait_ge(sem.mf, 2)
        g.iota(T.p16[:], [[0, 8], [1, 16]], 0, 0, allow_small_or_imprecise_dtypes=True).then_inc(sem.gp, 1)
        g.affine_select(T.idn[:], T.onf[:], [[-1, 128]], Op.is_equal, 0.0, 0, 1).then_inc(sem.gi, 1)
        g.wait_ge(sem.qr, 2)
        for i, r in enumerate(plan["to"]):
            if i and RB:
                post(tr(T.RS[:], [(plans[r]["inb"], col(T.HRS, 1, 256))], far, "hrs1"))
                for h, c in enumerate((plans[r]["inb"], plans[r]["out"][1])):
                    post(tr(raw(col(T.RC, h, 128)), [(c, raw(col(T.HRC, 2 + h, 128)))], far, "hrc1"))
                continue
            pair(T.RC[:], T.RS[:], plans[r]["inb"], (col(T.HRC, i, 256), col(T.HRS, i, 256)), far, ("hrc%d" % i, "hrs%d" % i))
    else:
        for k, name, see in ((1, "hp", same), (0, "hq", raw)):
            post(tr(see(Q[k]), [(scorers[1], see(slot(1)[k]))], far, name + "1"), tr(see(Q[k]), [(plan["passers"][0], see(slot(0)[k]))], near, name + "0"))
        on = plans[plan["to"][0]]["passers"][0]
        for name, src, land in zip(PIECES, pieces(T.XC, T.XS, 0), pieces(T.HYC, T.HYS, 0)):
            post(tr(src, [(on, land)], far, name + "0"))
        g.wait_ge(sem.qr, 2)
        for name, src, land, here, home in zip(PIECES, pieces(T.RC, T.RS, 0), pieces(T.HYC, T.HYS, 1), pieces(T.HRC, T.HRS, 0), ("hrs0", "hrc0")):
            post(tr(src, [(on, land)], far, name + "1"), tr(src, [(plan["scorer"], here)], near, home))
    g.wait_ge(sem.sb, 1)
    if ANVIA:
        post(tr(T.cnt[:, 0:1], [(plan["inb"], T.cnt[:, 0:1])], near, "an"))
    else:
        post(tr(T.cnt[:, 0:1], [(cores[chosen[0]], T.nb[:, 8 * me:8 * me + 1])], far, "an"))
    g.wait_ge(sem.qz0, 1)
    pair(col(T.OC, 0, 256), col(T.OS, 0, 256), plan["scorer"], (T.HZC[:], T.HZS[:]), near | far if B0ALL else near, ("hzc", "hzs"))
    for j in (1, 2):
        g.wait_ge(sem["qz%d" % (2 * j)], 1)
        if j == 2:
            g.wait_ge(sem.qz5, 1)
        if j == 1 and B1P:
            post(tr(col(T.OS, 1, 256), [(plan["out"][1], T.HZS[:])], near, "hzs"))
            post(tr(raw(col(T.OC, 1, 256)), [(cores[chosen[1]], raw(col(T.LC, 1, 256)))], far, "d2"))
            continue
        if j == 1 and B1VIA:
            pair(col(T.OC, 1, 256), col(T.OS, 1, 256), plan["out"][1], (T.HZC[:], T.HZS[:]), near | far, ("hzc", "hzs"))
            continue
        post(tr(raw(col(T.OC, j, 256)), [(cores[chosen[j]], raw(col(T.LC, j, 256)))], far, "d%d" % (2 * j)))
        post(tr(col(T.OS, j, 256), [(cores[chosen[j]], col(T.LS, j, 256))], far, "d%d" % (2 * j)))
    finish()


def helper_constants(V, T):
    V.memset(T.top[:], BIG).then_inc(T.sem.mt, 1)
    V.memset(T.msk[:], BIG).then_inc(T.sem.mk, 1)
    for h in range(2):
        V.memset(T.offd[:, h:h + 1], 16 * h + 15).then_inc(T.sem.mt, 1)
    V.wait_ge(T.sem.mk, 1)
    V.memset(T.msk[:, 0:32:16], -BIG).then_inc(T.sem.mt, 1)
    V.wait_ge(T.sem.mt, 4)


def hand_on(g, T, tr, post, wait, src, here, there, name, i, home, mate, near, far):
    g.wait_ge(T.sem[wait[0]], wait[1])
    post(*[tr(src, [(c, land)], mask, name + str(f)) for c, land, mask, f in ((home, here, near, 2 * i), (mate, there, far, 2 * i + 1)) if mask])


def spare_program(g, core, me, T, topo):
    plan = make_plan(me, T, topo)
    tr, post, finish = writer(g, core, T, topo)
    i = VIA[0]
    to = T.cores[make_plan(plan["to"][i], T, topo)["mate"]]
    far = topo.mask(core, to)
    for name, src, land, see in (("hys0", T.HYS, T.FXS, same), ("hya0", T.HYC, T.FXC, raw)):
        g.wait_ge(T.sem[name], count(far))
        post(tr(see(col(src, 0, 256)), [(to, see(col(land, 2 * i + 1, 256)))], far, "wx%d" % (2 * i + 1)))
    finish()


def helper_program(g, core, me, T, topo):
    plans = [make_plan(r, T, topo) for r in range(N)]
    plan = plans[me]
    cores, sem = T.cores, T.sem
    i = plan["out"].index(core)
    Op = AluOpType
    V, S, PE = g.vector, g.scalar, g.tensor
    tr, post, finish = writer(g, core, T, topo)
    home, mate, on = cores[me], cores[plan["mate"]], plans[plan["to"][i]]["out"][i]
    far, near = engines(core, home, plan, T, topo)
    E8 = count(far)
    V.memset(T.td[:, 32:32 + int(MARK)], -BIG).then_inc(sem.mf, 1)
    helper_constants(V, T)

    def score(u, a, c, p):
        PE.matmul_mx(T.psP[:, 512 * u:512 * u + 256], col(T.HQC, a, 128), col(T.HQS, a, 128), c[:, 0:256], p[:, 0:256], True, True).then_inc(sem["sm%d" % u], 1)
        running(V, T, u, T.psP[:, 512 * u:512 * u + 256])

    for name, halves in (("hxc", 2), ("hxs", 2), ("hq0", 2 if SWAP else 1 + i), ("hp0", 1 + i)):
        PE.wait_ge(sem[name], halves * E8 // 2)
    score(2, 2 - i, T.HXC, T.HXS)
    V.wait_ge(sem.sn2, 1)
    by_group(V, T, 2, T.rm[:, 512 + 7:768:8], None, 1 + i in FOUR)
    S.wait_ge(sem.cel2, 4)
    cell(S, T.td[:, 65:96:2], T.td[:, 95:96], col(T.lt, 3, 16), T.nin[:, 0:1], sem.n0)
    if i == 0:
        S.wait_ge(sem.n0, 1)
        S.activation(T.cnt[:, 0:1], T.nin[:, 0:1], ActivationFunctionType.Copy).then_inc(sem.sb, 1)
    for h, a in UNITS[i]:
        for name, n in (("hys0", 1), (("hya0", "hyb0")[h], 1)) + ((("hm", 2 - 2 * i),) if a else (("ho", 1), ("hw", 1))):
            if n:
                PE.wait_ge(sem[name], n * E8)
        if True:
            out, k = T.psD[:, 512 * (2 * h + a):512 * (2 * h + a) + 128], 256 * a + 128 * h
            PE.matmul_mx(out, col(T.HQC, a, 128), col(T.HQS, a, 128), col(T.HYC, h, 128), col(T.HYS, h, 128), True, True).then_inc(sem["sm%d" % a], 1)
            V.wait_ge(sem["sm%d" % a], h + 1)
            if h:
                V.wait_ge(sem["sn%d" % a], 1)
            V.tensor_tensor_scan(T.rm[:, k:k + 128], T.top[:, 0:128], out, T.rm[:, k - 1:k] if h else -BIG, Op.min, Op.max).then_inc(sem["sn%d" % a], 1)
    V.wait_ge(sem.sn0, 2)
    V.wait_ge(sem.sn1, 2)
    by_group(V, T, 0, T.rm[:, 15:512:16])
    S.wait_ge(sem.cel0, 4)
    S.wait_ge(sem.mf, 1)
    for a in range(2):
        n = 16 + a * int(MARK)
        cell(S, T.td[:, 16 * a:16 * a + n], T.td[:, 16 * a + 15:16 * a + 16], T.lt[:, 16 * a:16 * a + n], T.nin[:, 4 + 4 * a:5 + 4 * a], sem.so)

    ons = [on] + ([plan["spare"]] if i in VIA else [])
    if QH == 2 and i == 0:
        g.wait_ge(sem.hw, E8)
        post(tr(col(T.HQS, 0, 128), [(plan["out"][1], col(T.HQS, 0, 128))], near, "hw"))
    g.wait_ge(sem.hxs, E8)
    post(tr(T.HXS[:], [(c, col(T.HYS, 0, 256)) for c in ons], far, "hys0"))
    if i == 1:
        g.wait_ge(sem.hp0, E8)
        post(tr(col(T.HQS, 1, 128), [(plan["out"][0], col(T.HQS, 1, 128))], near, "hm"))
    g.wait_ge(sem.hxc, E8)
    for h in range(2):
        more = []
        if SPLIT and (i, h) == (1, 0):
            continue
        if i == 1 and h == HM:
            g.wait_ge(sem.hq0, E8)
            more = [tr(raw(col(T.HQC, 1, 128)), [(plan["out"][0], raw(col(T.HQC, 1, 128)))], near, "hm")]
        post(tr(raw(col(T.HXC, h, 128)), [(on, raw(col(T.HYC, h, 128)))], far, ("hya0", "hyb0")[h]), *more)
    if SPLIT and i == 0:
        post(tr(raw(col(T.HXC, 0, 128)), [(plans[plan["to"][1]]["out"][1], raw(col(T.HYC, 0, 128)))], far, "hya0"))
    for c in ons[1:]:
        post(tr(raw(T.HXC[:]), [(c, raw(col(T.HYC, 0, 256)))], far, "hya0"))
    if i == 1:
        if HM == 2:
            g.wait_ge(sem.hq0, E8)
            post(tr(raw(col(T.HQC, 1, 128)), [(plan["out"][0], raw(col(T.HQC, 1, 128)))], near, "hm"))
    elif QP == 1:
        g.wait_ge(sem.hw, E8)
        post(tr(col(T.HQS, 0, 128), [(plan["out"][1], col(T.HQS, 0, 128))], near, "hw"))
    elif QD == 0 and not QP and QH < 2:
        g.wait_ge(sem.hw, E8)
        post(tr(col(T.HQS, 0, 128), [(plan["out"][1], col(T.HQS, 0, 128))], near, "hw"))
    for k in range(4):
        if k == PRE[i]:
            g.wait_ge(sem.n0, 1)
            post(tr(T.nin[:, 0:1], [(home, T.nin[:, 4 + 4 * i:5 + 4 * i])], near, "n%d" % (1 + i)),
                 *[tr(T.nin[:, 0:1], [(cores[plan["chosen"][2]], T.adj[:, 4 * me:4 * me + 1])], far, "an") for once in range(i)])
        if k == 0:
            hand_on(g, T, tr, post, ("hys0", E8), col(T.HYS, 0, 256), col(T.FXS, 2 * i, 256), col(T.FXS, 2 * i + 1, 256), "wx", i, home, mate, near, 0 if i in VIA else far)
        elif k < 3:
            h = k - 1
            hand_on(g, T, tr, post, (("hya0", "hyb0")[h], E8), raw(col(T.HYC, h, 128)), raw(col(T.FXC, 4 * i + h, 128)), raw(col(T.FXC, 4 * i + 2 + h, 128)),
                    "wx", i, home, mate, near, 0 if i in VIA else far)
    if i == 1 and RB:
        hand_on(g, T, tr, post, ("hrc1", E8), raw(col(T.HRC, 3, 128)), raw(col(T.FRC, 5, 128)), raw(col(T.FRC, 7, 128)), "wr", 1, home, mate, near, far)
    s = plan["whole"][2 * i]
    if i == 0:
        g.wait_ge(sem.sb, 1)
        post(tr(T.cnt[:, 0:1], [(cores[plan["chosen"][1]], T.nb[:, 8 * me:8 * me + 1])], far, "an"))
    g.wait_ge(sem.so, 2)
    post(*[tr(T.nin[:, 4 + 4 * a:5 + 4 * a], [(c, T.adj[:, 4 * s:4 * s + 1])], mask, "aw%d" % i)
           for a, (c, mask) in enumerate(((home, near), (mate, far)))])
    if i == 1 and B1P:
        g.wait_ge(sem.hzs, E8)
        post(tr(T.HZS[:], [(cores[plan["chosen"][1]], col(T.LS, 1, 256))], far, "d2"))
    if i == 0 or B1VIA:
        for wait, src, land, see in (("hzs", T.HZS, T.LS, same), ("hzc", T.HZC, T.LC, raw)):
            g.wait_ge(sem[wait], count(near | far) if B0ALL else E8)
            post(tr(see(src[:]), [(cores[plan["chosen"][i]], see(col(land, i, 256)))], far, "d%d" % (2 * i)))
    finish()


def relay_program(g, core, me, T, topo):
    plan = make_plan(me, T, topo)
    tr, post, finish = writer(g, core, T, topo)
    home, mate = T.cores[me], T.cores[plan["mate"]]
    far, near = engines(core, home, plan, T, topo)
    if QP:
        g.wait_ge(T.sem.hw, count(near))
        post(tr(col(T.HQS, 0, 128), [(make_plan(plan["mate"], T, topo)["out"][1], col(T.HQS, 1, 128))], far, "hp0"),
             tr(col(T.HQS, 0, 128), [(h, col(T.HQS, 0, 128)) for h in plan["out"][:QP]], near, "hw"))
    for i in range(2):
        for wait, src, land, see in (("hrs", T.HRS, T.FRS, same), ("hrc", T.HRC, T.FRC, raw)):
            masks = (every_other(near), every_other(far)) if (i, wait) == (0, "hrs") else (near, far)
            if HOLD == 1 and (i, wait) == (1, "hrc"):
                g.wait_ge(T.sem.hrc1, count(far))
                g.iota(T.dly[:, 0:400], [[1, 400]], 0, 0, allow_small_or_imprecise_dtypes=True)
            if RB and (i, wait) == (1, "hrc"):
                hand_on(g, T, tr, post, ("hrc1", count(far)), raw(col(src, 2, 128)), raw(col(land, 4, 128)), raw(col(land, 6, 128)), "wr", i, home, mate, *masks)
                continue
            hand_on(g, T, tr, post, (wait + str(i), count(far)), see(col(src, i, 256)), see(col(land, 2 * i, 256)), see(col(land, 2 * i + 1, 256)), "wr", i, home, mate, *masks)
    if ANVIA:
        g.wait_ge(T.sem.an, count(near))
        post(tr(T.cnt[:, 0:1], [(T.cores[plan["chosen"][0]], T.nb[:, 8 * me:8 * me + 1])], far, "an"))
    finish()


def scorer_program(g, core, me, T, topo):
    plans = [make_plan(r, T, topo) for r in range(N)]
    plan = plans[me]
    cores, sem = T.cores, T.sem
    V, S, PE = g.vector, g.scalar, g.tensor
    tr, post, finish = writer(g, core, T, topo)
    far, near = engines(core, plan["home"], plan, T, topo)
    E8 = count(far)
    helper_constants(V, T)
    PE.wait_ge(sem.hxc, E8)
    PE.wait_ge(sem.hxs, E8)
    chains = []
    for u in range(2):
        PE.wait_ge(sem["hq%d" % u], E8 if SWAP else (1 + u) * E8 // 2)
        PE.wait_ge(sem["hp%d" % u], (1 + u) * E8 // 2)
        PE.matmul_mx(T.psP[:, 512 * u:512 * u + 256], col(T.HQC, u, 128), col(T.HQS, u, 128), T.HXC[:], T.HXS[:], True, True).then_inc(sem["sm%d" % u], 1)
        chains.append([lambda u=u: running(V, T, u, T.psP[:, 512 * u:512 * u + 256])]
                      + group_steps(V, T, u, T.rm[:, 256 * u + 7:256 * u + 256:8], ["sn%d" % u]))
    order = chains[0][:WEAVE + 1]
    for k in range(5):
        order += chains[1][k:k + 1] + chains[0][WEAVE + 1 + k:WEAVE + 2 + k]
    for step in order:
        step()
    for u in range(2):
        S.wait_ge(sem["cel%d" % u], 4)
        cell(S, T.td[:, 32 * u + 1:32 * u + 32:2], T.td[:, 32 * u + 31:32 * u + 32], col(T.lt, u, 16), T.nin[:, 4 * u:4 * u + 1], sem["n%d" % u])

    on, beside = plans[plan["to"][1]]["passers"][1], plan["passers"][1]

    def send(k, c, p, waits):
        for name, wait, src, land in zip(PIECES, waits, pieces(c, p, 0), pieces(T.HYC, T.HYS, k)):
            g.wait_ge(sem[wait], E8)
            post(tr(src, [(on, land)], far, name + str(k)))

    def number(u):
        g.wait_ge(sem["n%d" % u], 1)
        post(tr(T.nin[:, 4 * u:4 * u + 1], [(plan["home"], T.nin[:, 4 * u + 4:4 * u + 5])], near | far if WIDE else near, "n%d" % (u + 1)))

    send(0, T.HXC, T.HXS, ("hxs", "hxc", "hxc"))
    if TWINS == 1:
        g.wait_ge(sem.hp1, E8)
        post(tr(col(T.HQS, 1, 128), [(beside, col(T.HQS, 1, 128))], near, "hp1"))
    if QAT == 0:
        g.wait_ge(sem.hq1, E8)
        post(tr(raw(col(T.HQC, 1, 128)), [(beside, raw(col(T.HQC, 1, 128)))], near, "hq1"))
    number(0)
    if QAT == 1:
        g.wait_ge(sem.hq1, E8)
        post(tr(raw(col(T.HQC, 1, 128)), [(beside, raw(col(T.HQC, 1, 128)))], near, "hq1"))
    number(1)
    send(1, T.HRC, T.HRS, ("hrs0", "hrc0", "hrc0"))
    post(*[tr(T.nin[:, 4 * u:4 * u + 1], [(cores[plan["chosen"][1 + u]], T.adj[:, 4 * me:4 * me + 1])], every_other(far, u), "an") for u in range(2)])
    for wait, src, land, see in (("hzs", T.HZS, T.LS, same), ("hzc", T.HZC, T.LC, raw)):
        g.wait_ge(sem[wait], count(near | far))
        post(tr(see(src[:]), [(cores[plan["chosen"][0]], see(col(land, 0, 256)))], far, "d0"))
    finish()


def passer_program(g, core, me, T, topo):
    plan = make_plan(me, T, topo)
    cores, sem = T.cores, T.sem
    Op = AluOpType
    i = plan["passers"].index(core)
    V, PE = g.vector, g.tensor
    tr, post, finish = writer(g, core, T, topo)
    home, mate = cores[me], cores[plan["mate"]]
    far, near = engines(core, home, plan, T, topo)
    E8 = count(far)
    V.memset(T.anew[:], 1.0).then_inc(sem.mf, 1)
    V.wait_ge(sem.mf, 1)
    V.memset(T.anew[:, 16:17], 0.0).then_inc(sem.mf, 1)
    helper_constants(V, T)
    V.wait_ge(sem.mf, 2)
    for name in PIECES:
        PE.wait_ge(sem[name + "0"], E8)
    for a in range(2):
        PE.wait_ge(sem["hq%d" % a], E8)
        PE.wait_ge(sem["hp%d" % a], E8)
        PE.matmul_mx(T.psP[:, 512 * a:512 * a + 256], col(T.HQC, a, 128), col(T.HQS, a, 128), col(T.HYC, 0, 256), col(T.HYS, 0, 256),
                     True, True).then_inc(sem["sm%d" % a], 1)
        running(V, T, a, T.psP[:, 512 * a:512 * a + 256])
    V.wait_ge(sem.sn0, 1)
    V.wait_ge(sem.sn1, 1)
    by_group(V, T, 0, T.rm[:, 15:512:16])
    V.wait_ge(sem.cel0, 4)
    for a in range(2):
        k = 16 * a
        V.tensor_scalar(T.lt[:, k:k + 16], T.td[:, k:k + 16], T.td[:, k + 15:k + 16], a * MARK / 16, Op.is_lt, Op.add).then_inc(sem.cel0, 1)
    V.wait_ge(sem.cel0, 6)
    V.tensor_tensor_scan(T.cnt[:, 0:32], T.anew[:], T.lt[:, 0:32], 0.0, Op.mult, Op.add).then_inc(sem.cel0, 1)

    def numbers():
        s = plan["whole"][2 * i]
        g.wait_ge(sem.cel0, 7)
        post(*[tr(T.cnt[:, 16 * a + 15:16 * a + 16], [(c, T.nb[:, 8 * s:8 * s + 1])], mask, "aw%d" % i)
               for a, (c, mask) in enumerate(((home, near), (mate, far)))])

    if i == 0:
        twins = make_plan(plan["mate"], T, topo)["passers"][:TWINS]
        for name, t, see in (("hp", T.HQS, same), ("hq", T.HQC, raw)):
            g.wait_ge(sem[name + "0"], E8)
            post(*[tr(see(col(t, 0, 128)), [(c, see(col(t, a, 128))) for c in to], mask, name + str(a))
                   for a, (to, mask) in enumerate(((plan["passers"][1:], near), (twins, far)))])
    for k, (c, p) in enumerate(((T.FXC, T.FXS), (T.FRC, T.FRS))):
        for name, src, here, there in zip(PIECES, pieces(T.HYC, T.HYS, k), pieces(c, p, 2 * i), pieces(c, p, 2 * i + 1)):
            if (k, name) == NUMAT[i]:
                numbers()
            g.wait_ge(sem[name + str(k)], E8)
            post(tr(src, [(home, here)], near, ("wx%d", "wr%d")[k] % (2 * i)), tr(src, [(mate, there)], far, ("wx%d", "wr%d")[k] % (2 * i + 1)))
    if not NUMAT[i]:
        numbers()
    finish()
